import numpy as np
import ml_dtypes


def mxq(x, axis, fmt="e4m3"):
    dtype, down = {"e4m3": (ml_dtypes.float8_e4m3fn, 7), "e5m2": (ml_dtypes.float8_e5m2, 14)}[fmt]
    v = np.moveaxis(np.asarray(x, np.float32).astype(ml_dtypes.bfloat16).astype(np.float64), axis, -1)
    blocks = v.reshape(v.shape[:-1] + (-1, 32))
    amax = np.abs(blocks).max(-1, keepdims=True)
    byte = np.maximum(np.where(amax > 0, np.frexp(amax)[1] - 1 + 127, 0) - down, 1)
    scale = np.exp2(byte - 127.0)
    codes = (blocks / scale).astype(np.float32).astype(dtype).astype(np.float64)
    return np.moveaxis((codes * scale).reshape(v.shape), -1, axis)


WIDE = False


def mx_kscale(k):
    if not WIDE:
        return np.ones(k)
    levels = np.array([10, -10, 5, -5, 0])
    if k % 512:
        return np.exp2(np.random.permutation(np.resize(levels, k // 32))).repeat(32)
    a = np.empty((k // 512, 16))
    for p in range(k // 512):
        a[p, :8] = np.random.permutation(np.resize(levels, 8))
        for g in range(8):
            far = levels[np.abs(levels - a[p, g]) >= 10]
            a[p, g + 8] = far[np.random.randint(len(far))]
    return np.exp2(a.ravel()).repeat(32)


BF16 = ml_dtypes.bfloat16


def bf(x):
    return np.asarray(x, np.float32).astype(BF16)


def f64(x):
    return np.asarray(x).astype(np.float64)


E2M1 = np.array([0.0, 0.5, 1.0, 1.5, 2.0, 3.0, 4.0, 6.0, -0.0, -0.5, -1.0, -1.5, -2.0, -3.0, -4.0, -6.0])


def pack_weight(w, fmt):
    k, n = w.shape
    w = f64(bf(w)).reshape(k // 32, 32, n)
    amax = np.abs(w).max(1)
    if fmt == "e4m3":
        byte = np.frexp(amax)[1] - 1 + 127 - 7
    else:
        mant, ex = np.frexp(amax / 6.0)
        byte = np.where(mant > 0.5, ex, ex - 1) + 127
    byte = np.clip(np.where(amax > 0, byte, 1), 1, 254)
    scaled = (w * np.exp2(127.0 - byte)[:, None, :]).reshape(k, n).astype(np.float32)
    by_word = np.ascontiguousarray(scaled.reshape(k // 512, 128, 4, n).transpose(0, 1, 3, 2))
    if fmt == "e4m3":
        words = by_word.astype(ml_dtypes.float8_e4m3fn).view(np.uint8)
    else:
        c = by_word.astype(ml_dtypes.float4_e2m1fn).view(np.uint8) & 0xF
        words = c[..., 0::2] | (c[..., 1::2] << 4)
    return np.ascontiguousarray(words), np.ascontiguousarray(byte.astype(np.uint8).reshape(k // 512, 16, n))


def unpack_weight(words, scales, fmt):
    g, p, n, _ = words.shape
    if fmt == "e4m3":
        vals = np.ascontiguousarray(words).view(ml_dtypes.float8_e4m3fn).astype(np.float64)
    else:
        nib = np.empty((g, p, n, 4), np.uint8)
        nib[..., 0::2] = words & 0xF
        nib[..., 1::2] = words >> 4
        vals = E2M1[nib]
    vals = vals * np.repeat(np.exp2(scales.astype(np.float64) - 127.0), 8, axis=1)[..., None]
    return vals.transpose(0, 1, 3, 2).reshape(g * 512, n)
def pack4(w):
    words, scales = pack_weight(w, "e2m1")
    return words.reshape(words.shape[0], 128, -1), scales


def unpack4(words, scales):
    return unpack_weight(words.reshape(words.shape[0], 128, -1, 2), scales, "e2m1")


M, K, R = 2048, 512, 512


def draw0():
    s = mx_kscale(K)
    u = mx_kscale(M)
    loads = np.random.standard_normal((M, K)) * s * u[:, None]
    lag_loads = 0.25 * np.random.standard_normal((K, M)) / np.sqrt(K) / s[:, None]
    gain = 1 + 0.1 * np.random.standard_normal(M)
    private = (4 + 0.5 * np.random.standard_normal(M)) * u
    readout = 2 * np.random.standard_normal((M, R)) / np.sqrt(M) / u[:, None]
    words, scales = pack4(readout)
    return {"loads": bf(loads),
            "lag_loads": bf(lag_loads),
            "gain": bf(gain),
            "private": bf(private),
            "readout_words": words,
            "readout_scales": scales}


def core(loads, lag_loads, gain, private, readout_words, readout_scales):
    a = mxq(f64(loads), 1, "e4m3")
    b = mxq(f64(lag_loads), 0, "e4m3")
    shared = a @ b
    cov = shared * f64(gain)[:, None] + f64(private)[:, None] * np.eye(M)
    w = unpack4(readout_words, readout_scales)
    return w.T @ mxq(cov, 0, "e4m3")


def e4m3fn_bytes(y):
    return np.clip(np.asarray(y, np.float64), -448.0, 448.0).astype(np.float32).astype(ml_dtypes.float8_e4m3fn).view(np.uint8)


def e4m3fn_values(b):
    return np.asarray(b, np.uint8).view(ml_dtypes.float8_e4m3fn).astype(np.float64)


def setup_inputs():
    d = draw0()
    x0 = np.asarray(d['lag_loads']).astype(np.float64)
    s = (np.max(np.abs(x0), axis=(1,), keepdims=True) / 448.0).astype(np.float32)
    out = {}
    for k, v in d.items():
        if k == 'lag_loads':
            out['lag_loads_bytes'] = e4m3fn_bytes(x0 / s.astype(np.float64))
            out['lag_loads_scale'] = s
        else:
            out[k] = v
    return out


def reference(loads, lag_loads_bytes, lag_loads_scale, gain, private, readout_words, readout_scales):
    return core(loads, e4m3fn_values(lag_loads_bytes) * lag_loads_scale.astype(np.float64), gain, private, readout_words, readout_scales)

@@ -1,0 +1,590 @@
+from contextlib import ExitStack
+
+import concourse.mybir as mybir
+from concourse.masks import make_identity
+
+F32 = mybir.dt.float32
+BF16 = mybir.dt.bfloat16
+U32 = mybir.dt.uint32
+I32 = mybir.dt.int32
+U8 = mybir.dt.uint8
+FP8 = mybir.dt.float8_e4m3fn
+FP8X4 = mybir.dt.float8_e4m3fn_x4
+FP4X4 = mybir.dt.float4_e2m1fn_x4
+ALU = mybir.AluOpType
+ACT = mybir.ActivationFunctionType
+
+M, K, R = 2048, 512, 512
+FLOPS = 2 * M * K * M + 2 * R * M * M
+
+P = 128
+PE_LAG = ()
+HALF_UNITS = ()
+DIRECT = {12: (1,), 13: (1,), 14: (1,), 15: (1,)}
+LAG_AT = (((0, 1), (0, 3)), ((0, 3), (1, 1)), ((0, 3), (1, 1)))
+V_OTHER, V_INT, V_Q = 1, 1, 3
+T3_AT = (1, 2)
+T3S = False
+PE_HEAD = False
+ND = 4
+LAG0 = ((3, 4), (0, 1), (1, 2), (2, 3))
+WS0, WS = 0, (0, 1)
+O_D = (14, 14, 14, 10)
+V_SWITCH = 14
+BLOCK_ORDER = (3, 0, 1, 2)
+PITCH = 544
+
+
+def tile_spike_covariance_readout_s13_kernel(
+    tc, loads, lag_bytes, lag_scale, gain, private, w_words, w_scales, out
+):
+    nc = tc.nc
+    with ExitStack() as ctx:
+        keep = ctx.enter_context(tc.tile_pool(name="keep", bufs=1))
+        work = ctx.enter_context(tc.tile_pool(name="work", bufs=3))
+        psum = ctx.enter_context(tc.psum_pool(name="psum", bufs=4))
+        ctx.enter_context(tc.manual_schedule())
+
+        lagsc = keep.tile([P, 4], F32, name="lagsc")
+        nc.scalar.dma_start(out=lagsc[:], in_=lag_scale.rearrange("(p t) o -> p (t o)", t=4))
+        gp_rows = keep.tile([P, 512], BF16, name="gp_rows")
+        nc.vector.memset(gp_rows[:].bitcast(I32), 0)
+        nc.scalar.dma_start(out=gp_rows[0:4, :], in_=gain.rearrange("(g x) -> g x", g=4))
+        nc.scalar.dma_start(out=gp_rows[4:8, :], in_=private.rearrange("(g x) -> g x", g=4))
+
+        lag_view = lag_bytes.rearrange("(p t) j -> p t j", t=4)
+        lag_raw = {}
+        raw = {}
+
+        def load_lag(jb, parts=((0, 4),)):
+            lraw = work.tile([P, 4, 512], U8, name="lraw", bufs=4, align_bytes=64)
+            for a, b in parts:
+                nc.sync.dma_start(out=lraw[:, a:b, :], in_=lag_view[:, a:b, 512 * jb : 512 * jb + 512])
+            lag_raw[jb] = lraw
+
+        def load_loads(g, parts):
+            rows = work.tile([P, 4, 512], BF16, name="rows", bufs=4, align_bytes=64)
+            src = loads[512 * g : 512 * g + 512, :].rearrange("(m t) k -> m t k", t=4)
+            step = 4 // parts
+            for a in range(0, 4, step):
+                nc.sync.dma_start(out=rows[:, a : a + step, :], in_=src[:, a : a + step, :])
+            raw[g] = rows
+
+        load_lag(BLOCK_ORDER[0], LAG0)
+        load_loads(0, 2)
+        load_loads(1, 1)
+        load_lag(BLOCK_ORDER[1])
+        load_loads(2, 1)
+        load_loads(3, 1)
+        w_sb = keep.tile([P, 4, 1024], U8, name="w_sb", align_bytes=64)
+        nc.sync.dma_start(out=w_sb[:], in_=w_words.rearrange("g p n -> p g n"))
+        ws_sb = keep.tile([P, 4, 512], U8, name="ws_sb", align_bytes=64)
+        nc.vector.memset(ws_sb[:].rearrange("p g n -> p (g n)").bitcast(I32), 0)
+        ws_view = w_scales.bitcast(I32).rearrange("g q n -> q g n")
+        for quad in range(4):
+            nc.sync.dma_start(
+                out=ws_sb[32 * quad : 32 * quad + 4, :, :].bitcast(I32),
+                in_=ws_view[4 * quad : 4 * quad + 4, :, :],
+            )
+        load_lag(BLOCK_ORDER[2])
+        load_lag(BLOCK_ORDER[3])
+
+        warm = keep.tile([P, 1], F32, name="warm")
+        nc.gpsimd.memset(warm[:], 0.0)
+        warm2 = keep.tile([P, 1], F32, name="warm2")
+        nc.scalar.activation(out=warm2[:], in_=warm[:], func=ACT.Copy, scale=1.0)
+        dmini = keep.tile([P, 4, 128, 4], BF16, name="dmini")
+        nc.gpsimd.memset(dmini[:].rearrange("p q c t -> p (q c t)").bitcast(I32), 0)
+        ident = keep.tile([P, P], F32, name="ident")
+        make_identity(nc, ident[:])
+        ident_b = keep.tile([P, P], BF16, name="ident_b")
+        nc.gpsimd.tensor_copy(out=ident_b[:], in_=ident[:])
+        gp_f = keep.tile([P, 2, 16], F32, name="gp_f")
+        gain_f, priv_f = gp_f[:, 0, :], gp_f[:, 1, :]
+        diag = keep.tile([P, 16, P], BF16, name="diag")
+
+        def build_diag(jb):
+            for t in range(4):
+                if jb != BLOCK_ORDER[3]:
+                    dst, src = diag[:, 4 * jb + t, :], ident[:]
+                else:
+                    dst, src = dmini[:, :, 32 * t : 32 * t + 32, t], ident[:].rearrange("p (q m) -> p q m", q=4)
+                nc.vector.tensor_scalar(
+                    out=dst, in0=src, scalar1=priv_f[:, 4 * jb + t : 4 * jb + t + 1], scalar2=None, op0=ALU.mult
+                )
+
+        lag_planes, lag_grp, lag_codes, lag_sc = {}, {}, {}, {}
+        ld_grp, ld_codes, ld_sc = {}, {}, {}
+
+        def lag_alloc(jb):
+            lpl = work.tile([P, 4, 512], BF16, name="lpl", bufs=2, align_bytes=64)
+            lgr = work.tile([P, 512, 4], BF16, name="lgr", bufs=2, align_bytes=64)
+            lco = work.tile([P, 512], U32, name="lco", bufs=2, align_bytes=64)
+            lsc = work.tile([P, 512], U8, name="lsc", bufs=2, align_bytes=64)
+            lag_planes[jb], lag_grp[jb], lag_codes[jb], lag_sc[jb] = lpl, lgr, lco, lsc
+
+        def lag_widen(jb, t, on_scalar):
+            src = lag_raw[jb][:, t, :].bitcast(FP8)
+            dst = lag_planes[jb][:, t, :]
+            if on_scalar:
+                nc.scalar.activation(out=dst, in_=src, func=ACT.Copy, scale=lagsc[:, t : t + 1])
+            else:
+                nc.vector.tensor_scalar(out=dst, in0=src, scalar1=lagsc[:, t : t + 1], scalar2=None, op0=ALU.mult)
+
+        def lag_interleave(jb, h):
+            src = lag_planes[jb][:, :, 256 * h : 256 * h + 256].rearrange("p t (q m s) -> p q m t s", q=2, s=4)
+            dst = lag_grp[jb][:, 256 * h : 256 * h + 256, :].rearrange("p (q s m) t -> p q m t s", q=2, s=4)
+            nc.vector.tensor_copy(out=dst, in_=src)
+
+        lag_banks = {}
+
+        def lag_turn(jb, h):
+            s_bank = psum.tile([P, 1024], BF16, name="s_bank")
+            lag_banks[jb, h] = s_bank
+            for i in range(2):
+                q = 2 * h + i
+                nc.tensor.matmul(
+                    out=s_bank[:, 512 * i : 512 * i + 512],
+                    lhsT=ident_b[:],
+                    rhs=lag_planes[jb][:, :, 128 * q : 128 * q + 128].rearrange("p t (m s) -> p s m t", s=4),
+                    start=True,
+                    stop=True,
+                )
+
+        def lag_exit(jb, h):
+            nc.scalar.copy(
+                out=lag_grp[jb][:, 256 * h : 256 * h + 256, :].rearrange("p c t -> p (c t)"), in_=lag_banks[jb, h][:]
+            )
+
+        def lag_quant(jb):
+            nc.vector.quantize_mx(
+                out=lag_codes[jb][:].bitcast(FP8X4),
+                scales=lag_sc[jb][:],
+                in_=lag_grp[jb][:].rearrange("p c t -> p (c t)"),
+            )
+
+        turned = {}
+
+        def loads_turn(g, h):
+            if h == 0:
+                lg = work.tile([P, 512, 4], BF16, name="lg", bufs=2, align_bytes=64)
+                lc = work.tile([P, 512], U32, name="lc", bufs=4, align_bytes=64)
+                ls = work.tile([P, 512], U8, name="ls", bufs=4, align_bytes=64)
+                ld_grp[g], ld_codes[g], ld_sc[g] = lg, lc, ls
+            o_bank = psum.tile([P, 512], F32, name="o_bank")
+            view = o_bank[:].rearrange("p (t u m) -> p t u m", t=2, u=2)
+            for tt in range(2):
+                words = raw[g][:, 2 * h + tt, :].bitcast(F32)
+                for u in range(2):
+                    nc.tensor.transpose(view[:, tt, u, :], words[:, u:256:2], ident[:])
+            turned[g, h] = o_bank
+
+        def loads_exit(g, h, on_scalar=True):
+            src = turned[g, h][:].rearrange("p (t u m) -> p t m u", t=2, u=2)
+            dst = (
+                ld_grp[g][:, 256 * h : 256 * h + 256, :]
+                .rearrange("p c t -> p (c t)")
+                .bitcast(F32)
+                .rearrange("p (t m u) -> p t m u", t=2, u=2)
+            )
+            if on_scalar:
+                nc.scalar.copy(out=dst, in_=src)
+            else:
+                nc.vector.tensor_copy(out=dst, in_=src)
+
+        def loads_quant(g, lo=0, hi=512):
+            nc.vector.quantize_mx(
+                out=ld_codes[g][:, lo:hi].bitcast(FP8X4),
+                scales=ld_sc[g][:, lo:hi],
+                in_=ld_grp[g][:, lo:hi, :].rearrange("p c t -> p (c t)"),
+            )
+
+        units = [(jb, g) for jb in BLOCK_ORDER[:3] for g in range(4)] + [(BLOCK_ORDER[3], q) for q in range(4)]
+        NU = len(units)
+        WIDE = 12
+        banks, planes, grouped, codes, scales, wins = {}, {}, {}, {}, {}, {}
+        o_banks = {}
+
+        def direct(n, g):
+            return g in DIRECT.get(n, ())
+
+        def is_diag(n):
+            return n < WIDE and units[n][0] == units[n][1]
+
+        def s_pass(n, x):
+            jb, y = units[n]
+            s_bank = psum.tile([P, 512], F32, name="s_bank")
+            banks[n, x] = s_bank
+            if n in HALF_UNITS:
+                if x % 2 == 0:
+                    ts, c0, w = (x, x + 1), 0, 256
+                else:
+                    ts, c0, w = (0, 1, 2, 3), 256 + 64 * (x - 1), 128
+                for i, t in enumerate(ts):
+                    nc.tensor.matmul_mx(
+                        out=s_bank[:, w * i : w * i + w],
+                        lhsT=ld_codes[y][:, 128 * t : 128 * t + 128].bitcast(FP8X4),
+                        lhsT_scale=ld_sc[y][:, 128 * t : 128 * t + 128],
+                        rhs=lag_codes[jb][:, c0 : c0 + w].bitcast(FP8X4),
+                        rhs_scale=lag_sc[jb][:, c0 : c0 + w],
+                        start=True,
+                        stop=True,
+                    )
+            elif n < WIDE:
+                nc.tensor.matmul_mx(
+                    out=s_bank[:],
+                    lhsT=ld_codes[y][:, 128 * x : 128 * x + 128].bitcast(FP8X4),
+                    lhsT_scale=ld_sc[y][:, 128 * x : 128 * x + 128],
+                    rhs=lag_codes[jb][:].bitcast(FP8X4),
+                    rhs_scale=lag_sc[jb][:],
+                    start=True,
+                    stop=True,
+                )
+            else:
+                for t in range(4):
+                    nc.tensor.matmul_mx(
+                        out=s_bank[:, 128 * t : 128 * t + 128],
+                        lhsT=ld_codes[x][:, 128 * t : 128 * t + 128].bitcast(FP8X4),
+                        lhsT_scale=ld_sc[x][:, 128 * t : 128 * t + 128],
+                        rhs=lag_codes[jb][:, 128 * y : 128 * y + 128].bitcast(FP8X4),
+                        rhs_scale=lag_sc[jb][:, 128 * y : 128 * y + 128],
+                        start=True,
+                        stop=True,
+                    )
+
+        def x_alloc(n):
+            pl = work.tile([P, 4 * PITCH], BF16, name="pl", bufs=4, align_bytes=64)
+            gr = work.tile([P, 2048], BF16, name="gr", bufs=4, align_bytes=64)
+            co = work.tile([P, 512], U32, name="co", bufs=4, align_bytes=64)
+            sc = work.tile([P, 512], U8, name="sc", bufs=4, align_bytes=64)
+            planes[n], grouped[n], codes[n], scales[n] = pl, gr, co, sc
+            if is_diag(n) or n >= WIDE:
+                win = work.tile([P, 4, 128], F32, name="win", bufs=2)
+                wins[n] = win
+
+        def exit_scaled(dst, src, g, t):
+            nc.scalar.activation(out=dst, in_=src, func=ACT.Copy, scale=gain_f[:, 4 * g + t : 4 * g + t + 1])
+
+        def x_scalar(n, x):
+            jb, y = units[n]
+            bank = banks[n, x]
+            if n in HALF_UNITS:
+                if x % 2 == 0:
+                    for i in range(2):
+                        t = x + i
+                        exit_scaled(planes[n][:, 512 * t : 512 * t + 256], bank[:, 256 * i : 256 * i + 256], y, t)
+                return
+            if n < WIDE:
+                g, t = y, x
+                dst = planes[n][:, 512 * t : 512 * t + 512]
+                if g != jb:
+                    exit_scaled(dst, bank[:], g, t)
+                else:
+                    b4 = bank[:].rearrange("p (q c) -> p q c", q=4)
+                    d4 = dst.rearrange("p (q c) -> p q c", q=4)
+                    lo, hi = 32 * t, 32 * t + 32
+                    exit_scaled(wins[n][:, t, :].rearrange("p (q c) -> p q c", q=4), b4[:, :, lo:hi], g, t)
+                    if t > 0:
+                        exit_scaled(d4[:, :, 0:lo], b4[:, :, 0:lo], g, t)
+                    if t < 3:
+                        exit_scaled(d4[:, :, hi:128], b4[:, :, hi:128], g, t)
+            else:
+                g = x
+                if direct(n, g):
+                    return
+                for t in range(4):
+                    c = slice(128 * t, 128 * t + 128)
+                    dst = wins[n][:, t, :] if g == jb else planes[n][:, 512 * g + 128 * t : 512 * g + 128 * t + 128]
+                    exit_scaled(dst, bank[:, c], g, t)
+
+        def x_vector(n, x):
+            if n in HALF_UNITS and x % 2 == 1:
+                g, a = units[n][1], 1024 + 256 * (x - 1)
+            elif n >= WIDE and direct(n, x):
+                g, a = x, 512 * x
+            else:
+                return
+            nc.vector.tensor_tensor(
+                out=grouped[n][:, a : a + 512].rearrange("p (c t) -> p c t", t=4),
+                in0=banks[n, x][:].rearrange("p (t c) -> p c t", t=4),
+                in1=gain_f[:, 4 * g : 4 * g + 4].unsqueeze(1).to_broadcast([P, 128, 4]),
+                op=ALU.mult,
+            )
+
+        def add_windows(n):
+            g = units[n][1]
+            nc.vector.tensor_tensor(
+                out=planes[n][:].rearrange("p (t c) -> p t c", t=4)[:, :, 0:512].rearrange("p t (q c) -> p t q c", q=4)[
+                    :, :, :, 0:32
+                ],
+                in0=wins[n][:].rearrange("p t (q c) -> p t q c", q=4),
+                in1=diag[:, 4 * g : 4 * g + 4, :].rearrange("p t (q c) -> p t q c", q=4),
+                op=ALU.add,
+            )
+
+        def interleave(n, gs=(0, 1, 2, 3)):
+            if n < WIDE:
+                w = 256 if n in HALF_UNITS else 512
+                nc.vector.tensor_copy(
+                    out=grouped[n][:, 0 : 4 * w].rearrange("p (c i t) -> p c t i", i=4, t=4),
+                    in_=planes[n][:, 0:2048].rearrange("p (t c) -> p t c", t=4)[:, :, 0:w].rearrange(
+                        "p t (c i) -> p c t i", i=4
+                    ),
+                )
+                return
+            jb, q = units[n]
+            for g in gs:
+                if direct(n, g):
+                    continue
+                dst = grouped[n][:, 512 * g : 512 * g + 512]
+                if g == jb:
+                    nc.vector.tensor_tensor(
+                        out=dst.rearrange("p (c t) -> p c t", t=4),
+                        in0=wins[n][:].rearrange("p t c -> p c t"),
+                        in1=dmini[:, q, :, :],
+                        op=ALU.add,
+                    )
+                else:
+                    nc.vector.tensor_copy(
+                        out=dst.rearrange("p (c i t) -> p c t i", i=4, t=4),
+                        in_=planes[n][:, 512 * g : 512 * g + 512].rearrange("p (t c i) -> p c t i", t=4, i=4),
+                    )
+
+        def quant(n, lo=0, hi=512):
+            nc.vector.quantize_mx(
+                out=codes[n][:, lo:hi].bitcast(FP8X4), scales=scales[n][:, lo:hi], in_=grouped[n][:, 4 * lo : 4 * hi]
+            )
+
+        def w_op(g, r):
+            return w_sb[:, g, 256 * r : 256 * r + 256].bitcast(FP4X4), ws_sb[:, g, 128 * r : 128 * r + 128]
+
+        def o_pass(n, r):
+            jb, y = units[n]
+            if n < WIDE:
+                if y == 0:
+                    o_bank = psum.tile([P, 512], F32, name="o_bank")
+                    o_banks[n // 4, r] = o_bank
+                wc, ws = w_op(y, r)
+                nc.tensor.matmul_mx(
+                    out=o_banks[n // 4, r][:],
+                    lhsT=wc,
+                    lhsT_scale=ws,
+                    rhs=codes[n][:].bitcast(FP8X4),
+                    rhs_scale=scales[n][:],
+                    start=(y == 0),
+                    stop=(y == 3),
+                )
+            else:
+                if r == 0:
+                    o_bank = psum.tile([P, 512], F32, name="o_bank")
+                    o_banks[n, 0] = o_bank
+                for g in range(4):
+                    wc, ws = w_op(g, r)
+                    nc.tensor.matmul_mx(
+                        out=o_banks[n, 0][:, 128 * r : 128 * r + 128],
+                        lhsT=wc,
+                        lhsT_scale=ws,
+                        rhs=codes[n][:, 128 * g : 128 * g + 128].bitcast(FP8X4),
+                        rhs_scale=scales[n][:, 128 * g : 128 * g + 128],
+                        start=(g == 0),
+                        stop=(g == 3),
+                    )
+
+        def o_exit(k, r):
+            jb = BLOCK_ORDER[k]
+            ot = work.tile([P, 512], F32, name="ot", bufs=8)
+            nc.scalar.copy(
+                out=ot[:].rearrange("p (q m s) -> p q m s", q=4, s=4),
+                in_=o_banks[k, r][:].rearrange("p (q s m) -> p q m s", q=4, s=4),
+            )
+            nc.sync.dma_start(out=out[128 * r : 128 * r + 128, 512 * jb : 512 * jb + 512], in_=ot[:])
+
+        def o_exit_narrow(n):
+            jb, q = units[n]
+            j0 = 512 * jb + 128 * q
+            ot = work.tile([P, 512], F32, name="ot", bufs=8)
+            dst = ot[:].rearrange("p (r m s) -> p r m s", r=4, s=4)
+            src = o_banks[n, 0][:].rearrange("p (r s m) -> p r m s", r=4, s=4)
+            hbm = out[:, j0 : j0 + 128].rearrange("(r p) j -> p r j", p=P)
+            o3 = ot[:].rearrange("p (r j) -> p r j", r=4)
+            nc.scalar.copy(out=dst, in_=src)
+            nc.sync.dma_start(out=hbm, in_=o3)
+
+        def finish(n):
+            jb, q = units[n]
+            j0 = 512 * jb + 128 * q
+            accs = []
+            for r in range(4):
+                s_bank = psum.tile([P, 512], F32, name="s_bank")
+                accs.append(s_bank)
+            for g in range(4):
+                for r in range(4):
+                    wc, ws = w_op(g, r)
+                    nc.tensor.matmul_mx(
+                        out=accs[r][:, 0:128],
+                        lhsT=wc,
+                        lhsT_scale=ws,
+                        rhs=codes[n][:, 128 * g : 128 * g + 128].bitcast(FP8X4),
+                        rhs_scale=scales[n][:, 128 * g : 128 * g + 128],
+                        start=(g == 0),
+                        stop=(g == 3),
+                    )
+            ot = work.tile([P, 512], F32, name="ot", bufs=8)
+            o3 = ot[:].rearrange("p (r j) -> p r j", r=4)
+            hbm = out[:, j0 : j0 + 128].rearrange("(r p) j -> p r j", p=P)
+            for r in range(4):
+                dst = o3[:, r, :].rearrange("p (m s) -> p m s", s=4)
+                src = accs[r][:, 0:128].rearrange("p (s m) -> p m s", s=4)
+                if r % 2 == 0:
+                    nc.scalar.copy(out=dst, in_=src)
+                else:
+                    nc.vector.tensor_copy(out=dst, in_=src)
+                    nc.sync.dma_start(out=hbm[:, r - 1 : r + 1], in_=o3[:, r - 1 : r + 1])
+
+        jb0 = BLOCK_ORDER[0]
+        lag_alloc(jb0)
+        lag_widen(jb0, 3, True)
+        for t in range(3):
+            lag_widen(jb0, t, False)
+        if PE_HEAD:
+            loads_turn(0, 0)
+            lag_turn(jb0, 0)
+            loads_exit(0, 0)
+            lag_exit(jb0, 0)
+            loads_turn(0, 1)
+            lag_turn(jb0, 1)
+            lag_exit(jb0, 1)
+            loads_exit(0, 1)
+        else:
+            loads_turn(0, 0)
+            loads_exit(0, 0)
+            loads_turn(0, 1)
+            loads_exit(0, 1)
+            lag_interleave(jb0, 0)
+            lag_interleave(jb0, 1)
+        loads_quant(0, 0, 256)
+        lag_quant(jb0)
+        loads_quant(0, 256, 512)
+        for h in range(2):
+            loads_turn(1, h)
+            loads_exit(1, h)
+        o_bank = psum.tile([P, 1024], BF16, name="o_bank")
+        for t in range(4):
+            nc.tensor.transpose(o_bank[:, 128 * t : 128 * t + 128], gp_rows[:, t:512:4], ident_b[:])
+        nc.scalar.copy(
+            out=gp_f[:].rearrange("p a (g t) -> p a g t", t=4),
+            in_=o_bank[:, 0:512].rearrange("p (t r) -> p t r", t=4)[:, :, 0:8].rearrange("p t (a g) -> p a g t", a=2),
+        )
+        lag_alloc(BLOCK_ORDER[1])
+        for t in range(4):
+            lag_widen(BLOCK_ORDER[1], t, t < WS0)
+        loads_quant(1)
+
+        jobs = []
+        for n in range(NU):
+            for x in range(4):
+                jobs.append(("unit", n, x))
+                k = n // 4
+                if n < 12 and k in PE_LAG and (n % 4, x) in LAG_AT[k]:
+                    jobs.append(("lag", k, LAG_AT[k].index((n % 4, x))))
+
+        def fill(job):
+            kind, a, b = job
+            if kind == "lag":
+                lag_turn(BLOCK_ORDER[a + 1], b)
+            else:
+                s_pass(a, b)
+
+        def vector_work(n, x):
+            k = n // 4
+            if n == 0:
+                if x == 1:
+                    lag_interleave(BLOCK_ORDER[1], 0)
+                    lag_interleave(BLOCK_ORDER[1], 1)
+                    for jb in BLOCK_ORDER[:ND]:
+                        build_diag(jb)
+                if x == 2:
+                    loads_quant(2)
+                if x == 3:
+                    if not T3S:
+                        loads_exit(3, 0, on_scalar=False)
+                        loads_exit(3, 1, on_scalar=False)
+                    lag_quant(BLOCK_ORDER[1])
+                    if not T3S:
+                        loads_quant(3)
+                return
+            if T3S and n == 1 and x == 1:
+                loads_quant(3)
+            if x == 0 and is_diag(n - 1):
+                add_windows(n - 1)
+            if x == V_OTHER:
+                if n in (2, 4, 5) and {2: 1, 4: 2, 5: 3}[n] >= ND:
+                    build_diag(BLOCK_ORDER[{2: 1, 4: 2, 5: 3}[n]])
+                if n in (3, 7):
+                    jb = BLOCK_ORDER[k + 2]
+                    lag_alloc(jb)
+                    for t in range(4):
+                        lag_widen(jb, t, t < WS[k])
+                if n in (5, 9) and k not in PE_LAG:
+                    lag_interleave(BLOCK_ORDER[k + 1], 0)
+                    lag_interleave(BLOCK_ORDER[k + 1], 1)
+                if n in (6, 10):
+                    lag_quant(BLOCK_ORDER[k + 1])
+            if x == V_INT:
+                interleave(n - 1)
+            if x == V_Q:
+                if n < V_SWITCH and n >= 2:
+                    quant(n - 2)
+                if n == V_SWITCH:
+                    quant(n - 2)
+                if n >= V_SWITCH:
+                    quant(n - 1)
+
+        o_done = [0]
+
+        def out_passes(step, most):
+            for i in range(most):
+                o = o_done[0]
+                if o >= 4 * (NU - 1) or o + O_D[o // 16] > step:
+                    return
+                if o % 16 < 4 and o >= 16:
+                    o_exit(o // 16 - 1, o % 16)
+                o_pass(o // 4, o % 4)
+                if o // 4 >= WIDE and o % 4 == 3:
+                    o_exit_narrow(o // 4)
+                o_done[0] = o + 1
+
+        for job in jobs[:4]:
+            fill(job)
+        loads_turn(2, 0)
+        loads_turn(2, 1)
+        step = 0
+        for j, (kind, n, x) in enumerate(jobs):
+            if kind == "lag":
+                lag_exit(BLOCK_ORDER[n + 1], x)
+                if j + 4 < len(jobs):
+                    fill(jobs[j + 4])
+                continue
+            if x == 0:
+                x_alloc(n)
+            x_scalar(n, x)
+            x_vector(n, x)
+            if n == 0 and x in (1, 2):
+                loads_exit(2, x - 1)
+            if T3S and step in (3, 5):
+                loads_exit(3, (step - 3) // 2)
+            if j + 4 < len(jobs):
+                fill(jobs[j + 4])
+            if n == 0 and x in T3_AT:
+                loads_turn(3, T3_AT.index(x))
+            vector_work(n, x)
+            out_passes(step, 2)
+            step += 1
+        if V_SWITCH > NU - 1:
+            quant(NU - 2)
+        interleave(NU - 1, (0, 1, 2))
+        quant(NU - 1, 0, 256)
+        interleave(NU - 1, (3,))
+        quant(NU - 1, 256, 512)
+        out_passes(1000, 1000)
+        finish(NU - 1)

@@ -18,21 +18,13 @@ M, K, R = 2048, 512, 512
 FLOPS = 2 * M * K * M + 2 * R * M * M
 
 P = 128
-PE_LAG = ()
-HALF_UNITS = ()
-DIRECT = {12: (1,), 13: (1,), 14: (1,), 15: (1,)}
-LAG_AT = (((0, 1), (0, 3)), ((0, 3), (1, 1)), ((0, 3), (1, 1)))
-V_OTHER, V_INT, V_Q = 1, 1, 3
-T3_AT = (1, 2)
-T3S = False
-PE_HEAD = False
-ND = 4
-LAG0 = ((3, 4), (0, 1), (1, 2), (2, 3))
-WS0, WS = 0, (0, 1)
-O_D = (14, 14, 14, 10)
-V_SWITCH = 14
-BLOCK_ORDER = (3, 0, 1, 2)
-PITCH = 544
+PANELS = (2, 3, 0, 1)
+PERIODS = 8
+G_COLS = (384, 512)
+WIDEN_V = (3, 4, 0, 0)
+LAG_S = (0, 0, 1, 1)
+RING = 4
+G2_S = (True, True)
 
 
 def tile_spike_covariance_readout_s13_kernel(
@@ -42,40 +34,44 @@ def tile_spike_covariance_readout_s13_kernel(
     with ExitStack() as ctx:
         keep = ctx.enter_context(tc.tile_pool(name="keep", bufs=1))
         work = ctx.enter_context(tc.tile_pool(name="work", bufs=3))
-        psum = ctx.enter_context(tc.psum_pool(name="psum", bufs=4))
+        psum = ctx.enter_context(tc.psum_pool(name="psum", bufs=1))
         ctx.enter_context(tc.manual_schedule())
 
-        lagsc = keep.tile([P, 4], F32, name="lagsc")
-        nc.scalar.dma_start(out=lagsc[:], in_=lag_scale.rearrange("(p t) o -> p (t o)", t=4))
         gp_rows = keep.tile([P, 512], BF16, name="gp_rows")
         nc.vector.memset(gp_rows[:].bitcast(I32), 0)
+        ident = keep.tile([P, P], F32, name="ident")
+        make_identity(nc, ident[:])
+        lagsc = keep.tile([P, 4], F32, name="lagsc")
+        nc.scalar.dma_start(out=lagsc[:], in_=lag_scale.rearrange("(p t) o -> p (t o)", t=4))
         nc.scalar.dma_start(out=gp_rows[0:4, :], in_=gain.rearrange("(g x) -> g x", g=4))
         nc.scalar.dma_start(out=gp_rows[4:8, :], in_=private.rearrange("(g x) -> g x", g=4))
 
         lag_view = lag_bytes.rearrange("(p t) j -> p t j", t=4)
-        lag_raw = {}
-        raw = {}
+        lag_raw, rows = {}, {}
 
-        def load_lag(jb, parts=((0, 4),)):
-            lraw = work.tile([P, 4, 512], U8, name="lraw", bufs=4, align_bytes=64)
-            for a, b in parts:
-                nc.sync.dma_start(out=lraw[:, a:b, :], in_=lag_view[:, a:b, 512 * jb : 512 * jb + 512])
-            lag_raw[jb] = lraw
+        def load_lag(k, parts):
+            jb = PANELS[k]
+            lraw = keep.tile([P, 4, 512], U8, name="lraw%d" % k, align_bytes=64)
+            step = 4 // parts
+            for a in range(0, 4, step):
+                nc.sync.dma_start(out=lraw[:, a : a + step, :], in_=lag_view[:, a : a + step, 512 * jb : 512 * jb + 512])
+            lag_raw[k] = lraw
 
-        def load_loads(g, parts):
-            rows = work.tile([P, 4, 512], BF16, name="rows", bufs=4, align_bytes=64)
+        def load_rows(g, parts):
             src = loads[512 * g : 512 * g + 512, :].rearrange("(m t) k -> m t k", t=4)
             step = 4 // parts
             for a in range(0, 4, step):
-                nc.sync.dma_start(out=rows[:, a : a + step, :], in_=src[:, a : a + step, :])
-            raw[g] = rows
+                tile = keep.tile([P, step, 512], BF16, name="rows%d_%d" % (g, a), align_bytes=64)
+                nc.sync.dma_start(out=tile[:], in_=src[:, a : a + step, :])
+                for t in range(step):
+                    rows[g, a + t] = tile[:, t, :]
 
-        load_lag(BLOCK_ORDER[0], LAG0)
-        load_loads(0, 2)
-        load_loads(1, 1)
-        load_lag(BLOCK_ORDER[1])
-        load_loads(2, 1)
-        load_loads(3, 1)
+        load_lag(0, 2)
+        load_rows(0, 2)
+        load_rows(1, 1)
+        load_lag(1, 1)
+        load_rows(2, 1)
+        load_rows(3, 1)
         w_sb = keep.tile([P, 4, 1024], U8, name="w_sb", align_bytes=64)
         nc.sync.dma_start(out=w_sb[:], in_=w_words.rearrange("g p n -> p g n"))
         ws_sb = keep.tile([P, 4, 512], U8, name="ws_sb", align_bytes=64)
@@ -86,107 +82,75 @@ def tile_spike_covariance_readout_s13_kernel(
                 out=ws_sb[32 * quad : 32 * quad + 4, :, :].bitcast(I32),
                 in_=ws_view[4 * quad : 4 * quad + 4, :, :],
             )
-        load_lag(BLOCK_ORDER[2])
-        load_lag(BLOCK_ORDER[3])
+        load_lag(2, 1)
+        load_lag(3, 1)
 
-        warm = keep.tile([P, 1], F32, name="warm")
-        nc.gpsimd.memset(warm[:], 0.0)
-        warm2 = keep.tile([P, 1], F32, name="warm2")
-        nc.scalar.activation(out=warm2[:], in_=warm[:], func=ACT.Copy, scale=1.0)
-        dmini = keep.tile([P, 4, 128, 4], BF16, name="dmini")
-        nc.gpsimd.memset(dmini[:].rearrange("p q c t -> p (q c t)").bitcast(I32), 0)
-        ident = keep.tile([P, P], F32, name="ident")
-        make_identity(nc, ident[:])
-        ident_b = keep.tile([P, P], BF16, name="ident_b")
-        nc.gpsimd.tensor_copy(out=ident_b[:], in_=ident[:])
         gp_f = keep.tile([P, 2, 16], F32, name="gp_f")
         gain_f, priv_f = gp_f[:, 0, :], gp_f[:, 1, :]
         diag = keep.tile([P, 16, P], BF16, name="diag")
 
-        def build_diag(jb):
+        turns = [0]
+
+        def side_bank():
+            bank = psum.tile([P, 512], F32, name="out_bank%d" % (turns[0] % 4))
+            turns[0] = turns[0] + 1
+            return bank
+
+        def build_diag(k):
             for t in range(4):
-                if jb != BLOCK_ORDER[3]:
-                    dst, src = diag[:, 4 * jb + t, :], ident[:]
-                else:
-                    dst, src = dmini[:, :, 32 * t : 32 * t + 32, t], ident[:].rearrange("p (q m) -> p q m", q=4)
+                i = 4 * PANELS[k] + t
                 nc.vector.tensor_scalar(
-                    out=dst, in0=src, scalar1=priv_f[:, 4 * jb + t : 4 * jb + t + 1], scalar2=None, op0=ALU.mult
+                    out=diag[:, i, :], in0=ident[:], scalar1=priv_f[:, i : i + 1], scalar2=None, op0=ALU.mult
                 )
 
         lag_planes, lag_grp, lag_codes, lag_sc = {}, {}, {}, {}
-        ld_grp, ld_codes, ld_sc = {}, {}, {}
+        ld_grp, ld_codes, ld_sc, turned = {}, {}, {}, {}
 
-        def lag_alloc(jb):
-            lpl = work.tile([P, 4, 512], BF16, name="lpl", bufs=2, align_bytes=64)
-            lgr = work.tile([P, 512, 4], BF16, name="lgr", bufs=2, align_bytes=64)
-            lco = work.tile([P, 512], U32, name="lco", bufs=2, align_bytes=64)
-            lsc = work.tile([P, 512], U8, name="lsc", bufs=2, align_bytes=64)
-            lag_planes[jb], lag_grp[jb], lag_codes[jb], lag_sc[jb] = lpl, lgr, lco, lsc
-
-        def lag_widen(jb, t, on_scalar):
-            src = lag_raw[jb][:, t, :].bitcast(FP8)
-            dst = lag_planes[jb][:, t, :]
-            if on_scalar:
-                nc.scalar.activation(out=dst, in_=src, func=ACT.Copy, scale=lagsc[:, t : t + 1])
-            else:
+        def lag_widen(k, t):
+            if k not in lag_planes:
+                lag_planes[k] = work.tile([P, 4, 512], BF16, name="lag_planes", bufs=2, align_bytes=64)
+            src = lag_raw[k][:, t, :].bitcast(FP8)
+            dst = lag_planes[k][:, t, :]
+            if t < WIDEN_V[k]:
                 nc.vector.tensor_scalar(out=dst, in0=src, scalar1=lagsc[:, t : t + 1], scalar2=None, op0=ALU.mult)
+            else:
+                nc.scalar.activation(out=dst, in_=src, func=ACT.Copy, scale=lagsc[:, t : t + 1])
 
-        def lag_interleave(jb, h):
-            src = lag_planes[jb][:, :, 256 * h : 256 * h + 256].rearrange("p t (q m s) -> p q m t s", q=2, s=4)
-            dst = lag_grp[jb][:, 256 * h : 256 * h + 256, :].rearrange("p (q s m) t -> p q m t s", q=2, s=4)
-            nc.vector.tensor_copy(out=dst, in_=src)
+        def lag_interleave(k, h):
+            if k not in lag_grp:
+                lag_grp[k] = work.tile([P, 512, 4], BF16, name="lag_grp", bufs=2, align_bytes=64)
+            src = lag_planes[k][:].rearrange("p t (m s) -> p m t s", s=4)[:, 64 * h : 64 * h + 64]
+            dst = lag_grp[k][:].rearrange("p (s m) t -> p m t s", s=4)[:, 64 * h : 64 * h + 64]
+            if h < LAG_S[k]:
+                nc.scalar.copy(out=dst, in_=src)
+            else:
+                nc.vector.tensor_copy(out=dst, in_=src)
 
-        lag_banks = {}
-
-        def lag_turn(jb, h):
-            s_bank = psum.tile([P, 1024], BF16, name="s_bank")
-            lag_banks[jb, h] = s_bank
-            for i in range(2):
-                q = 2 * h + i
-                nc.tensor.matmul(
-                    out=s_bank[:, 512 * i : 512 * i + 512],
-                    lhsT=ident_b[:],
-                    rhs=lag_planes[jb][:, :, 128 * q : 128 * q + 128].rearrange("p t (m s) -> p s m t", s=4),
-                    start=True,
-                    stop=True,
-                )
-
-        def lag_exit(jb, h):
-            nc.scalar.copy(
-                out=lag_grp[jb][:, 256 * h : 256 * h + 256, :].rearrange("p c t -> p (c t)"), in_=lag_banks[jb, h][:]
-            )
-
-        def lag_quant(jb):
+        def lag_quant(k):
+            lag_codes[k] = work.tile([P, 512], U32, name="lag_codes", bufs=3, align_bytes=64)
+            lag_sc[k] = work.tile([P, 512], U8, name="lag_sc", bufs=3, align_bytes=64)
             nc.vector.quantize_mx(
-                out=lag_codes[jb][:].bitcast(FP8X4),
-                scales=lag_sc[jb][:],
-                in_=lag_grp[jb][:].rearrange("p c t -> p (c t)"),
+                out=lag_codes[k][:].bitcast(FP8X4),
+                scales=lag_sc[k][:],
+                in_=lag_grp[k][:].rearrange("p c t -> p (c t)"),
             )
-
-        turned = {}
 
         def loads_turn(g, h):
-            if h == 0:
-                lg = work.tile([P, 512, 4], BF16, name="lg", bufs=2, align_bytes=64)
-                lc = work.tile([P, 512], U32, name="lc", bufs=4, align_bytes=64)
-                ls = work.tile([P, 512], U8, name="ls", bufs=4, align_bytes=64)
-                ld_grp[g], ld_codes[g], ld_sc[g] = lg, lc, ls
-            o_bank = psum.tile([P, 512], F32, name="o_bank")
-            view = o_bank[:].rearrange("p (t u m) -> p t u m", t=2, u=2)
+            bank = side_bank()
+            view = bank[:].rearrange("p (t u m) -> p t u m", t=2, u=2)
             for tt in range(2):
-                words = raw[g][:, 2 * h + tt, :].bitcast(F32)
+                words = rows[g, 2 * h + tt].bitcast(F32)
                 for u in range(2):
                     nc.tensor.transpose(view[:, tt, u, :], words[:, u:256:2], ident[:])
-            turned[g, h] = o_bank
+            turned[g, h] = bank
 
         def loads_exit(g, h, on_scalar=True):
+            if h == 0:
+                ld_grp[g] = work.tile([P, 2048], BF16, name="ld_grp", bufs=3, align_bytes=64)
+                ld_codes[g] = keep.tile([P, 512], U32, name="ld_codes%d" % g, align_bytes=64)
+                ld_sc[g] = keep.tile([P, 512], U8, name="ld_sc%d" % g, align_bytes=64)
             src = turned[g, h][:].rearrange("p (t u m) -> p t m u", t=2, u=2)
-            dst = (
-                ld_grp[g][:, 256 * h : 256 * h + 256, :]
-                .rearrange("p c t -> p (c t)")
-                .bitcast(F32)
-                .rearrange("p (t m u) -> p t m u", t=2, u=2)
-            )
+            dst = ld_grp[g][:, 1024 * h : 1024 * h + 1024].bitcast(F32).rearrange("p (t m u) -> p t m u", t=2, u=2)
             if on_scalar:
                 nc.scalar.copy(out=dst, in_=src)
             else:
@@ -194,397 +158,257 @@ def tile_spike_covariance_readout_s13_kernel(
 
         def loads_quant(g, lo=0, hi=512):
             nc.vector.quantize_mx(
-                out=ld_codes[g][:, lo:hi].bitcast(FP8X4),
-                scales=ld_sc[g][:, lo:hi],
-                in_=ld_grp[g][:, lo:hi, :].rearrange("p c t -> p (c t)"),
+                out=ld_codes[g][:, lo:hi].bitcast(FP8X4), scales=ld_sc[g][:, lo:hi], in_=ld_grp[g][:, 4 * lo : 4 * hi]
             )
 
-        units = [(jb, g) for jb in BLOCK_ORDER[:3] for g in range(4)] + [(BLOCK_ORDER[3], q) for q in range(4)]
-        NU = len(units)
-        WIDE = 12
-        banks, planes, grouped, codes, scales, wins = {}, {}, {}, {}, {}, {}
-        o_banks = {}
+        def group(n):
+            return (PANELS[n // 4] + 2 + n) % 4
 
-        def direct(n, g):
-            return g in DIRECT.get(n, ())
+        def has_diag(n):
+            return n % 4 == 2
 
-        def is_diag(n):
-            return n < WIDE and units[n][0] == units[n][1]
+        banks, planes, grouped, codes, scales, out_banks = {}, {}, {}, {}, {}, {}
 
-        def s_pass(n, x):
-            jb, y = units[n]
-            s_bank = psum.tile([P, 512], F32, name="s_bank")
-            banks[n, x] = s_bank
-            if n in HALF_UNITS:
-                if x % 2 == 0:
-                    ts, c0, w = (x, x + 1), 0, 256
-                else:
-                    ts, c0, w = (0, 1, 2, 3), 256 + 64 * (x - 1), 128
-                for i, t in enumerate(ts):
-                    nc.tensor.matmul_mx(
-                        out=s_bank[:, w * i : w * i + w],
-                        lhsT=ld_codes[y][:, 128 * t : 128 * t + 128].bitcast(FP8X4),
-                        lhsT_scale=ld_sc[y][:, 128 * t : 128 * t + 128],
-                        rhs=lag_codes[jb][:, c0 : c0 + w].bitcast(FP8X4),
-                        rhs_scale=lag_sc[jb][:, c0 : c0 + w],
-                        start=True,
-                        stop=True,
+        def s_pass(bank, at, n, t, lo, hi):
+            g, k = group(n), n // 4
+            nc.tensor.matmul_mx(
+                out=bank[:, at : at + hi - lo],
+                lhsT=ld_codes[g][:, 128 * t : 128 * t + 128].bitcast(FP8X4),
+                lhsT_scale=ld_sc[g][:, 128 * t : 128 * t + 128],
+                rhs=lag_codes[k][:, lo:hi].bitcast(FP8X4),
+                rhs_scale=lag_sc[k][:, lo:hi],
+                start=True,
+                stop=True,
+            )
+
+        def off_diag(t):
+            return [(a, b) for a, b in ((0, 128 * t), (128 * t + 128, 512)) if b > a]
+
+        def fill(j):
+            if j >= len(jobs):
+                return
+            kind, n, x = jobs[j]
+            bank = psum.tile([P, 512], F32, name="ring%d" % (j % RING))
+            banks[j] = bank
+            if kind == "direct":
+                for t in range(4):
+                    s_pass(bank, 128 * t, n, t, 128 * x, 128 * x + 128)
+            elif kind == "diag":
+                for t in range(4):
+                    s_pass(bank, 128 * t, n, t, 128 * t, 128 * t + 128)
+            elif not has_diag(n):
+                s_pass(bank, 0, n, x, 0, 512)
+            else:
+                for lo, hi in ((0, 256), (256, 512)):
+                    if lo <= 128 * x < hi:
+                        lo = lo + 128 - (128 * x - lo)
+                        hi = lo + 128
+                    s_pass(bank, lo, n, x, lo, hi)
+
+        def planes_of(n):
+            if n not in planes:
+                planes[n] = work.tile([P, 4, 512], BF16, name="planes", bufs=3, align_bytes=64)
+            return planes[n]
+
+        def empty(j):
+            kind, n, x = jobs[j]
+            g, bank = group(n), banks[j]
+            if kind == "direct":
+                if x == 0:
+                    grouped[n] = work.tile([P, 2048], BF16, name="direct_grp", bufs=2, align_bytes=64)
+                nc.vector.tensor_tensor(
+                    out=grouped[n][:, 512 * x : 512 * x + 512].rearrange("p (c t) -> p c t", t=4),
+                    in0=bank[:].rearrange("p (t c) -> p c t", t=4),
+                    in1=gain_f[:, 4 * g : 4 * g + 4].unsqueeze(1).to_broadcast([P, 128, 4]),
+                    op=ALU.mult,
+                )
+            elif kind == "diag":
+                for t in range(4):
+                    nc.vector.scalar_tensor_tensor(
+                        out=planes_of(n)[:, t, 128 * t : 128 * t + 128],
+                        in0=bank[:, 128 * t : 128 * t + 128],
+                        scalar=gain_f[:, 4 * g + t : 4 * g + t + 1],
+                        in1=diag[:, 4 * g + t, :],
+                        op0=ALU.mult,
+                        op1=ALU.add,
                     )
-            elif n < WIDE:
-                nc.tensor.matmul_mx(
-                    out=s_bank[:],
-                    lhsT=ld_codes[y][:, 128 * x : 128 * x + 128].bitcast(FP8X4),
-                    lhsT_scale=ld_sc[y][:, 128 * x : 128 * x + 128],
-                    rhs=lag_codes[jb][:].bitcast(FP8X4),
-                    rhs_scale=lag_sc[jb][:],
-                    start=True,
-                    stop=True,
+            else:
+                for lo, hi in off_diag(x) if has_diag(n) else [(0, 512)]:
+                    nc.scalar.activation(
+                        out=planes_of(n)[:, x, lo:hi],
+                        in_=bank[:, lo:hi],
+                        func=ACT.Copy,
+                        scale=gain_f[:, 4 * g + x : 4 * g + x + 1],
+                    )
+
+        def interleave(n, lo, hi, on_gpsimd):
+            if hi <= lo:
+                return
+            if n not in grouped:
+                grouped[n] = work.tile([P, 2048], BF16, name="planed_grp", bufs=1, align_bytes=64)
+            dst, src = grouped[n][:, 4 * lo : 4 * hi], planes[n][:, :, lo:hi]
+            if on_gpsimd:
+                nc.gpsimd.tensor_scalar(
+                    out=dst.rearrange("p (c t) -> p c t", t=4),
+                    in0=src.rearrange("p t c -> p c t"),
+                    scalar1=1.0,
+                    scalar2=0.0,
+                    op0=ALU.mult,
+                    op1=ALU.add,
                 )
             else:
-                for t in range(4):
-                    nc.tensor.matmul_mx(
-                        out=s_bank[:, 128 * t : 128 * t + 128],
-                        lhsT=ld_codes[x][:, 128 * t : 128 * t + 128].bitcast(FP8X4),
-                        lhsT_scale=ld_sc[x][:, 128 * t : 128 * t + 128],
-                        rhs=lag_codes[jb][:, 128 * y : 128 * y + 128].bitcast(FP8X4),
-                        rhs_scale=lag_sc[jb][:, 128 * y : 128 * y + 128],
-                        start=True,
-                        stop=True,
-                    )
-
-        def x_alloc(n):
-            pl = work.tile([P, 4 * PITCH], BF16, name="pl", bufs=4, align_bytes=64)
-            gr = work.tile([P, 2048], BF16, name="gr", bufs=4, align_bytes=64)
-            co = work.tile([P, 512], U32, name="co", bufs=4, align_bytes=64)
-            sc = work.tile([P, 512], U8, name="sc", bufs=4, align_bytes=64)
-            planes[n], grouped[n], codes[n], scales[n] = pl, gr, co, sc
-            if is_diag(n) or n >= WIDE:
-                win = work.tile([P, 4, 128], F32, name="win", bufs=2)
-                wins[n] = win
-
-        def exit_scaled(dst, src, g, t):
-            nc.scalar.activation(out=dst, in_=src, func=ACT.Copy, scale=gain_f[:, 4 * g + t : 4 * g + t + 1])
-
-        def x_scalar(n, x):
-            jb, y = units[n]
-            bank = banks[n, x]
-            if n in HALF_UNITS:
-                if x % 2 == 0:
-                    for i in range(2):
-                        t = x + i
-                        exit_scaled(planes[n][:, 512 * t : 512 * t + 256], bank[:, 256 * i : 256 * i + 256], y, t)
-                return
-            if n < WIDE:
-                g, t = y, x
-                dst = planes[n][:, 512 * t : 512 * t + 512]
-                if g != jb:
-                    exit_scaled(dst, bank[:], g, t)
-                else:
-                    b4 = bank[:].rearrange("p (q c) -> p q c", q=4)
-                    d4 = dst.rearrange("p (q c) -> p q c", q=4)
-                    lo, hi = 32 * t, 32 * t + 32
-                    exit_scaled(wins[n][:, t, :].rearrange("p (q c) -> p q c", q=4), b4[:, :, lo:hi], g, t)
-                    if t > 0:
-                        exit_scaled(d4[:, :, 0:lo], b4[:, :, 0:lo], g, t)
-                    if t < 3:
-                        exit_scaled(d4[:, :, hi:128], b4[:, :, hi:128], g, t)
-            else:
-                g = x
-                if direct(n, g):
-                    return
-                for t in range(4):
-                    c = slice(128 * t, 128 * t + 128)
-                    dst = wins[n][:, t, :] if g == jb else planes[n][:, 512 * g + 128 * t : 512 * g + 128 * t + 128]
-                    exit_scaled(dst, bank[:, c], g, t)
-
-        def x_vector(n, x):
-            if n in HALF_UNITS and x % 2 == 1:
-                g, a = units[n][1], 1024 + 256 * (x - 1)
-            elif n >= WIDE and direct(n, x):
-                g, a = x, 512 * x
-            else:
-                return
-            nc.vector.tensor_tensor(
-                out=grouped[n][:, a : a + 512].rearrange("p (c t) -> p c t", t=4),
-                in0=banks[n, x][:].rearrange("p (t c) -> p c t", t=4),
-                in1=gain_f[:, 4 * g : 4 * g + 4].unsqueeze(1).to_broadcast([P, 128, 4]),
-                op=ALU.mult,
-            )
-
-        def add_windows(n):
-            g = units[n][1]
-            nc.vector.tensor_tensor(
-                out=planes[n][:].rearrange("p (t c) -> p t c", t=4)[:, :, 0:512].rearrange("p t (q c) -> p t q c", q=4)[
-                    :, :, :, 0:32
-                ],
-                in0=wins[n][:].rearrange("p t (q c) -> p t q c", q=4),
-                in1=diag[:, 4 * g : 4 * g + 4, :].rearrange("p t (q c) -> p t q c", q=4),
-                op=ALU.add,
-            )
-
-        def interleave(n, gs=(0, 1, 2, 3)):
-            if n < WIDE:
-                w = 256 if n in HALF_UNITS else 512
                 nc.vector.tensor_copy(
-                    out=grouped[n][:, 0 : 4 * w].rearrange("p (c i t) -> p c t i", i=4, t=4),
-                    in_=planes[n][:, 0:2048].rearrange("p (t c) -> p t c", t=4)[:, :, 0:w].rearrange(
-                        "p t (c i) -> p c t i", i=4
-                    ),
+                    out=dst.rearrange("p (c i t) -> p c t i", i=4, t=4), in_=src.rearrange("p t (c i) -> p c t i", i=4)
                 )
-                return
-            jb, q = units[n]
-            for g in gs:
-                if direct(n, g):
-                    continue
-                dst = grouped[n][:, 512 * g : 512 * g + 512]
-                if g == jb:
-                    nc.vector.tensor_tensor(
-                        out=dst.rearrange("p (c t) -> p c t", t=4),
-                        in0=wins[n][:].rearrange("p t c -> p c t"),
-                        in1=dmini[:, q, :, :],
-                        op=ALU.add,
-                    )
-                else:
-                    nc.vector.tensor_copy(
-                        out=dst.rearrange("p (c i t) -> p c t i", i=4, t=4),
-                        in_=planes[n][:, 512 * g : 512 * g + 512].rearrange("p (t c i) -> p c t i", t=4, i=4),
-                    )
 
-        def quant(n, lo=0, hi=512):
-            nc.vector.quantize_mx(
-                out=codes[n][:, lo:hi].bitcast(FP8X4), scales=scales[n][:, lo:hi], in_=grouped[n][:, 4 * lo : 4 * hi]
+        def quant(n):
+            codes[n] = work.tile([P, 512], U32, name="codes", bufs=4, align_bytes=64)
+            scales[n] = work.tile([P, 512], U8, name="scales", bufs=4, align_bytes=64)
+            nc.vector.quantize_mx(out=codes[n][:].bitcast(FP8X4), scales=scales[n][:], in_=grouped[n][:])
+
+        def out_pass(n, r, first, last):
+            k, g = n // 4, group(n)
+            if first:
+                out_banks[k, r] = psum.tile([P, 512], F32, name="out_bank%d" % r)
+            nc.tensor.matmul_mx(
+                out=out_banks[k, r][:],
+                lhsT=w_sb[:, g, 256 * r : 256 * r + 256].bitcast(FP4X4),
+                lhsT_scale=ws_sb[:, g, 128 * r : 128 * r + 128],
+                rhs=codes[n][:].bitcast(FP8X4),
+                rhs_scale=scales[n][:],
+                start=first,
+                stop=last,
             )
 
-        def w_op(g, r):
-            return w_sb[:, g, 256 * r : 256 * r + 256].bitcast(FP4X4), ws_sb[:, g, 128 * r : 128 * r + 128]
-
-        def o_pass(n, r):
-            jb, y = units[n]
-            if n < WIDE:
-                if y == 0:
-                    o_bank = psum.tile([P, 512], F32, name="o_bank")
-                    o_banks[n // 4, r] = o_bank
-                wc, ws = w_op(y, r)
-                nc.tensor.matmul_mx(
-                    out=o_banks[n // 4, r][:],
-                    lhsT=wc,
-                    lhsT_scale=ws,
-                    rhs=codes[n][:].bitcast(FP8X4),
-                    rhs_scale=scales[n][:],
-                    start=(y == 0),
-                    stop=(y == 3),
-                )
+        def out_exit(k, r, on_scalar=True):
+            jb = PANELS[k]
+            ot = work.tile([P, 512], F32, name="ot", bufs=6)
+            dst = ot[:].rearrange("p (m s) -> p m s", s=4)
+            src = out_banks[k, r][:].rearrange("p (s m) -> p m s", s=4)
+            if on_scalar:
+                nc.scalar.copy(out=dst, in_=src)
             else:
-                if r == 0:
-                    o_bank = psum.tile([P, 512], F32, name="o_bank")
-                    o_banks[n, 0] = o_bank
-                for g in range(4):
-                    wc, ws = w_op(g, r)
-                    nc.tensor.matmul_mx(
-                        out=o_banks[n, 0][:, 128 * r : 128 * r + 128],
-                        lhsT=wc,
-                        lhsT_scale=ws,
-                        rhs=codes[n][:, 128 * g : 128 * g + 128].bitcast(FP8X4),
-                        rhs_scale=scales[n][:, 128 * g : 128 * g + 128],
-                        start=(g == 0),
-                        stop=(g == 3),
-                    )
-
-        def o_exit(k, r):
-            jb = BLOCK_ORDER[k]
-            ot = work.tile([P, 512], F32, name="ot", bufs=8)
-            nc.scalar.copy(
-                out=ot[:].rearrange("p (q m s) -> p q m s", q=4, s=4),
-                in_=o_banks[k, r][:].rearrange("p (q s m) -> p q m s", q=4, s=4),
-            )
+                nc.vector.tensor_copy(out=dst, in_=src)
             nc.sync.dma_start(out=out[128 * r : 128 * r + 128, 512 * jb : 512 * jb + 512], in_=ot[:])
 
-        def o_exit_narrow(n):
-            jb, q = units[n]
-            j0 = 512 * jb + 128 * q
-            ot = work.tile([P, 512], F32, name="ot", bufs=8)
-            dst = ot[:].rearrange("p (r m s) -> p r m s", r=4, s=4)
-            src = o_banks[n, 0][:].rearrange("p (r s m) -> p r m s", r=4, s=4)
-            hbm = out[:, j0 : j0 + 128].rearrange("(r p) j -> p r j", p=P)
-            o3 = ot[:].rearrange("p (r j) -> p r j", r=4)
-            nc.scalar.copy(out=dst, in_=src)
-            nc.sync.dma_start(out=hbm, in_=o3)
+        jobs, period_jobs = [], []
+        for pi in range(PERIODS + 1):
+            mine = []
+            if pi >= 1:
+                mine = mine + [("direct", 2 * pi - 1, q) for q in range(4)]
+            if pi < PERIODS and has_diag(2 * pi):
+                mine = mine + [("diag", 2 * pi, 0)]
+            if pi < PERIODS:
+                mine = mine + [("planed", 2 * pi, t) for t in range(4)]
+            period_jobs.append(list(range(len(jobs), len(jobs) + len(mine))))
+            jobs.extend(mine)
 
-        def finish(n):
-            jb, q = units[n]
-            j0 = 512 * jb + 128 * q
-            accs = []
-            for r in range(4):
-                s_bank = psum.tile([P, 512], F32, name="s_bank")
-                accs.append(s_bank)
-            for g in range(4):
-                for r in range(4):
-                    wc, ws = w_op(g, r)
-                    nc.tensor.matmul_mx(
-                        out=accs[r][:, 0:128],
-                        lhsT=wc,
-                        lhsT_scale=ws,
-                        rhs=codes[n][:, 128 * g : 128 * g + 128].bitcast(FP8X4),
-                        rhs_scale=scales[n][:, 128 * g : 128 * g + 128],
-                        start=(g == 0),
-                        stop=(g == 3),
-                    )
-            ot = work.tile([P, 512], F32, name="ot", bufs=8)
-            o3 = ot[:].rearrange("p (r j) -> p r j", r=4)
-            hbm = out[:, j0 : j0 + 128].rearrange("(r p) j -> p r j", p=P)
-            for r in range(4):
-                dst = o3[:, r, :].rearrange("p (m s) -> p m s", s=4)
-                src = accs[r][:, 0:128].rearrange("p (s m) -> p m s", s=4)
-                if r % 2 == 0:
-                    nc.scalar.copy(out=dst, in_=src)
-                else:
-                    nc.vector.tensor_copy(out=dst, in_=src)
-                    nc.sync.dma_start(out=hbm[:, r - 1 : r + 1], in_=o3[:, r - 1 : r + 1])
-
-        jb0 = BLOCK_ORDER[0]
-        lag_alloc(jb0)
-        lag_widen(jb0, 3, True)
-        for t in range(3):
-            lag_widen(jb0, t, False)
-        if PE_HEAD:
-            loads_turn(0, 0)
-            lag_turn(jb0, 0)
-            loads_exit(0, 0)
-            lag_exit(jb0, 0)
-            loads_turn(0, 1)
-            lag_turn(jb0, 1)
-            lag_exit(jb0, 1)
-            loads_exit(0, 1)
-        else:
-            loads_turn(0, 0)
-            loads_exit(0, 0)
-            loads_turn(0, 1)
-            loads_exit(0, 1)
-            lag_interleave(jb0, 0)
-            lag_interleave(jb0, 1)
-        loads_quant(0, 0, 256)
-        lag_quant(jb0)
-        loads_quant(0, 256, 512)
-        for h in range(2):
-            loads_turn(1, h)
-            loads_exit(1, h)
-        o_bank = psum.tile([P, 1024], BF16, name="o_bank")
-        for t in range(4):
-            nc.tensor.transpose(o_bank[:, 128 * t : 128 * t + 128], gp_rows[:, t:512:4], ident_b[:])
+        loads_turn(0, 0)
+        loads_turn(0, 1)
+        bank = side_bank()
+        for u in range(2):
+            nc.tensor.transpose(bank[:, 128 * u : 128 * u + 128], gp_rows[:].bitcast(F32)[:, u:256:2], ident[:])
+        for t in (3, 0, 1, 2):
+            lag_widen(0, t)
+        loads_exit(0, 0)
+        loads_exit(0, 1)
         nc.scalar.copy(
-            out=gp_f[:].rearrange("p a (g t) -> p a g t", t=4),
-            in_=o_bank[:, 0:512].rearrange("p (t r) -> p t r", t=4)[:, :, 0:8].rearrange("p t (a g) -> p a g t", a=2),
+            out=gp_f[:].rearrange("p a (g u e) -> p (a g) u e", u=2, e=2),
+            in_=bank[:, 0:256].bitcast(BF16).rearrange("p (u r e) -> p r u e", u=2, e=2)[:, 0:8],
         )
-        lag_alloc(BLOCK_ORDER[1])
-        for t in range(4):
-            lag_widen(BLOCK_ORDER[1], t, t < WS0)
-        loads_quant(1)
-
-        jobs = []
-        for n in range(NU):
-            for x in range(4):
-                jobs.append(("unit", n, x))
-                k = n // 4
-                if n < 12 and k in PE_LAG and (n % 4, x) in LAG_AT[k]:
-                    jobs.append(("lag", k, LAG_AT[k].index((n % 4, x))))
-
-        def fill(job):
-            kind, a, b = job
-            if kind == "lag":
-                lag_turn(BLOCK_ORDER[a + 1], b)
-            else:
-                s_pass(a, b)
-
-        def vector_work(n, x):
-            k = n // 4
-            if n == 0:
-                if x == 1:
-                    lag_interleave(BLOCK_ORDER[1], 0)
-                    lag_interleave(BLOCK_ORDER[1], 1)
-                    for jb in BLOCK_ORDER[:ND]:
-                        build_diag(jb)
-                if x == 2:
-                    loads_quant(2)
-                if x == 3:
-                    if not T3S:
-                        loads_exit(3, 0, on_scalar=False)
-                        loads_exit(3, 1, on_scalar=False)
-                    lag_quant(BLOCK_ORDER[1])
-                    if not T3S:
-                        loads_quant(3)
-                return
-            if T3S and n == 1 and x == 1:
-                loads_quant(3)
-            if x == 0 and is_diag(n - 1):
-                add_windows(n - 1)
-            if x == V_OTHER:
-                if n in (2, 4, 5) and {2: 1, 4: 2, 5: 3}[n] >= ND:
-                    build_diag(BLOCK_ORDER[{2: 1, 4: 2, 5: 3}[n]])
-                if n in (3, 7):
-                    jb = BLOCK_ORDER[k + 2]
-                    lag_alloc(jb)
-                    for t in range(4):
-                        lag_widen(jb, t, t < WS[k])
-                if n in (5, 9) and k not in PE_LAG:
-                    lag_interleave(BLOCK_ORDER[k + 1], 0)
-                    lag_interleave(BLOCK_ORDER[k + 1], 1)
-                if n in (6, 10):
-                    lag_quant(BLOCK_ORDER[k + 1])
-            if x == V_INT:
-                interleave(n - 1)
-            if x == V_Q:
-                if n < V_SWITCH and n >= 2:
-                    quant(n - 2)
-                if n == V_SWITCH:
-                    quant(n - 2)
-                if n >= V_SWITCH:
-                    quant(n - 1)
-
-        o_done = [0]
-
-        def out_passes(step, most):
-            for i in range(most):
-                o = o_done[0]
-                if o >= 4 * (NU - 1) or o + O_D[o // 16] > step:
-                    return
-                if o % 16 < 4 and o >= 16:
-                    o_exit(o // 16 - 1, o % 16)
-                o_pass(o // 4, o % 4)
-                if o // 4 >= WIDE and o % 4 == 3:
-                    o_exit_narrow(o // 4)
-                o_done[0] = o + 1
-
-        for job in jobs[:4]:
-            fill(job)
+        lag_interleave(0, 0)
+        lag_interleave(0, 1)
+        loads_quant(0, 0, 256)
+        lag_quant(0)
+        loads_quant(0, 256, 512)
+        loads_turn(1, 0)
+        loads_exit(1, 0)
+        fill(0)
+        fill(1)
+        loads_turn(1, 1)
+        fill(2)
+        fill(3)
         loads_turn(2, 0)
         loads_turn(2, 1)
-        step = 0
-        for j, (kind, n, x) in enumerate(jobs):
-            if kind == "lag":
-                lag_exit(BLOCK_ORDER[n + 1], x)
-                if j + 4 < len(jobs):
-                    fill(jobs[j + 4])
-                continue
-            if x == 0:
-                x_alloc(n)
-            x_scalar(n, x)
-            x_vector(n, x)
-            if n == 0 and x in (1, 2):
-                loads_exit(2, x - 1)
-            if T3S and step in (3, 5):
-                loads_exit(3, (step - 3) // 2)
-            if j + 4 < len(jobs):
-                fill(jobs[j + 4])
-            if n == 0 and x in T3_AT:
-                loads_turn(3, T3_AT.index(x))
-            vector_work(n, x)
-            out_passes(step, 2)
-            step += 1
-        if V_SWITCH > NU - 1:
-            quant(NU - 2)
-        interleave(NU - 1, (0, 1, 2))
-        quant(NU - 1, 0, 256)
-        interleave(NU - 1, (3,))
-        quant(NU - 1, 256, 512)
-        out_passes(1000, 1000)
-        finish(NU - 1)
+
+        for t in range(4):
+            lag_widen(1, t)
+        empty(0)
+        loads_exit(1, 1)
+        build_diag(0)
+        lag_interleave(1, 0)
+        loads_quant(1)
+        fill(4)
+        empty(1)
+        loads_exit(2, 0, G2_S[0])
+        fill(5)
+        loads_turn(3, 0)
+        empty(2)
+        loads_exit(2, 1, G2_S[1])
+        lag_interleave(1, 1)
+        loads_quant(2)
+        fill(6)
+        loads_turn(3, 1)
+        empty(3)
+        fill(7)
+
+        def scalar_extras(pi):
+            k = (pi + 3) // 2
+            widen = [(lag_widen, (k, 2 * (1 - pi % 2) + i)) for i in range(2)] if k < 4 else []
+            exits = [(out_exit, ((pi - 3) // 2, 2 * ((pi - 3) % 2) + i)) for i in range(2)] if pi >= 3 else []
+            if pi == 1:
+                return [(loads_exit, (3, 0)), (loads_exit, (3, 1))] + widen
+            if pi % 2 == 0:
+                return exits + widen
+            turn = [(lag_interleave, (k - 1, 0))] if k <= 4 and LAG_S[k - 1] else []
+            return (widen + [None, None])[:2] + exits[:1] + turn + [None] * (1 - len(turn)) + exits[1:]
+
+        def vector_shared(pi):
+            k = pi // 2 + 1
+            n = 2 * pi - 2
+            if pi == 1:
+                loads_quant(3)
+            if pi % 2 == 0 and pi < PERIODS:
+                build_diag(pi // 2)
+            if 1 < k < 4 and pi % 2 == 0:
+                lag_interleave(k, 1)
+            if 1 < k < 4 and pi % 2 == 1 and not LAG_S[k]:
+                lag_interleave(k, 0)
+            interleave(n, G_COLS[int(has_diag(n + 2))], 512, False)
+            if k < 4 and pi % 2 == 1:
+                lag_quant(k)
+            if pi < PERIODS:
+                quant(n + 1)
+                quant(n)
+            else:
+                quant(n)
+                quant(n + 1)
+
+        for pi in range(1, PERIODS + 1):
+            passes = []
+            if pi >= 2:
+                n = 2 * pi - 4
+                for r in range(4):
+                    passes = passes + [(n + 1, r, pi % 2 == 0, False), (n, r, False, pi % 2 == 1)]
+            interleave(2 * pi - 2, 0, G_COLS[int(has_diag(2 * pi))], True)
+            extras = scalar_extras(pi)
+            mine = period_jobs[pi]
+            last_vector = max([i for i, j in enumerate(mine) if jobs[j][0] != "planed"])
+            for i, j in enumerate(mine):
+                if passes:
+                    out_pass(*passes.pop(0))
+                for item in extras[i : i + 1] if i < last_vector else extras[i:]:
+                    if item and i <= last_vector:
+                        item[0](*item[1])
+                empty(j)
+                if i == last_vector:
+                    vector_shared(pi)
+                fill(j + RING)
+            while passes:
+                out_pass(*passes.pop(0))
+
+        for r in range(4):
+            out_pass(14, r, False, False)
+        for r in range(4):
+            out_pass(15, r, False, True)
+            out_exit(3, r, on_scalar=(r % 2 == 0))

@@ -20,7 +20,7 @@ FLOPS = 2 * M * K * M + 2 * R * M * M
 P = 128
 PANELS = (2, 3, 0, 1)
 PERIODS = 8
-G_COLS = (384, 512)
+G_COLS = (256, 256)
 WIDEN_V = (3, 4, 0, 0)
 LAG_S = (0, 0, 1, 1)
 RING = 4

@@ -18,13 +18,16 @@ M, K, R = 2048, 512, 512
 FLOPS = 2 * M * K * M + 2 * R * M * M
 
 P = 128
-PANELS = (2, 3, 0, 1)
+PANELS = (0, 1, 2, 3)
 PERIODS = 8
-G_COLS = (256, 256)
-WIDEN_V = (3, 4, 0, 0)
-LAG_S = (0, 0, 1, 1)
+G_COLS = (352, 448)
+WIDEN_V = (3, 2, 0, 0)
+LAG_S = (0, 1, 1, 1)
 RING = 4
-G2_S = (True, True)
+G_LAST = 288
+AHEAD = 1
+REST_S = ()
+DIAG_V = (1, 0, 0, 0)
 
 
 def tile_spike_covariance_readout_s13_kernel(
@@ -38,13 +41,11 @@ def tile_spike_covariance_readout_s13_kernel(
         ctx.enter_context(tc.manual_schedule())
 
         gp_rows = keep.tile([P, 512], BF16, name="gp_rows")
-        nc.vector.memset(gp_rows[:].bitcast(I32), 0)
+        nc.gpsimd.memset(gp_rows[:].bitcast(I32), 0)
         ident = keep.tile([P, P], F32, name="ident")
         make_identity(nc, ident[:])
         lagsc = keep.tile([P, 4], F32, name="lagsc")
         nc.scalar.dma_start(out=lagsc[:], in_=lag_scale.rearrange("(p t) o -> p (t o)", t=4))
-        nc.scalar.dma_start(out=gp_rows[0:4, :], in_=gain.rearrange("(g x) -> g x", g=4))
-        nc.scalar.dma_start(out=gp_rows[4:8, :], in_=private.rearrange("(g x) -> g x", g=4))
 
         lag_view = lag_bytes.rearrange("(p t) j -> p t j", t=4)
         lag_raw, rows = {}, {}
@@ -52,8 +53,8 @@ def tile_spike_covariance_readout_s13_kernel(
         def load_lag(k, parts):
             jb = PANELS[k]
             lraw = keep.tile([P, 4, 512], U8, name="lraw%d" % k, align_bytes=64)
-            step = 4 // parts
-            for a in range(0, 4, step):
+            step = 4 // len(parts)
+            for a in parts:
                 nc.sync.dma_start(out=lraw[:, a : a + step, :], in_=lag_view[:, a : a + step, 512 * jb : 512 * jb + 512])
             lag_raw[k] = lraw
 
@@ -66,12 +67,15 @@ def tile_spike_covariance_readout_s13_kernel(
                 for t in range(step):
                     rows[g, a + t] = tile[:, t, :]
 
-        load_lag(0, 2)
+        load_lag(0, (2, 0))
         load_rows(0, 2)
+        nc.sync.dma_start(out=gp_rows[0:4, :], in_=gain.rearrange("(g x) -> g x", g=4))
+        nc.sync.dma_start(out=gp_rows[4:8, :], in_=private.rearrange("(g x) -> g x", g=4))
         load_rows(1, 1)
-        load_lag(1, 1)
+        load_lag(1, (0,))
         load_rows(2, 1)
         load_rows(3, 1)
+        load_lag(2, (0,))
         w_sb = keep.tile([P, 4, 1024], U8, name="w_sb", align_bytes=64)
         nc.sync.dma_start(out=w_sb[:], in_=w_words.rearrange("g p n -> p g n"))
         ws_sb = keep.tile([P, 4, 512], U8, name="ws_sb", align_bytes=64)
@@ -82,8 +86,7 @@ def tile_spike_covariance_readout_s13_kernel(
                 out=ws_sb[32 * quad : 32 * quad + 4, :, :].bitcast(I32),
                 in_=ws_view[4 * quad : 4 * quad + 4, :, :],
             )
-        load_lag(2, 1)
-        load_lag(3, 1)
+        load_lag(3, (0,))
 
         gp_f = keep.tile([P, 2, 16], F32, name="gp_f")
         gain_f, priv_f = gp_f[:, 0, :], gp_f[:, 1, :]
@@ -99,9 +102,12 @@ def tile_spike_covariance_readout_s13_kernel(
         def build_diag(k):
             for t in range(4):
                 i = 4 * PANELS[k] + t
-                nc.vector.tensor_scalar(
-                    out=diag[:, i, :], in0=ident[:], scalar1=priv_f[:, i : i + 1], scalar2=None, op0=ALU.mult
-                )
+                if DIAG_V[k]:
+                    nc.vector.tensor_scalar(
+                        out=diag[:, i, :], in0=ident[:], scalar1=priv_f[:, i : i + 1], scalar2=None, op0=ALU.mult
+                    )
+                else:
+                    nc.scalar.activation(out=diag[:, i, :], in_=ident[:], func=ACT.Copy, scale=priv_f[:, i : i + 1])
 
         lag_planes, lag_grp, lag_codes, lag_sc = {}, {}, {}, {}
         ld_grp, ld_codes, ld_sc, turned = {}, {}, {}, {}
@@ -162,10 +168,10 @@ def tile_spike_covariance_readout_s13_kernel(
             )
 
         def group(n):
-            return (PANELS[n // 4] + 2 + n) % 4
+            return (PANELS[n // 4] + n) % 4
 
         def has_diag(n):
-            return n % 4 == 2
+            return n % 4 == 0
 
         banks, planes, grouped, codes, scales, out_banks = {}, {}, {}, {}, {}, {}
 
@@ -241,13 +247,13 @@ def tile_spike_covariance_readout_s13_kernel(
                         scale=gain_f[:, 4 * g + x : 4 * g + x + 1],
                     )
 
-        def interleave(n, lo, hi, on_gpsimd):
+        def interleave(n, lo, hi, engine):
             if hi <= lo:
                 return
             if n not in grouped:
                 grouped[n] = work.tile([P, 2048], BF16, name="planed_grp", bufs=1, align_bytes=64)
             dst, src = grouped[n][:, 4 * lo : 4 * hi], planes[n][:, :, lo:hi]
-            if on_gpsimd:
+            if engine == "gpsimd":
                 nc.gpsimd.tensor_scalar(
                     out=dst.rearrange("p (c t) -> p c t", t=4),
                     in0=src.rearrange("p t c -> p c t"),
@@ -257,14 +263,16 @@ def tile_spike_covariance_readout_s13_kernel(
                     op1=ALU.add,
                 )
             else:
-                nc.vector.tensor_copy(
-                    out=dst.rearrange("p (c i t) -> p c t i", i=4, t=4), in_=src.rearrange("p t (c i) -> p c t i", i=4)
-                )
+                copy = nc.vector.tensor_copy if engine == "vector" else nc.scalar.copy
+                copy(out=dst.rearrange("p (c i t) -> p c t i", i=4, t=4), in_=src.rearrange("p t (c i) -> p c t i", i=4))
 
-        def quant(n):
-            codes[n] = work.tile([P, 512], U32, name="codes", bufs=4, align_bytes=64)
-            scales[n] = work.tile([P, 512], U8, name="scales", bufs=4, align_bytes=64)
-            nc.vector.quantize_mx(out=codes[n][:].bitcast(FP8X4), scales=scales[n][:], in_=grouped[n][:])
+        def quant(n, lo=0, hi=512):
+            if lo == 0:
+                codes[n] = work.tile([P, 512], U32, name="codes", bufs=4, align_bytes=64)
+                scales[n] = work.tile([P, 512], U8, name="scales", bufs=4, align_bytes=64)
+            nc.vector.quantize_mx(
+                out=codes[n][:, lo:hi].bitcast(FP8X4), scales=scales[n][:, lo:hi], in_=grouped[n][:, 4 * lo : 4 * hi]
+            )
 
         def out_pass(n, r, first, last):
             k, g = n // 4, group(n)
@@ -291,15 +299,14 @@ def tile_spike_covariance_readout_s13_kernel(
                 nc.vector.tensor_copy(out=dst, in_=src)
             nc.sync.dma_start(out=out[128 * r : 128 * r + 128, 512 * jb : 512 * jb + 512], in_=ot[:])
 
-        jobs, period_jobs = [], []
-        for pi in range(PERIODS + 1):
-            mine = []
-            if pi >= 1:
-                mine = mine + [("direct", 2 * pi - 1, q) for q in range(4)]
-            if pi < PERIODS and has_diag(2 * pi):
-                mine = mine + [("diag", 2 * pi, 0)]
-            if pi < PERIODS:
-                mine = mine + [("planed", 2 * pi, t) for t in range(4)]
+        jobs = [("planed", 0, 0), ("planed", 0, 1), ("diag", 0, 0), ("planed", 0, 2), ("planed", 0, 3)]
+        period_jobs = [list(range(5))]
+        for pi in range(1, PERIODS + 1):
+            direct = [("direct", 2 * pi - 1, q) for q in range(4)]
+            planed = [("planed", 2 * pi, t) for t in range(4)] if pi < PERIODS else []
+            windows = [("diag", 2 * pi, 0)] if pi < PERIODS and has_diag(2 * pi) else []
+            ahead = int(pi > 1)
+            mine = direct[:3] + planed[:ahead] + direct[3:] + windows + planed[ahead:]
             period_jobs.append(list(range(len(jobs), len(jobs) + len(mine))))
             jobs.extend(mine)
 
@@ -308,105 +315,129 @@ def tile_spike_covariance_readout_s13_kernel(
         bank = side_bank()
         for u in range(2):
             nc.tensor.transpose(bank[:, 128 * u : 128 * u + 128], gp_rows[:].bitcast(F32)[:, u:256:2], ident[:])
-        for t in (3, 0, 1, 2):
+        for t in (3, 2, 0, 1):
             lag_widen(0, t)
         loads_exit(0, 0)
+        lag_interleave(0, 0)
+        lag_interleave(0, 1)
         loads_exit(0, 1)
         nc.scalar.copy(
             out=gp_f[:].rearrange("p a (g u e) -> p (a g) u e", u=2, e=2),
             in_=bank[:, 0:256].bitcast(BF16).rearrange("p (u r e) -> p r u e", u=2, e=2)[:, 0:8],
         )
-        lag_interleave(0, 0)
-        lag_interleave(0, 1)
-        loads_quant(0, 0, 256)
         lag_quant(0)
+        loads_quant(0, 0, 256)
         loads_quant(0, 256, 512)
         loads_turn(1, 0)
-        loads_exit(1, 0)
-        fill(0)
-        fill(1)
         loads_turn(1, 1)
-        fill(2)
-        fill(3)
+        for j in range(RING):
+            fill(j)
         loads_turn(2, 0)
         loads_turn(2, 1)
 
-        for t in range(4):
-            lag_widen(1, t)
-        empty(0)
+        loads_exit(1, 0)
         loads_exit(1, 1)
         build_diag(0)
-        lag_interleave(1, 0)
+        for t in range(WIDEN_V[1]):
+            lag_widen(1, t)
         loads_quant(1)
+        empty(0)
         fill(4)
         empty(1)
-        loads_exit(2, 0, G2_S[0])
         fill(5)
-        loads_turn(3, 0)
         empty(2)
-        loads_exit(2, 1, G2_S[1])
-        lag_interleave(1, 1)
-        loads_quant(2)
-        fill(6)
-        loads_turn(3, 1)
         empty(3)
+        fill(6)
         fill(7)
+        loads_turn(3, 0)
+        empty(4)
+        fill(8)
+        loads_turn(3, 1)
+
+        def run(items):
+            for item in items:
+                if item:
+                    item[0](*item[1])
 
         def scalar_extras(pi):
             k = (pi + 3) // 2
-            widen = [(lag_widen, (k, 2 * (1 - pi % 2) + i)) for i in range(2)] if k < 4 else []
-            exits = [(out_exit, ((pi - 3) // 2, 2 * ((pi - 3) % 2) + i)) for i in range(2)] if pi >= 3 else []
+            widen = [(lag_widen, (k, t)) for t in range(4)] if k < 4 else []
+            exits = [(out_exit, ((pi - 3) // 2, r)) for r in range(4)] if pi >= 3 else []
             if pi == 1:
-                return [(loads_exit, (3, 0)), (loads_exit, (3, 1))] + widen
-            if pi % 2 == 0:
-                return exits + widen
-            turn = [(lag_interleave, (k - 1, 0))] if k <= 4 and LAG_S[k - 1] else []
-            return (widen + [None, None])[:2] + exits[:1] + turn + [None] * (1 - len(turn)) + exits[1:]
+                turned_out = [(loads_exit, (g, h)) for g in (2, 3) for h in range(2)]
+                rest = [(lag_widen, (1, t)) for t in range(WIDEN_V[1], 4)]
+                return turned_out[:2] + rest + turned_out[2:] + [(lag_interleave, (1, 0))], widen[:2]
+            rest = [(interleave, (2 * pi - 2, G_COLS[1 - pi % 2], 512, "scalar"))] if pi in REST_S else []
+            if pi % 2 == 1:
+                turn = [(lag_interleave, (k - 1, 1))] if k <= 4 and LAG_S[k - 1] == 2 else []
+                return turn + rest + widen[:1] + exits[:2], exits[2:3] * (pi < PERIODS - 1) + widen[1:2]
+            turn = [(lag_interleave, (k, 0))] if k < 4 and LAG_S[k] else []
+            return [(build_diag, (pi // 2,))] + rest + exits[3:] + widen[2:], turn
 
         def vector_shared(pi):
             k = pi // 2 + 1
             n = 2 * pi - 2
             if pi == 1:
+                loads_quant(2)
+            if pi not in REST_S and pi % 2 == 1:
+                interleave(n, G_COLS[0], 512, "vector")
+            quant(n + 1)
+            if pi == 1:
+                lag_interleave(1, 1)
                 loads_quant(3)
-            if pi % 2 == 0 and pi < PERIODS:
-                build_diag(pi // 2)
-            if 1 < k < 4 and pi % 2 == 0:
-                lag_interleave(k, 1)
-            if 1 < k < 4 and pi % 2 == 1 and not LAG_S[k]:
-                lag_interleave(k, 0)
-            interleave(n, G_COLS[int(has_diag(n + 2))], 512, False)
             if k < 4 and pi % 2 == 1:
                 lag_quant(k)
-            if pi < PERIODS:
-                quant(n + 1)
-                quant(n)
-            else:
-                quant(n)
-                quant(n + 1)
+            if pi % 2 == 0:
+                if pi not in REST_S:
+                    interleave(n, G_COLS[1], 512, "vector")
+                for h in range(LAG_S[k] if k < 4 else 2, 2):
+                    lag_interleave(k, h)
+            quant(n)
 
-        for pi in range(1, PERIODS + 1):
-            passes = []
-            if pi >= 2:
-                n = 2 * pi - 4
-                for r in range(4):
-                    passes = passes + [(n + 1, r, pi % 2 == 0, False), (n, r, False, pi % 2 == 1)]
-            interleave(2 * pi - 2, 0, G_COLS[int(has_diag(2 * pi))], True)
-            extras = scalar_extras(pi)
+        def unit_pass(n, r):
+            out_pass(n, r, n % 4 == 1, n % 4 == 2)
+
+        def early_passes(pi):
+            n = 2 * pi - 4
+            return [(unit_pass, (n, r)) for r in range(AHEAD)] + [
+                (unit_pass, (m, r)) for r in range(AHEAD, 4) for m in (n + 1, n)
+            ]
+
+        for pi in range(1, PERIODS):
+            interleave(2 * pi - 2, 0, G_COLS[int(has_diag(2 * pi))], "gpsimd")
+            early, late = scalar_extras(pi)
             mine = period_jobs[pi]
             last_vector = max([i for i, j in enumerate(mine) if jobs[j][0] != "planed"])
+            passes = early_passes(pi) if pi >= 2 else []
+            passes = passes + [None] * (8 - AHEAD - len(passes)) + [(unit_pass, (2 * pi - 1, r)) for r in range(AHEAD)]
+            passes = passes[: 8 - AHEAD] + [None] * (len(mine) - 7) + passes[8 - AHEAD :]
+            run(passes[:1])
             for i, j in enumerate(mine):
-                if passes:
-                    out_pass(*passes.pop(0))
-                for item in extras[i : i + 1] if i < last_vector else extras[i:]:
-                    if item and i <= last_vector:
-                        item[0](*item[1])
+                run(passes[i + 1 : i + 2])
                 empty(j)
+                if i == 3:
+                    run(early)
                 if i == last_vector:
                     vector_shared(pi)
-                fill(j + RING)
-            while passes:
-                out_pass(*passes.pop(0))
+                    if pi == 1:
+                        for held in mine[:3]:
+                            fill(held + RING)
+                if pi > 1 or i >= last_vector:
+                    fill(j + RING)
+            run(late)
 
+        interleave(14, 0, G_LAST, "gpsimd")
+        out_exit(2, 2)
+        interleave(14, G_LAST, 512, "scalar")
+        out_exit(2, 3)
+        last = period_jobs[PERIODS]
+        run(early_passes(PERIODS))
+        for j in last[:3]:
+            empty(j)
+        quant(14)
+        empty(last[3])
+        quant(15, 0, 256)
+        quant(15, 256, 512)
         for r in range(4):
             out_pass(14, r, False, False)
         for r in range(4):

@@ -42,6 +42,13 @@ def tile_spike_covariance_readout_s13_kernel(
 
         gp_rows = keep.tile([P, 512], BF16, name="gp_rows")
         nc.gpsimd.memset(gp_rows[:].bitcast(I32), 0)
+        idle = keep.tile([P, 512], F32, name="idle")
+        nc.vector.memset(idle[:], 0.0)
+
+        def warm_up(width):
+            bank = psum.tile([P, 512], F32, name="ring%d" % (RING - 1))
+            nc.tensor.matmul(out=bank[:, 0:width], lhsT=idle[:, 0:P], rhs=idle[:, 0:width], start=True, stop=True)
+
         ident = keep.tile([P, P], F32, name="ident")
         make_identity(nc, ident[:])
         lagsc = keep.tile([P, 4], F32, name="lagsc")
@@ -310,6 +317,8 @@ def tile_spike_covariance_readout_s13_kernel(
             period_jobs.append(list(range(len(jobs), len(jobs) + len(mine))))
             jobs.extend(mine)
 
+        warm_up(512)
+        warm_up(128)
         loads_turn(0, 0)
         loads_turn(0, 1)
         bank = side_bank()
@@ -328,6 +337,7 @@ def tile_spike_covariance_readout_s13_kernel(
         lag_quant(0)
         loads_quant(0, 0, 256)
         loads_quant(0, 256, 512)
+        warm_up(256)
         loads_turn(1, 0)
         loads_turn(1, 1)
         for j in range(RING):

@@ -21,13 +21,13 @@ P = 128
 PANELS = (0, 1, 2, 3)
 PERIODS = 8
 G_COLS = (352, 448)
-WIDEN_V = (3, 2, 0, 0)
+WIDEN_V = (3, 4, 0, 0)
 LAG_S = (0, 1, 1, 1)
 RING = 4
-G_LAST = 288
+G_LAST = 240
 AHEAD = 1
 REST_S = ()
-DIAG_V = (1, 0, 0, 0)
+DIAG_V = (0, 0, 0, 0)
 
 
 def tile_spike_covariance_readout_s13_kernel(
@@ -43,7 +43,7 @@ def tile_spike_covariance_readout_s13_kernel(
         gp_rows = keep.tile([P, 512], BF16, name="gp_rows")
         nc.gpsimd.memset(gp_rows[:].bitcast(I32), 0)
         idle = keep.tile([P, 512], F32, name="idle")
-        nc.vector.memset(idle[:], 0.0)
+        nc.vector.memset(idle[:].bitcast(I32), 0)
 
         def warm_up(width):
             bank = psum.tile([P, 512], F32, name="ring%d" % (RING - 1))
@@ -74,7 +74,7 @@ def tile_spike_covariance_readout_s13_kernel(
                 for t in range(step):
                     rows[g, a + t] = tile[:, t, :]
 
-        load_lag(0, (2, 0))
+        load_lag(0, (0, 3, 1, 2))
         load_rows(0, 2)
         nc.sync.dma_start(out=gp_rows[0:4, :], in_=gain.rearrange("(g x) -> g x", g=4))
         nc.sync.dma_start(out=gp_rows[4:8, :], in_=private.rearrange("(g x) -> g x", g=4))
@@ -295,16 +295,16 @@ def tile_spike_covariance_readout_s13_kernel(
                 stop=last,
             )
 
-        def out_exit(k, r, on_scalar=True):
-            jb = PANELS[k]
+        def out_exit(k, r, on_scalar=True, parts=1):
             ot = work.tile([P, 512], F32, name="ot", bufs=6)
             dst = ot[:].rearrange("p (m s) -> p m s", s=4)
             src = out_banks[k, r][:].rearrange("p (s m) -> p m s", s=4)
-            if on_scalar:
-                nc.scalar.copy(out=dst, in_=src)
-            else:
-                nc.vector.tensor_copy(out=dst, in_=src)
-            nc.sync.dma_start(out=out[128 * r : 128 * r + 128, 512 * jb : 512 * jb + 512], in_=ot[:])
+            copy = nc.scalar.copy if on_scalar else nc.vector.tensor_copy
+            step = 128 // parts
+            for m in range(0, 128, step):
+                copy(out=dst[:, m : m + step], in_=src[:, m : m + step])
+                j = 512 * PANELS[k] + 4 * m
+                nc.sync.dma_start(out=out[128 * r : 128 * r + 128, j : j + 4 * step], in_=ot[:, 4 * m : 4 * (m + step)])
 
         jobs = [("planed", 0, 0), ("planed", 0, 1), ("diag", 0, 0), ("planed", 0, 2), ("planed", 0, 3)]
         period_jobs = [list(range(5))]
@@ -324,7 +324,7 @@ def tile_spike_covariance_readout_s13_kernel(
         bank = side_bank()
         for u in range(2):
             nc.tensor.transpose(bank[:, 128 * u : 128 * u + 128], gp_rows[:].bitcast(F32)[:, u:256:2], ident[:])
-        for t in (3, 2, 0, 1):
+        for t in (0, 3, 1, 2):
             lag_widen(0, t)
         loads_exit(0, 0)
         lag_interleave(0, 0)
@@ -334,8 +334,8 @@ def tile_spike_covariance_readout_s13_kernel(
             out=gp_f[:].rearrange("p a (g u e) -> p (a g) u e", u=2, e=2),
             in_=bank[:, 0:256].bitcast(BF16).rearrange("p (u r e) -> p r u e", u=2, e=2)[:, 0:8],
         )
-        lag_quant(0)
         loads_quant(0, 0, 256)
+        lag_quant(0)
         loads_quant(0, 256, 512)
         warm_up(256)
         loads_turn(1, 0)
@@ -343,11 +343,10 @@ def tile_spike_covariance_readout_s13_kernel(
         for j in range(RING):
             fill(j)
         loads_turn(2, 0)
-        loads_turn(2, 1)
 
+        build_diag(0)
         loads_exit(1, 0)
         loads_exit(1, 1)
-        build_diag(0)
         for t in range(WIDEN_V[1]):
             lag_widen(1, t)
         loads_quant(1)
@@ -359,9 +358,10 @@ def tile_spike_covariance_readout_s13_kernel(
         empty(3)
         fill(6)
         fill(7)
-        loads_turn(3, 0)
+        loads_turn(2, 1)
         empty(4)
         fill(8)
+        loads_turn(3, 0)
         loads_turn(3, 1)
 
         def run(items):
@@ -376,7 +376,8 @@ def tile_spike_covariance_readout_s13_kernel(
             if pi == 1:
                 turned_out = [(loads_exit, (g, h)) for g in (2, 3) for h in range(2)]
                 rest = [(lag_widen, (1, t)) for t in range(WIDEN_V[1], 4)]
-                return turned_out[:2] + rest + turned_out[2:] + [(lag_interleave, (1, 0))], widen[:2]
+                turn = [(lag_interleave, (1, h)) for h in range(LAG_S[1])]
+                return turned_out[:1] + rest + turn[:1] + turned_out[1:] + turn[1:], widen[:2]
             rest = [(interleave, (2 * pi - 2, G_COLS[1 - pi % 2], 512, "scalar"))] if pi in REST_S else []
             if pi % 2 == 1:
                 turn = [(lag_interleave, (k - 1, 1))] if k <= 4 and LAG_S[k - 1] == 2 else []
@@ -393,7 +394,8 @@ def tile_spike_covariance_readout_s13_kernel(
                 interleave(n, G_COLS[0], 512, "vector")
             quant(n + 1)
             if pi == 1:
-                lag_interleave(1, 1)
+                for h in range(LAG_S[1], 2):
+                    lag_interleave(1, h)
                 loads_quant(3)
             if k < 4 and pi % 2 == 1:
                 lag_quant(k)
@@ -452,4 +454,4 @@ def tile_spike_covariance_readout_s13_kernel(
             out_pass(14, r, False, False)
         for r in range(4):
             out_pass(15, r, False, True)
-            out_exit(3, r, on_scalar=(r % 2 == 0))
+            out_exit(3, r, on_scalar=(r % 2 == 0), parts=2 if r == 0 else 1)

@@ -20,12 +20,13 @@ FLOPS = 2 * M * K * M + 2 * R * M * M
 P = 128
 PANELS = (0, 1, 2, 3)
 PERIODS = 8
-G_COLS = (352, 448)
+G_COLS = (384, 512)
 WIDEN_V = (3, 4, 0, 0)
 LAG_S = (0, 1, 1, 1)
 RING = 4
-G_LAST = 240
-AHEAD = 1
+G_LAST = 288
+AHEAD = (1, 1)
+LATE_SLOTS = 2
 REST_S = ()
 DIAG_V = (0, 0, 0, 0)
 
@@ -135,7 +136,7 @@ def tile_spike_covariance_readout_s13_kernel(
             src = lag_planes[k][:].rearrange("p t (m s) -> p m t s", s=4)[:, 64 * h : 64 * h + 64]
             dst = lag_grp[k][:].rearrange("p (s m) t -> p m t s", s=4)[:, 64 * h : 64 * h + 64]
             if h < LAG_S[k]:
-                nc.scalar.copy(out=dst, in_=src)
+                nc.scalar.copy(out=dst.rearrange("p m t s -> p s m t"), in_=src.rearrange("p m t s -> p s m t"))
             else:
                 nc.vector.tensor_copy(out=dst, in_=src)
 
@@ -269,9 +270,12 @@ def tile_spike_covariance_readout_s13_kernel(
                     op0=ALU.mult,
                     op1=ALU.add,
                 )
+            elif engine == "scalar":
+                nc.scalar.copy(out=dst.rearrange("p (c t) -> p c t", t=4), in_=src.rearrange("p t c -> p c t"))
             else:
-                copy = nc.vector.tensor_copy if engine == "vector" else nc.scalar.copy
-                copy(out=dst.rearrange("p (c i t) -> p c t i", i=4, t=4), in_=src.rearrange("p t (c i) -> p c t i", i=4))
+                nc.vector.tensor_copy(
+                    out=dst.rearrange("p (c i t) -> p c t i", i=4, t=4), in_=src.rearrange("p t (c i) -> p c t i", i=4)
+                )
 
         def quant(n, lo=0, hi=512):
             if lo == 0:
@@ -409,10 +413,13 @@ def tile_spike_covariance_readout_s13_kernel(
         def unit_pass(n, r):
             out_pass(n, r, n % 4 == 1, n % 4 == 2)
 
+        def ahead(pi):
+            return 4 if pi == 1 else AHEAD[pi % 2]
+
         def early_passes(pi):
-            n = 2 * pi - 4
-            return [(unit_pass, (n, r)) for r in range(AHEAD)] + [
-                (unit_pass, (m, r)) for r in range(AHEAD, 4) for m in (n + 1, n)
+            n, done = 2 * pi - 4, ahead(pi - 1)
+            return [(unit_pass, (n, r)) for r in range(done)] + [
+                (unit_pass, (m, r)) for r in range(done, 4) for m in (n + 1, n)
             ]
 
         for pi in range(1, PERIODS):
@@ -421,8 +428,9 @@ def tile_spike_covariance_readout_s13_kernel(
             mine = period_jobs[pi]
             last_vector = max([i for i, j in enumerate(mine) if jobs[j][0] != "planed"])
             passes = early_passes(pi) if pi >= 2 else []
-            passes = passes + [None] * (8 - AHEAD - len(passes)) + [(unit_pass, (2 * pi - 1, r)) for r in range(AHEAD)]
-            passes = passes[: 8 - AHEAD] + [None] * (len(mine) - 7) + passes[8 - AHEAD :]
+            late_passes = [(unit_pass, (2 * pi - 1, r)) for r in range(ahead(pi))]
+            passes = passes + [None] * (len(mine) + 1 - len(passes) - len(late_passes[:LATE_SLOTS]))
+            passes = passes + late_passes[:LATE_SLOTS]
             run(passes[:1])
             for i, j in enumerate(mine):
                 run(passes[i + 1 : i + 2])
@@ -432,10 +440,13 @@ def tile_spike_covariance_readout_s13_kernel(
                 if i == last_vector:
                     vector_shared(pi)
                     if pi == 1:
-                        for held in mine[:3]:
+                        for held in mine[:4]:
                             fill(held + RING)
-                if pi > 1 or i >= last_vector:
+                        run(late_passes)
+                        passes, late_passes = [], []
+                if pi > 1 or i > last_vector:
                     fill(j + RING)
+            run(late_passes[LATE_SLOTS:])
             run(late)
 
         interleave(14, 0, G_LAST, "gpsimd")

@@ -20,11 +20,11 @@ FLOPS = 2 * M * K * M + 2 * R * M * M
 P = 128
 PANELS = (0, 1, 2, 3)
 PERIODS = 8
-G_COLS = (384, 512)
+G_COLS = (352, 512)
 WIDEN_V = (3, 4, 0, 0)
 LAG_S = (0, 1, 1, 1)
 RING = 4
-G_LAST = 288
+G_LAST = 256
 AHEAD = (1, 1)
 LATE_SLOTS = 2
 REST_S = ()
@@ -136,7 +136,7 @@ def tile_spike_covariance_readout_s13_kernel(
             src = lag_planes[k][:].rearrange("p t (m s) -> p m t s", s=4)[:, 64 * h : 64 * h + 64]
             dst = lag_grp[k][:].rearrange("p (s m) t -> p m t s", s=4)[:, 64 * h : 64 * h + 64]
             if h < LAG_S[k]:
-                nc.scalar.copy(out=dst.rearrange("p m t s -> p s m t"), in_=src.rearrange("p m t s -> p s m t"))
+                nc.scalar.copy(out=dst, in_=src)
             else:
                 nc.vector.tensor_copy(out=dst, in_=src)
 
@@ -270,12 +270,9 @@ def tile_spike_covariance_readout_s13_kernel(
                     op0=ALU.mult,
                     op1=ALU.add,
                 )
-            elif engine == "scalar":
-                nc.scalar.copy(out=dst.rearrange("p (c t) -> p c t", t=4), in_=src.rearrange("p t c -> p c t"))
             else:
-                nc.vector.tensor_copy(
-                    out=dst.rearrange("p (c i t) -> p c t i", i=4, t=4), in_=src.rearrange("p t (c i) -> p c t i", i=4)
-                )
+                copy = nc.vector.tensor_copy if engine == "vector" else nc.scalar.copy
+                copy(out=dst.rearrange("p (c i t) -> p c t i", i=4, t=4), in_=src.rearrange("p t (c i) -> p c t i", i=4))
 
         def quant(n, lo=0, hi=512):
             if lo == 0:
@@ -453,16 +450,15 @@ def tile_spike_covariance_readout_s13_kernel(
         out_exit(2, 2)
         interleave(14, G_LAST, 512, "scalar")
         out_exit(2, 3)
-        last = period_jobs[PERIODS]
         run(early_passes(PERIODS))
-        for j in last[:3]:
+        for j in period_jobs[PERIODS]:
             empty(j)
         quant(14)
-        empty(last[3])
-        quant(15, 0, 256)
-        quant(15, 256, 512)
-        for r in range(4):
-            out_pass(14, r, False, False)
-        for r in range(4):
-            out_pass(15, r, False, True)
-            out_exit(3, r, on_scalar=(r % 2 == 0), parts=2 if r == 0 else 1)
+        quant(15)
+        for pair in ((0, 1), (2,), (3,)):
+            for r in pair:
+                out_pass(14, r, False, False)
+            for r in pair:
+                out_pass(15, r, False, True)
+                outer = r in (0, 3)
+                out_exit(3, r, on_scalar=outer, parts=2 if outer else 1)

@@ -42,13 +42,13 @@ def tile_spike_covariance_readout_s13_kernel(
         ctx.enter_context(tc.manual_schedule())
 
         gp_rows = keep.tile([P, 512], BF16, name="gp_rows")
-        nc.gpsimd.memset(gp_rows[:].bitcast(I32), 0)
-        idle = keep.tile([P, 512], F32, name="idle")
-        nc.vector.memset(idle[:].bitcast(I32), 0)
-
-        def warm_up(width):
-            bank = psum.tile([P, 512], F32, name="ring%d" % (RING - 1))
-            nc.tensor.matmul(out=bank[:, 0:width], lhsT=idle[:, 0:P], rhs=idle[:, 0:width], start=True, stop=True)
+        nc.vector.memset(gp_rows[:].bitcast(I32), 0)
+        def warm_up(width, bank_name):
+            bank = psum.tile([P, 512], F32, name=bank_name)
+            moving = ident[:].unsqueeze(1).to_broadcast([P, width // P, P])
+            nc.tensor.matmul(
+                out=bank[:, 0:width].rearrange("p (a c) -> p a c", c=P), lhsT=ident[:], rhs=moving, start=True, stop=True
+            )
 
         ident = keep.tile([P, P], F32, name="ident")
         make_identity(nc, ident[:])
@@ -318,8 +318,7 @@ def tile_spike_covariance_readout_s13_kernel(
             period_jobs.append(list(range(len(jobs), len(jobs) + len(mine))))
             jobs.extend(mine)
 
-        warm_up(512)
-        warm_up(128)
+        warm_up(512, "ring3")
         loads_turn(0, 0)
         loads_turn(0, 1)
         bank = side_bank()
@@ -338,7 +337,7 @@ def tile_spike_covariance_readout_s13_kernel(
         loads_quant(0, 0, 256)
         lag_quant(0)
         loads_quant(0, 256, 512)
-        warm_up(256)
+        warm_up(256, "ring3")
         loads_turn(1, 0)
         loads_turn(1, 1)
         for j in range(RING):
@@ -364,6 +363,7 @@ def tile_spike_covariance_readout_s13_kernel(
         fill(8)
         loads_turn(3, 0)
         loads_turn(3, 1)
+        warm_up(256, "out_bank1")
 
         def run(items):
             for item in items:

@@ -60,7 +60,7 @@ def tile_spike_covariance_readout_s13_kernel(
 
         def load_lag(k, parts):
             jb = PANELS[k]
-            lraw = keep.tile([P, 4, 512], U8, name="lraw%d" % k, align_bytes=64)
+            lraw = keep.tile([P, 4, 512], U8, name="lraw%d" % k, align_bytes=256)
             step = 4 // len(parts)
             for a in parts:
                 nc.sync.dma_start(out=lraw[:, a : a + step, :], in_=lag_view[:, a : a + step, 512 * jb : 512 * jb + 512])
@@ -70,7 +70,7 @@ def tile_spike_covariance_readout_s13_kernel(
             src = loads[512 * g : 512 * g + 512, :].rearrange("(m t) k -> m t k", t=4)
             step = 4 // parts
             for a in range(0, 4, step):
-                tile = keep.tile([P, step, 512], BF16, name="rows%d_%d" % (g, a), align_bytes=64)
+                tile = keep.tile([P, step, 512], BF16, name="rows%d_%d" % (g, a), align_bytes=256)
                 nc.sync.dma_start(out=tile[:], in_=src[:, a : a + step, :])
                 for t in range(step):
                     rows[g, a + t] = tile[:, t, :]
@@ -84,9 +84,9 @@ def tile_spike_covariance_readout_s13_kernel(
         load_rows(2, 1)
         load_rows(3, 1)
         load_lag(2, (0,))
-        w_sb = keep.tile([P, 4, 1024], U8, name="w_sb", align_bytes=64)
+        w_sb = keep.tile([P, 4, 1024], U8, name="w_sb", align_bytes=256)
         nc.sync.dma_start(out=w_sb[:], in_=w_words.rearrange("g p n -> p g n"))
-        ws_sb = keep.tile([P, 4, 512], U8, name="ws_sb", align_bytes=64)
+        ws_sb = keep.tile([P, 4, 512], U8, name="ws_sb", align_bytes=256)
         nc.vector.memset(ws_sb[:].rearrange("p g n -> p (g n)").bitcast(I32), 0)
         ws_view = w_scales.bitcast(I32).rearrange("g q n -> q g n")
         for quad in range(4):
@@ -122,7 +122,7 @@ def tile_spike_covariance_readout_s13_kernel(
 
         def lag_widen(k, t):
             if k not in lag_planes:
-                lag_planes[k] = work.tile([P, 4, 512], BF16, name="lag_planes", bufs=2, align_bytes=64)
+                lag_planes[k] = work.tile([P, 4, 512], BF16, name="lag_planes", bufs=2, align_bytes=256)
             src = lag_raw[k][:, t, :].bitcast(FP8)
             dst = lag_planes[k][:, t, :]
             if t < WIDEN_V[k]:
@@ -132,7 +132,7 @@ def tile_spike_covariance_readout_s13_kernel(
 
         def lag_interleave(k, h):
             if k not in lag_grp:
-                lag_grp[k] = work.tile([P, 512, 4], BF16, name="lag_grp", bufs=2, align_bytes=64)
+                lag_grp[k] = work.tile([P, 512, 4], BF16, name="lag_grp", bufs=2, align_bytes=256)
             src = lag_planes[k][:].rearrange("p t (m s) -> p m t s", s=4)[:, 64 * h : 64 * h + 64]
             dst = lag_grp[k][:].rearrange("p (s m) t -> p m t s", s=4)[:, 64 * h : 64 * h + 64]
             if h < LAG_S[k]:
@@ -141,8 +141,8 @@ def tile_spike_covariance_readout_s13_kernel(
                 nc.vector.tensor_copy(out=dst, in_=src)
 
         def lag_quant(k):
-            lag_codes[k] = work.tile([P, 512], U32, name="lag_codes", bufs=3, align_bytes=64)
-            lag_sc[k] = work.tile([P, 512], U8, name="lag_sc", bufs=3, align_bytes=64)
+            lag_codes[k] = work.tile([P, 512], U32, name="lag_codes", bufs=3, align_bytes=256)
+            lag_sc[k] = work.tile([P, 512], U8, name="lag_sc", bufs=3, align_bytes=256)
             nc.vector.quantize_mx(
                 out=lag_codes[k][:].bitcast(FP8X4),
                 scales=lag_sc[k][:],
@@ -160,9 +160,9 @@ def tile_spike_covariance_readout_s13_kernel(
 
         def loads_exit(g, h, on_scalar=True):
             if h == 0:
-                ld_grp[g] = work.tile([P, 2048], BF16, name="ld_grp", bufs=3, align_bytes=64)
-                ld_codes[g] = keep.tile([P, 512], U32, name="ld_codes%d" % g, align_bytes=64)
-                ld_sc[g] = keep.tile([P, 512], U8, name="ld_sc%d" % g, align_bytes=64)
+                ld_grp[g] = work.tile([P, 2048], BF16, name="ld_grp", bufs=3, align_bytes=256)
+                ld_codes[g] = keep.tile([P, 512], U32, name="ld_codes%d" % g, align_bytes=256)
+                ld_sc[g] = keep.tile([P, 512], U8, name="ld_sc%d" % g, align_bytes=256)
             src = turned[g, h][:].rearrange("p (t u m) -> p t m u", t=2, u=2)
             dst = ld_grp[g][:, 1024 * h : 1024 * h + 1024].bitcast(F32).rearrange("p (t m u) -> p t m u", t=2, u=2)
             if on_scalar:
@@ -221,7 +221,7 @@ def tile_spike_covariance_readout_s13_kernel(
 
         def planes_of(n):
             if n not in planes:
-                planes[n] = work.tile([P, 4, 512], BF16, name="planes", bufs=3, align_bytes=64)
+                planes[n] = work.tile([P, 4, 512], BF16, name="planes", bufs=3, align_bytes=256)
             return planes[n]
 
         def empty(j):
@@ -229,7 +229,7 @@ def tile_spike_covariance_readout_s13_kernel(
             g, bank = group(n), banks[j]
             if kind == "direct":
                 if x == 0:
-                    grouped[n] = work.tile([P, 2048], BF16, name="direct_grp", bufs=2, align_bytes=64)
+                    grouped[n] = work.tile([P, 2048], BF16, name="direct_grp", bufs=2, align_bytes=256)
                 nc.vector.tensor_tensor(
                     out=grouped[n][:, 512 * x : 512 * x + 512].rearrange("p (c t) -> p c t", t=4),
                     in0=bank[:].rearrange("p (t c) -> p c t", t=4),
@@ -259,7 +259,7 @@ def tile_spike_covariance_readout_s13_kernel(
             if hi <= lo:
                 return
             if n not in grouped:
-                grouped[n] = work.tile([P, 2048], BF16, name="planed_grp", bufs=1, align_bytes=64)
+                grouped[n] = work.tile([P, 2048], BF16, name="planed_grp", bufs=1, align_bytes=256)
             dst, src = grouped[n][:, 4 * lo : 4 * hi], planes[n][:, :, lo:hi]
             if engine == "gpsimd":
                 nc.gpsimd.tensor_scalar(
@@ -276,8 +276,8 @@ def tile_spike_covariance_readout_s13_kernel(
 
         def quant(n, lo=0, hi=512):
             if lo == 0:
-                codes[n] = work.tile([P, 512], U32, name="codes", bufs=4, align_bytes=64)
-                scales[n] = work.tile([P, 512], U8, name="scales", bufs=4, align_bytes=64)
+                codes[n] = work.tile([P, 512], U32, name="codes", bufs=4, align_bytes=256)
+                scales[n] = work.tile([P, 512], U8, name="scales", bufs=4, align_bytes=256)
             nc.vector.quantize_mx(
                 out=codes[n][:, lo:hi].bitcast(FP8X4), scales=scales[n][:, lo:hi], in_=grouped[n][:, 4 * lo : 4 * hi]
             )

@@ -18,17 +18,13 @@ M, K, R = 2048, 512, 512
 FLOPS = 2 * M * K * M + 2 * R * M * M
 
 P = 128
-PANELS = (0, 1, 2, 3)
-PERIODS = 8
-G_COLS = (352, 512)
-WIDEN_V = (3, 4, 0, 0)
-LAG_S = (0, 1, 1, 1)
+WIDTH = 512
+PANELS = M // WIDTH
+PERIODS = 2 * PANELS
 RING = 4
-G_LAST = 256
-AHEAD = (1, 1)
-LATE_SLOTS = 2
-REST_S = ()
-DIAG_V = (0, 0, 0, 0)
+ALIGN = 256
+GPSIMD_ODD = 352
+GPSIMD_LAST = 256
 
 
 def tile_spike_covariance_readout_s13_kernel(
@@ -41,52 +37,45 @@ def tile_spike_covariance_readout_s13_kernel(
         psum = ctx.enter_context(tc.psum_pool(name="psum", bufs=1))
         ctx.enter_context(tc.manual_schedule())
 
-        gp_rows = keep.tile([P, 512], BF16, name="gp_rows")
+        gp_rows = keep.tile([P, WIDTH], BF16, name="gp_rows")
         nc.vector.memset(gp_rows[:].bitcast(I32), 0)
-        def warm_up(width, bank_name):
-            bank = psum.tile([P, 512], F32, name=bank_name)
-            moving = ident[:].unsqueeze(1).to_broadcast([P, width // P, P])
-            nc.tensor.matmul(
-                out=bank[:, 0:width].rearrange("p (a c) -> p a c", c=P), lhsT=ident[:], rhs=moving, start=True, stop=True
-            )
-
         ident = keep.tile([P, P], F32, name="ident")
         make_identity(nc, ident[:])
-        lagsc = keep.tile([P, 4], F32, name="lagsc")
-        nc.scalar.dma_start(out=lagsc[:], in_=lag_scale.rearrange("(p t) o -> p (t o)", t=4))
+        lag_factor = keep.tile([P, 4], F32, name="lag_factor")
+        nc.scalar.dma_start(out=lag_factor[:], in_=lag_scale.rearrange("(p t) o -> p (t o)", t=4))
 
         lag_view = lag_bytes.rearrange("(p t) j -> p t j", t=4)
         lag_raw, rows = {}, {}
 
-        def load_lag(k, parts):
-            jb = PANELS[k]
-            lraw = keep.tile([P, 4, 512], U8, name="lraw%d" % k, align_bytes=256)
-            step = 4 // len(parts)
-            for a in parts:
-                nc.sync.dma_start(out=lraw[:, a : a + step, :], in_=lag_view[:, a : a + step, 512 * jb : 512 * jb + 512])
-            lag_raw[k] = lraw
+        def load_lag(panel, first_slots=(0,)):
+            raw = keep.tile([P, 4, WIDTH], U8, name="lag_raw%d" % panel, align_bytes=ALIGN)
+            step = 4 // len(first_slots)
+            columns = slice(WIDTH * panel, WIDTH * (panel + 1))
+            for t in first_slots:
+                nc.sync.dma_start(out=raw[:, t : t + step, :], in_=lag_view[:, t : t + step, columns])
+            lag_raw[panel] = raw
 
-        def load_rows(g, parts):
-            src = loads[512 * g : 512 * g + 512, :].rearrange("(m t) k -> m t k", t=4)
+        def load_rows(g, parts=1):
+            src = loads[WIDTH * g : WIDTH * (g + 1), :].rearrange("(m t) k -> m t k", t=4)
             step = 4 // parts
-            for a in range(0, 4, step):
-                tile = keep.tile([P, step, 512], BF16, name="rows%d_%d" % (g, a), align_bytes=256)
-                nc.sync.dma_start(out=tile[:], in_=src[:, a : a + step, :])
+            for first in range(0, 4, step):
+                tile = keep.tile([P, step, K], BF16, name="rows%d_%d" % (g, first), align_bytes=ALIGN)
+                nc.sync.dma_start(out=tile[:], in_=src[:, first : first + step, :])
                 for t in range(step):
-                    rows[g, a + t] = tile[:, t, :]
+                    rows[g, first + t] = tile[:, t, :]
 
-        load_lag(0, (0, 3, 1, 2))
-        load_rows(0, 2)
+        first_order = (0, 3, 1, 2)
+        load_lag(0, first_order)
+        load_rows(0, parts=2)
         nc.sync.dma_start(out=gp_rows[0:4, :], in_=gain.rearrange("(g x) -> g x", g=4))
         nc.sync.dma_start(out=gp_rows[4:8, :], in_=private.rearrange("(g x) -> g x", g=4))
-        load_rows(1, 1)
-        load_lag(1, (0,))
-        load_rows(2, 1)
-        load_rows(3, 1)
-        load_lag(2, (0,))
-        w_sb = keep.tile([P, 4, 1024], U8, name="w_sb", align_bytes=256)
+        load_rows(1)
+        load_lag(1)
+        load_rows(2)
+        load_rows(3)
+        w_sb = keep.tile([P, 4, 2 * R], U8, name="w_sb", align_bytes=ALIGN)
         nc.sync.dma_start(out=w_sb[:], in_=w_words.rearrange("g p n -> p g n"))
-        ws_sb = keep.tile([P, 4, 512], U8, name="ws_sb", align_bytes=256)
+        ws_sb = keep.tile([P, 4, R], U8, name="ws_sb", align_bytes=ALIGN)
         nc.vector.memset(ws_sb[:].rearrange("p g n -> p (g n)").bitcast(I32), 0)
         ws_view = w_scales.bitcast(I32).rearrange("g q n -> q g n")
         for quad in range(4):
@@ -94,89 +83,90 @@ def tile_spike_covariance_readout_s13_kernel(
                 out=ws_sb[32 * quad : 32 * quad + 4, :, :].bitcast(I32),
                 in_=ws_view[4 * quad : 4 * quad + 4, :, :],
             )
-        load_lag(3, (0,))
+        load_lag(2)
+        load_lag(3)
 
         gp_f = keep.tile([P, 2, 16], F32, name="gp_f")
         gain_f, priv_f = gp_f[:, 0, :], gp_f[:, 1, :]
         diag = keep.tile([P, 16, P], BF16, name="diag")
 
-        turns = [0]
-
-        def side_bank():
-            bank = psum.tile([P, 512], F32, name="out_bank%d" % (turns[0] % 4))
-            turns[0] = turns[0] + 1
-            return bank
-
-        def build_diag(k):
-            for t in range(4):
-                i = 4 * PANELS[k] + t
-                if DIAG_V[k]:
-                    nc.vector.tensor_scalar(
-                        out=diag[:, i, :], in0=ident[:], scalar1=priv_f[:, i : i + 1], scalar2=None, op0=ALU.mult
-                    )
-                else:
-                    nc.scalar.activation(out=diag[:, i, :], in_=ident[:], func=ACT.Copy, scale=priv_f[:, i : i + 1])
-
-        lag_planes, lag_grp, lag_codes, lag_sc = {}, {}, {}, {}
-        ld_grp, ld_codes, ld_sc, turned = {}, {}, {}, {}
-
-        def lag_widen(k, t):
-            if k not in lag_planes:
-                lag_planes[k] = work.tile([P, 4, 512], BF16, name="lag_planes", bufs=2, align_bytes=256)
-            src = lag_raw[k][:, t, :].bitcast(FP8)
-            dst = lag_planes[k][:, t, :]
-            if t < WIDEN_V[k]:
-                nc.vector.tensor_scalar(out=dst, in0=src, scalar1=lagsc[:, t : t + 1], scalar2=None, op0=ALU.mult)
-            else:
-                nc.scalar.activation(out=dst, in_=src, func=ACT.Copy, scale=lagsc[:, t : t + 1])
-
-        def lag_interleave(k, h):
-            if k not in lag_grp:
-                lag_grp[k] = work.tile([P, 512, 4], BF16, name="lag_grp", bufs=2, align_bytes=256)
-            src = lag_planes[k][:].rearrange("p t (m s) -> p m t s", s=4)[:, 64 * h : 64 * h + 64]
-            dst = lag_grp[k][:].rearrange("p (s m) t -> p m t s", s=4)[:, 64 * h : 64 * h + 64]
-            if h < LAG_S[k]:
-                nc.scalar.copy(out=dst, in_=src)
-            else:
-                nc.vector.tensor_copy(out=dst, in_=src)
-
-        def lag_quant(k):
-            lag_codes[k] = work.tile([P, 512], U32, name="lag_codes", bufs=3, align_bytes=256)
-            lag_sc[k] = work.tile([P, 512], U8, name="lag_sc", bufs=3, align_bytes=256)
-            nc.vector.quantize_mx(
-                out=lag_codes[k][:].bitcast(FP8X4),
-                scales=lag_sc[k][:],
-                in_=lag_grp[k][:].rearrange("p c t -> p (c t)"),
+        def warm_up(width, bank_name):
+            bank = psum.tile([P, WIDTH], F32, name=bank_name)
+            moving = ident[:].unsqueeze(1).to_broadcast([P, width // P, P])
+            nc.tensor.matmul(
+                out=bank[:, 0:width].rearrange("p (a c) -> p a c", c=P), lhsT=ident[:], rhs=moving, start=True, stop=True
             )
 
-        def loads_turn(g, h):
+        side_banks = []
+
+        def side_bank():
+            bank = psum.tile([P, WIDTH], F32, name="out_bank%d" % (len(side_banks) % 4))
+            side_banks.append(bank)
+            return bank
+
+        def build_diag(g):
+            for i in range(4 * g, 4 * g + 4):
+                nc.scalar.activation(out=diag[:, i, :], in_=ident[:], func=ACT.Copy, scale=priv_f[:, i : i + 1])
+
+        lag_planes, lag_grouped, lag_codes, lag_scales = {}, {}, {}, {}
+        ld_grouped, ld_codes, ld_scales, turned = {}, {}, {}, {}
+
+        def lag_widen(panel, t, on_vector=False):
+            if panel not in lag_planes:
+                lag_planes[panel] = work.tile([P, 4, WIDTH], BF16, name="lag_planes", bufs=2, align_bytes=ALIGN)
+            src, dst, factor = lag_raw[panel][:, t, :].bitcast(FP8), lag_planes[panel][:, t, :], lag_factor[:, t : t + 1]
+            if on_vector:
+                nc.vector.tensor_scalar(out=dst, in0=src, scalar1=factor, scalar2=None, op0=ALU.mult)
+            else:
+                nc.scalar.activation(out=dst, in_=src, func=ACT.Copy, scale=factor)
+
+        def lag_interleave(panel, half, on_vector):
+            if panel not in lag_grouped:
+                lag_grouped[panel] = work.tile([P, WIDTH, 4], BF16, name="lag_grouped", bufs=2, align_bytes=ALIGN)
+            part = slice(64 * half, 64 * half + 64)
+            src = lag_planes[panel][:].rearrange("p t (m s) -> p m t s", s=4)[:, part]
+            dst = lag_grouped[panel][:].rearrange("p (s m) t -> p m t s", s=4)[:, part]
+            copy = nc.vector.tensor_copy if on_vector else nc.scalar.copy
+            copy(out=dst, in_=src)
+
+        def lag_quant(panel):
+            lag_codes[panel] = work.tile([P, WIDTH], U32, name="lag_codes", bufs=3, align_bytes=ALIGN)
+            lag_scales[panel] = work.tile([P, WIDTH], U8, name="lag_scales", bufs=3, align_bytes=ALIGN)
+            nc.vector.quantize_mx(
+                out=lag_codes[panel][:].bitcast(FP8X4),
+                scales=lag_scales[panel][:],
+                in_=lag_grouped[panel][:].rearrange("p c t -> p (c t)"),
+            )
+
+        def loads_turn(g, half):
             bank = side_bank()
             view = bank[:].rearrange("p (t u m) -> p t u m", t=2, u=2)
-            for tt in range(2):
-                words = rows[g, 2 * h + tt].bitcast(F32)
+            for t in range(2):
+                words = rows[g, 2 * half + t].bitcast(F32)
                 for u in range(2):
-                    nc.tensor.transpose(view[:, tt, u, :], words[:, u:256:2], ident[:])
-            turned[g, h] = bank
+                    nc.tensor.transpose(view[:, t, u, :], words[:, u:256:2], ident[:])
+            turned[g, half] = bank
 
-        def loads_exit(g, h, on_scalar=True):
-            if h == 0:
-                ld_grp[g] = work.tile([P, 2048], BF16, name="ld_grp", bufs=3, align_bytes=256)
-                ld_codes[g] = keep.tile([P, 512], U32, name="ld_codes%d" % g, align_bytes=256)
-                ld_sc[g] = keep.tile([P, 512], U8, name="ld_sc%d" % g, align_bytes=256)
-            src = turned[g, h][:].rearrange("p (t u m) -> p t m u", t=2, u=2)
-            dst = ld_grp[g][:, 1024 * h : 1024 * h + 1024].bitcast(F32).rearrange("p (t m u) -> p t m u", t=2, u=2)
-            if on_scalar:
-                nc.scalar.copy(out=dst, in_=src)
-            else:
-                nc.vector.tensor_copy(out=dst, in_=src)
+        def loads_exit(g, half):
+            if half == 0:
+                ld_grouped[g] = work.tile([P, 4 * WIDTH], BF16, name="ld_grouped", bufs=3, align_bytes=ALIGN)
+                ld_codes[g] = keep.tile([P, WIDTH], U32, name="ld_codes%d" % g, align_bytes=ALIGN)
+                ld_scales[g] = keep.tile([P, WIDTH], U8, name="ld_scales%d" % g, align_bytes=ALIGN)
+            dst = ld_grouped[g][:, 1024 * half : 1024 * half + 1024].bitcast(F32)
+            nc.scalar.copy(
+                out=dst.rearrange("p (t m u) -> p t m u", t=2, u=2),
+                in_=turned[g, half][:].rearrange("p (t u m) -> p t m u", t=2, u=2),
+            )
 
-        def loads_quant(g, lo=0, hi=512):
+        def loads_quant(g, lo=0, hi=WIDTH):
             nc.vector.quantize_mx(
-                out=ld_codes[g][:, lo:hi].bitcast(FP8X4), scales=ld_sc[g][:, lo:hi], in_=ld_grp[g][:, 4 * lo : 4 * hi]
+                out=ld_codes[g][:, lo:hi].bitcast(FP8X4),
+                scales=ld_scales[g][:, lo:hi],
+                in_=ld_grouped[g][:, 4 * lo : 4 * hi],
             )
 
         def group(n):
-            return (PANELS[n // 4] + n) % 4
+            return (n // 4 + n) % 4
 
         def has_diag(n):
             return n % 4 == 0
@@ -184,44 +174,39 @@ def tile_spike_covariance_readout_s13_kernel(
         banks, planes, grouped, codes, scales, out_banks = {}, {}, {}, {}, {}, {}
 
         def s_pass(bank, at, n, t, lo, hi):
-            g, k = group(n), n // 4
+            g, panel = group(n), n // 4
             nc.tensor.matmul_mx(
                 out=bank[:, at : at + hi - lo],
-                lhsT=ld_codes[g][:, 128 * t : 128 * t + 128].bitcast(FP8X4),
-                lhsT_scale=ld_sc[g][:, 128 * t : 128 * t + 128],
-                rhs=lag_codes[k][:, lo:hi].bitcast(FP8X4),
-                rhs_scale=lag_sc[k][:, lo:hi],
+                lhsT=ld_codes[g][:, P * t : P * (t + 1)].bitcast(FP8X4),
+                lhsT_scale=ld_scales[g][:, P * t : P * (t + 1)],
+                rhs=lag_codes[panel][:, lo:hi].bitcast(FP8X4),
+                rhs_scale=lag_scales[panel][:, lo:hi],
                 start=True,
                 stop=True,
             )
-
-        def off_diag(t):
-            return [(a, b) for a, b in ((0, 128 * t), (128 * t + 128, 512)) if b > a]
 
         def fill(j):
             if j >= len(jobs):
                 return
             kind, n, x = jobs[j]
-            bank = psum.tile([P, 512], F32, name="ring%d" % (j % RING))
+            bank = psum.tile([P, WIDTH], F32, name="ring%d" % (j % RING))
             banks[j] = bank
             if kind == "direct":
                 for t in range(4):
-                    s_pass(bank, 128 * t, n, t, 128 * x, 128 * x + 128)
-            elif kind == "diag":
+                    s_pass(bank, P * t, n, t, P * x, P * (x + 1))
+            elif kind == "windows":
                 for t in range(4):
-                    s_pass(bank, 128 * t, n, t, 128 * t, 128 * t + 128)
+                    s_pass(bank, P * t, n, t, P * t, P * (t + 1))
             elif not has_diag(n):
-                s_pass(bank, 0, n, x, 0, 512)
+                s_pass(bank, 0, n, x, 0, WIDTH)
             else:
-                for lo, hi in ((0, 256), (256, 512)):
-                    if lo <= 128 * x < hi:
-                        lo = lo + 128 - (128 * x - lo)
-                        hi = lo + 128
+                for half in range(2):
+                    lo, hi = (P * (x ^ 1), P * (x ^ 1) + P) if half == x // 2 else (256 * half, 256 * half + 256)
                     s_pass(bank, lo, n, x, lo, hi)
 
         def planes_of(n):
             if n not in planes:
-                planes[n] = work.tile([P, 4, 512], BF16, name="planes", bufs=3, align_bytes=256)
+                planes[n] = work.tile([P, 4, WIDTH], BF16, name="planes", bufs=3, align_bytes=ALIGN)
             return planes[n]
 
         def empty(j):
@@ -229,114 +214,114 @@ def tile_spike_covariance_readout_s13_kernel(
             g, bank = group(n), banks[j]
             if kind == "direct":
                 if x == 0:
-                    grouped[n] = work.tile([P, 2048], BF16, name="direct_grp", bufs=2, align_bytes=256)
+                    grouped[n] = work.tile([P, 4 * WIDTH], BF16, name="direct_grouped", bufs=2, align_bytes=ALIGN)
                 nc.vector.tensor_tensor(
-                    out=grouped[n][:, 512 * x : 512 * x + 512].rearrange("p (c t) -> p c t", t=4),
+                    out=grouped[n][:, WIDTH * x : WIDTH * (x + 1)].rearrange("p (c t) -> p c t", t=4),
                     in0=bank[:].rearrange("p (t c) -> p c t", t=4),
-                    in1=gain_f[:, 4 * g : 4 * g + 4].unsqueeze(1).to_broadcast([P, 128, 4]),
+                    in1=gain_f[:, 4 * g : 4 * g + 4].unsqueeze(1).to_broadcast([P, P, 4]),
                     op=ALU.mult,
                 )
-            elif kind == "diag":
+            elif kind == "windows":
                 for t in range(4):
                     nc.vector.scalar_tensor_tensor(
-                        out=planes_of(n)[:, t, 128 * t : 128 * t + 128],
-                        in0=bank[:, 128 * t : 128 * t + 128],
+                        out=planes_of(n)[:, t, P * t : P * (t + 1)],
+                        in0=bank[:, P * t : P * (t + 1)],
                         scalar=gain_f[:, 4 * g + t : 4 * g + t + 1],
                         in1=diag[:, 4 * g + t, :],
                         op0=ALU.mult,
                         op1=ALU.add,
                     )
             else:
-                for lo, hi in off_diag(x) if has_diag(n) else [(0, 512)]:
-                    nc.scalar.activation(
-                        out=planes_of(n)[:, x, lo:hi],
-                        in_=bank[:, lo:hi],
-                        func=ACT.Copy,
-                        scale=gain_f[:, 4 * g + x : 4 * g + x + 1],
-                    )
+                spans = [(0, P * x), (P * (x + 1), WIDTH)] if has_diag(n) else [(0, WIDTH)]
+                for lo, hi in spans:
+                    if hi > lo:
+                        nc.scalar.activation(
+                            out=planes_of(n)[:, x, lo:hi],
+                            in_=bank[:, lo:hi],
+                            func=ACT.Copy,
+                            scale=gain_f[:, 4 * g + x : 4 * g + x + 1],
+                        )
 
-        def interleave(n, lo, hi, engine):
-            if hi <= lo:
-                return
-            if n not in grouped:
-                grouped[n] = work.tile([P, 2048], BF16, name="planed_grp", bufs=1, align_bytes=256)
-            dst, src = grouped[n][:, 4 * lo : 4 * hi], planes[n][:, :, lo:hi]
-            if engine == "gpsimd":
-                nc.gpsimd.tensor_scalar(
-                    out=dst.rearrange("p (c t) -> p c t", t=4),
-                    in0=src.rearrange("p t c -> p c t"),
-                    scalar1=1.0,
-                    scalar2=0.0,
-                    op0=ALU.mult,
-                    op1=ALU.add,
-                )
-            else:
-                copy = nc.vector.tensor_copy if engine == "vector" else nc.scalar.copy
-                copy(out=dst.rearrange("p (c i t) -> p c t i", i=4, t=4), in_=src.rearrange("p t (c i) -> p c t i", i=4))
-
-        def quant(n, lo=0, hi=512):
-            if lo == 0:
-                codes[n] = work.tile([P, 512], U32, name="codes", bufs=4, align_bytes=256)
-                scales[n] = work.tile([P, 512], U8, name="scales", bufs=4, align_bytes=256)
-            nc.vector.quantize_mx(
-                out=codes[n][:, lo:hi].bitcast(FP8X4), scales=scales[n][:, lo:hi], in_=grouped[n][:, 4 * lo : 4 * hi]
+        def interleave_gpsimd(n, hi):
+            grouped[n] = work.tile([P, 4 * WIDTH], BF16, name="planed_grouped", bufs=1, align_bytes=ALIGN)
+            nc.gpsimd.tensor_scalar(
+                out=grouped[n][:, 0 : 4 * hi].rearrange("p (c t) -> p c t", t=4),
+                in0=planes[n][:, :, 0:hi].rearrange("p t c -> p c t"),
+                scalar1=1.0,
+                scalar2=0.0,
+                op0=ALU.mult,
+                op1=ALU.add,
             )
 
-        def out_pass(n, r, first, last):
-            k, g = n // 4, group(n)
-            if first:
-                out_banks[k, r] = psum.tile([P, 512], F32, name="out_bank%d" % r)
+        def interleave_rest(n, lo, copy):
+            copy(
+                out=grouped[n][:, 4 * lo :].rearrange("p (c i t) -> p c t i", i=4, t=4),
+                in_=planes[n][:, :, lo:].rearrange("p t (c i) -> p c t i", i=4),
+            )
+
+        def quant(n):
+            codes[n] = work.tile([P, WIDTH], U32, name="codes", bufs=4, align_bytes=ALIGN)
+            scales[n] = work.tile([P, WIDTH], U8, name="scales", bufs=4, align_bytes=ALIGN)
+            nc.vector.quantize_mx(out=codes[n][:].bitcast(FP8X4), scales=scales[n][:], in_=grouped[n][:])
+
+        added = {}
+
+        def out_pass(n, r):
+            panel, g = n // 4, group(n)
+            count = added.get((panel, r), 0)
+            added[panel, r] = count + 1
+            if count == 0:
+                out_banks[panel, r] = psum.tile([P, WIDTH], F32, name="out_bank%d" % r)
             nc.tensor.matmul_mx(
-                out=out_banks[k, r][:],
-                lhsT=w_sb[:, g, 256 * r : 256 * r + 256].bitcast(FP4X4),
-                lhsT_scale=ws_sb[:, g, 128 * r : 128 * r + 128],
+                out=out_banks[panel, r][:],
+                lhsT=w_sb[:, g, 2 * P * r : 2 * P * (r + 1)].bitcast(FP4X4),
+                lhsT_scale=ws_sb[:, g, P * r : P * (r + 1)],
                 rhs=codes[n][:].bitcast(FP8X4),
                 rhs_scale=scales[n][:],
-                start=first,
-                stop=last,
+                start=(count == 0),
+                stop=(count == 3),
             )
 
-        def out_exit(k, r, on_scalar=True, parts=1):
-            ot = work.tile([P, 512], F32, name="ot", bufs=6)
-            dst = ot[:].rearrange("p (m s) -> p m s", s=4)
-            src = out_banks[k, r][:].rearrange("p (s m) -> p m s", s=4)
-            copy = nc.scalar.copy if on_scalar else nc.vector.tensor_copy
-            step = 128 // parts
-            for m in range(0, 128, step):
+        def out_exit(panel, r, copy=nc.scalar.copy, parts=1):
+            staged = work.tile([P, WIDTH], F32, name="staged", bufs=6)
+            dst = staged[:].rearrange("p (m s) -> p m s", s=4)
+            src = out_banks[panel, r][:].rearrange("p (s m) -> p m s", s=4)
+            step = P // parts
+            for m in range(0, P, step):
                 copy(out=dst[:, m : m + step], in_=src[:, m : m + step])
-                j = 512 * PANELS[k] + 4 * m
-                nc.sync.dma_start(out=out[128 * r : 128 * r + 128, j : j + 4 * step], in_=ot[:, 4 * m : 4 * (m + step)])
+                j = WIDTH * panel + 4 * m
+                nc.sync.dma_start(out=out[P * r : P * (r + 1), j : j + 4 * step], in_=staged[:, 4 * m : 4 * (m + step)])
 
-        jobs = [("planed", 0, 0), ("planed", 0, 1), ("diag", 0, 0), ("planed", 0, 2), ("planed", 0, 3)]
-        period_jobs = [list(range(5))]
-        for pi in range(1, PERIODS + 1):
-            direct = [("direct", 2 * pi - 1, q) for q in range(4)]
-            planed = [("planed", 2 * pi, t) for t in range(4)] if pi < PERIODS else []
-            windows = [("diag", 2 * pi, 0)] if pi < PERIODS and has_diag(2 * pi) else []
-            ahead = int(pi > 1)
-            mine = direct[:3] + planed[:ahead] + direct[3:] + windows + planed[ahead:]
+        jobs = [("plane", 0, 0), ("plane", 0, 1), ("plane", 0, 2), ("windows", 0, 0), ("plane", 0, 3)]
+        period_jobs = [list(range(len(jobs)))]
+        for period in range(1, PERIODS + 1):
+            direct = [("direct", 2 * period - 1, q) for q in range(4)]
+            plane = [("plane", 2 * period, t) for t in range(4)] if period < PERIODS else []
+            windows = [("windows", 2 * period, 0)] if period < PERIODS and has_diag(2 * period) else []
+            leading = 1 if period > 1 else 0
+            mine = direct[:3] + plane[:leading] + direct[3:] + windows + plane[leading:]
             period_jobs.append(list(range(len(jobs), len(jobs) + len(mine))))
             jobs.extend(mine)
 
         warm_up(512, "ring3")
         loads_turn(0, 0)
         loads_turn(0, 1)
-        bank = side_bank()
+        gp_bank = side_bank()
         for u in range(2):
-            nc.tensor.transpose(bank[:, 128 * u : 128 * u + 128], gp_rows[:].bitcast(F32)[:, u:256:2], ident[:])
-        for t in (0, 3, 1, 2):
-            lag_widen(0, t)
+            nc.tensor.transpose(gp_bank[:, P * u : P * (u + 1)], gp_rows[:].bitcast(F32)[:, u:256:2], ident[:])
+        for t in first_order:
+            lag_widen(0, t, on_vector=(t < 3))
         loads_exit(0, 0)
-        lag_interleave(0, 0)
-        lag_interleave(0, 1)
+        lag_interleave(0, 0, on_vector=True)
+        lag_interleave(0, 1, on_vector=True)
         loads_exit(0, 1)
         nc.scalar.copy(
             out=gp_f[:].rearrange("p a (g u e) -> p (a g) u e", u=2, e=2),
-            in_=bank[:, 0:256].bitcast(BF16).rearrange("p (u r e) -> p r u e", u=2, e=2)[:, 0:8],
+            in_=gp_bank[:, 0:256].bitcast(BF16).rearrange("p (u r e) -> p r u e", u=2, e=2)[:, 0:8],
         )
         loads_quant(0, 0, 256)
         lag_quant(0)
-        loads_quant(0, 256, 512)
+        loads_quant(0, 256, WIDTH)
         warm_up(256, "ring3")
         loads_turn(1, 0)
         loads_turn(1, 1)
@@ -347,118 +332,110 @@ def tile_spike_covariance_readout_s13_kernel(
         build_diag(0)
         loads_exit(1, 0)
         loads_exit(1, 1)
-        for t in range(WIDEN_V[1]):
-            lag_widen(1, t)
+        for t in range(4):
+            lag_widen(1, t, on_vector=True)
         loads_quant(1)
-        empty(0)
-        fill(4)
-        empty(1)
-        fill(5)
-        empty(2)
-        empty(3)
-        fill(6)
-        fill(7)
+        for j in period_jobs[0]:
+            empty(j)
+            fill(j + RING)
         loads_turn(2, 1)
-        empty(4)
-        fill(8)
         loads_turn(3, 0)
         loads_turn(3, 1)
         warm_up(256, "out_bank1")
 
-        def run(items):
-            for item in items:
-                if item:
-                    item[0](*item[1])
+        def run(calls):
+            for call in calls:
+                if call:
+                    call[0](*call[1:])
 
-        def scalar_extras(pi):
-            k = (pi + 3) // 2
-            widen = [(lag_widen, (k, t)) for t in range(4)] if k < 4 else []
-            exits = [(out_exit, ((pi - 3) // 2, r)) for r in range(4)] if pi >= 3 else []
-            if pi == 1:
-                turned_out = [(loads_exit, (g, h)) for g in (2, 3) for h in range(2)]
-                rest = [(lag_widen, (1, t)) for t in range(WIDEN_V[1], 4)]
-                turn = [(lag_interleave, (1, h)) for h in range(LAG_S[1])]
-                return turned_out[:1] + rest + turn[:1] + turned_out[1:] + turn[1:], widen[:2]
-            rest = [(interleave, (2 * pi - 2, G_COLS[1 - pi % 2], 512, "scalar"))] if pi in REST_S else []
-            if pi % 2 == 1:
-                turn = [(lag_interleave, (k - 1, 1))] if k <= 4 and LAG_S[k - 1] == 2 else []
-                return turn + rest + widen[:1] + exits[:2], exits[2:3] * (pi < PERIODS - 1) + widen[1:2]
-            turn = [(lag_interleave, (k, 0))] if k < 4 and LAG_S[k] else []
-            return [(build_diag, (pi // 2,))] + rest + exits[3:] + widen[2:], turn
+        def scalar_extras(period):
+            panel = (period + 3) // 2
+            widen = [(lag_widen, panel, t) for t in range(4)] if panel < PANELS else []
+            if period == 1:
+                exits = [(loads_exit, g, half) for g in (2, 3) for half in range(2)]
+                return exits[:1] + [(lag_interleave, 1, 0, False)] + exits[1:], widen[:2]
+            exits = [(out_exit, (period - 3) // 2, r) for r in range(4)] if period >= 3 else []
+            if period % 2 == 1:
+                return widen[:1] + exits[:2], exits[2:3] + widen[1:2]
+            half = [(lag_interleave, panel, 0, False)] if panel < PANELS else []
+            return [(build_diag, period // 2)] + exits[3:] + widen[2:], half
 
-        def vector_shared(pi):
-            k = pi // 2 + 1
-            n = 2 * pi - 2
-            if pi == 1:
+        def vector_port_work(period):
+            panel = period // 2 + 1
+            planed_unit, direct_unit = 2 * period - 2, 2 * period - 1
+            if period % 2 == 1:
+                interleave_rest(planed_unit, GPSIMD_ODD, nc.vector.tensor_copy)
+            if period == 1:
                 loads_quant(2)
-            if pi not in REST_S and pi % 2 == 1:
-                interleave(n, G_COLS[0], 512, "vector")
-            quant(n + 1)
-            if pi == 1:
-                for h in range(LAG_S[1], 2):
-                    lag_interleave(1, h)
+            quant(direct_unit)
+            if period == 1:
+                lag_interleave(panel, 1, on_vector=True)
                 loads_quant(3)
-            if k < 4 and pi % 2 == 1:
-                lag_quant(k)
-            if pi % 2 == 0:
-                if pi not in REST_S:
-                    interleave(n, G_COLS[1], 512, "vector")
-                for h in range(LAG_S[k] if k < 4 else 2, 2):
-                    lag_interleave(k, h)
-            quant(n)
+            if panel < PANELS and period % 2 == 1:
+                lag_quant(panel)
+            if panel < PANELS and period % 2 == 0:
+                lag_interleave(panel, 1, on_vector=True)
+            quant(planed_unit)
 
-        def unit_pass(n, r):
-            out_pass(n, r, n % 4 == 1, n % 4 == 2)
+        def passes_ahead(period):
+            return 4 if period == 1 else 1
 
-        def ahead(pi):
-            return 4 if pi == 1 else AHEAD[pi % 2]
-
-        def early_passes(pi):
-            n, done = 2 * pi - 4, ahead(pi - 1)
-            return [(unit_pass, (n, r)) for r in range(done)] + [
-                (unit_pass, (m, r)) for r in range(done, 4) for m in (n + 1, n)
+        def passes_due(period):
+            planed_unit, direct_unit, done = 2 * period - 4, 2 * period - 3, passes_ahead(period - 1)
+            return [(out_pass, planed_unit, r) for r in range(done)] + [
+                (out_pass, n, r) for r in range(done, 4) for n in (direct_unit, planed_unit)
             ]
 
-        for pi in range(1, PERIODS):
-            interleave(2 * pi - 2, 0, G_COLS[int(has_diag(2 * pi))], "gpsimd")
-            early, late = scalar_extras(pi)
-            mine = period_jobs[pi]
-            last_vector = max([i for i, j in enumerate(mine) if jobs[j][0] != "planed"])
-            passes = early_passes(pi) if pi >= 2 else []
-            late_passes = [(unit_pass, (2 * pi - 1, r)) for r in range(ahead(pi))]
-            passes = passes + [None] * (len(mine) + 1 - len(passes) - len(late_passes[:LATE_SLOTS]))
-            passes = passes + late_passes[:LATE_SLOTS]
+        interleave_gpsimd(0, GPSIMD_ODD)
+        early, late = scalar_extras(1)
+        direct_jobs, plane_jobs = period_jobs[1][:4], period_jobs[1][4:]
+        for j in direct_jobs:
+            empty(j)
+        run(early)
+        vector_port_work(1)
+        for j in direct_jobs:
+            fill(j + RING)
+        out_pass(1, 0)
+        out_pass(1, 1)
+        for i, j in enumerate(plane_jobs):
+            if i >= 2:
+                out_pass(1, i)
+            empty(j)
+            fill(j + RING)
+        run(late)
+
+        for period in range(2, PERIODS):
+            interleave_gpsimd(2 * period - 2, GPSIMD_ODD if period % 2 else WIDTH)
+            early, late = scalar_extras(period)
+            mine = period_jobs[period]
+            last_on_vector = max([i for i, j in enumerate(mine) if jobs[j][0] != "plane"])
+            due = passes_due(period)
+            passes = due + [None] * (len(mine) - len(due)) + [(out_pass, 2 * period - 1, 0)]
             run(passes[:1])
             for i, j in enumerate(mine):
                 run(passes[i + 1 : i + 2])
                 empty(j)
                 if i == 3:
                     run(early)
-                if i == last_vector:
-                    vector_shared(pi)
-                    if pi == 1:
-                        for held in mine[:4]:
-                            fill(held + RING)
-                        run(late_passes)
-                        passes, late_passes = [], []
-                if pi > 1 or i > last_vector:
-                    fill(j + RING)
-            run(late_passes[LATE_SLOTS:])
+                if i == last_on_vector:
+                    vector_port_work(period)
+                fill(j + RING)
             run(late)
 
-        interleave(14, 0, G_LAST, "gpsimd")
-        out_exit(2, 2)
-        interleave(14, G_LAST, 512, "scalar")
-        out_exit(2, 3)
-        run(early_passes(PERIODS))
+        interleave_gpsimd(14, GPSIMD_LAST)
+        interleave_rest(14, GPSIMD_LAST, nc.scalar.copy)
+        out_exit(PANELS - 2, 3)
+        run(passes_due(PERIODS))
         for j in period_jobs[PERIODS]:
             empty(j)
         quant(14)
         quant(15)
-        for pair in ((0, 1), (2,), (3,)):
-            for r in pair:
-                out_pass(14, r, False, False)
-            for r in pair:
-                out_pass(15, r, False, True)
-                outer = r in (0, 3)
-                out_exit(3, r, on_scalar=outer, parts=2 if outer else 1)
+        for blocks in ((0, 1), (2,), (3,)):
+            for r in blocks:
+                out_pass(14, r)
+            for r in blocks:
+                out_pass(15, r)
+                if r in (0, 3):
+                    out_exit(PANELS - 1, r, parts=2)
+                else:
+                    out_exit(PANELS - 1, r, copy=nc.vector.tensor_copy)

@@ -25,6 +25,10 @@ RING = 4
 ALIGN = 256
 GPSIMD_ODD = 352
 GPSIMD_LAST = 256
+HEAD_V = 96
+GPSIMD_EVEN = 448
+GPSIMD_FIRST = 352
+AHEAD1 = 1
 
 
 def tile_spike_covariance_readout_s13_kernel(
@@ -73,6 +77,7 @@ def tile_spike_covariance_readout_s13_kernel(
         load_lag(1)
         load_rows(2)
         load_rows(3)
+        load_lag(2)
         w_sb = keep.tile([P, 4, 2 * R], U8, name="w_sb", align_bytes=ALIGN)
         nc.sync.dma_start(out=w_sb[:], in_=w_words.rearrange("g p n -> p g n"))
         ws_sb = keep.tile([P, 4, R], U8, name="ws_sb", align_bytes=ALIGN)
@@ -83,7 +88,6 @@ def tile_spike_covariance_readout_s13_kernel(
                 out=ws_sb[32 * quad : 32 * quad + 4, :, :].bitcast(I32),
                 in_=ws_view[4 * quad : 4 * quad + 4, :, :],
             )
-        load_lag(2)
         load_lag(3)
 
         gp_f = keep.tile([P, 2, 16], F32, name="gp_f")
@@ -96,13 +100,6 @@ def tile_spike_covariance_readout_s13_kernel(
             nc.tensor.matmul(
                 out=bank[:, 0:width].rearrange("p (a c) -> p a c", c=P), lhsT=ident[:], rhs=moving, start=True, stop=True
             )
-
-        side_banks = []
-
-        def side_bank():
-            bank = psum.tile([P, WIDTH], F32, name="out_bank%d" % (len(side_banks) % 4))
-            side_banks.append(bank)
-            return bank
 
         def build_diag(g):
             for i in range(4 * g, 4 * g + 4):
@@ -120,10 +117,13 @@ def tile_spike_covariance_readout_s13_kernel(
             else:
                 nc.scalar.activation(out=dst, in_=src, func=ACT.Copy, scale=factor)
 
-        def lag_interleave(panel, half, on_vector):
+        def lag_interleave(panel, lo, hi, on_vector):
             if panel not in lag_grouped:
-                lag_grouped[panel] = work.tile([P, WIDTH, 4], BF16, name="lag_grouped", bufs=2, align_bytes=ALIGN)
-            part = slice(64 * half, 64 * half + 64)
+                if panel == 1:
+                    lag_grouped[panel] = work.tile([P, WIDTH, 4], BF16, name="planed_grouped", bufs=1, align_bytes=ALIGN)
+                else:
+                    lag_grouped[panel] = work.tile([P, WIDTH, 4], BF16, name="lag_grouped", bufs=2, align_bytes=ALIGN)
+            part = slice(lo, hi)
             src = lag_planes[panel][:].rearrange("p t (m s) -> p m t s", s=4)[:, part]
             dst = lag_grouped[panel][:].rearrange("p (s m) t -> p m t s", s=4)[:, part]
             copy = nc.vector.tensor_copy if on_vector else nc.scalar.copy
@@ -138,8 +138,8 @@ def tile_spike_covariance_readout_s13_kernel(
                 in_=lag_grouped[panel][:].rearrange("p c t -> p (c t)"),
             )
 
-        def loads_turn(g, half):
-            bank = side_bank()
+        def loads_turn(g, half, bank_name):
+            bank = psum.tile([P, WIDTH], F32, name=bank_name)
             view = bank[:].rearrange("p (t u m) -> p t u m", t=2, u=2)
             for t in range(2):
                 words = rows[g, 2 * half + t].bitcast(F32)
@@ -185,11 +185,11 @@ def tile_spike_covariance_readout_s13_kernel(
                 stop=True,
             )
 
-        def fill(j):
+        def fill(j, bank_name=None):
             if j >= len(jobs):
                 return
             kind, n, x = jobs[j]
-            bank = psum.tile([P, WIDTH], F32, name="ring%d" % (j % RING))
+            bank = psum.tile([P, WIDTH], F32, name=bank_name or "ring%d" % (j % RING))
             banks[j] = bank
             if kind == "direct":
                 for t in range(4):
@@ -292,7 +292,7 @@ def tile_spike_covariance_readout_s13_kernel(
                 j = WIDTH * panel + 4 * m
                 nc.sync.dma_start(out=out[P * r : P * (r + 1), j : j + 4 * step], in_=staged[:, 4 * m : 4 * (m + step)])
 
-        jobs = [("plane", 0, 0), ("plane", 0, 1), ("plane", 0, 2), ("windows", 0, 0), ("plane", 0, 3)]
+        jobs = [("plane", 0, 0), ("windows", 0, 0), ("plane", 0, 1), ("plane", 0, 2), ("plane", 0, 3)]
         period_jobs = [list(range(len(jobs)))]
         for period in range(1, PERIODS + 1):
             direct = [("direct", 2 * period - 1, q) for q in range(4)]
@@ -303,82 +303,74 @@ def tile_spike_covariance_readout_s13_kernel(
             period_jobs.append(list(range(len(jobs), len(jobs) + len(mine))))
             jobs.extend(mine)
 
-        warm_up(512, "ring3")
-        loads_turn(0, 0)
-        loads_turn(0, 1)
-        gp_bank = side_bank()
-        for u in range(2):
-            nc.tensor.transpose(gp_bank[:, P * u : P * (u + 1)], gp_rows[:].bitcast(F32)[:, u:256:2], ident[:])
-        for t in first_order:
-            lag_widen(0, t, on_vector=(t < 3))
-        loads_exit(0, 0)
-        lag_interleave(0, 0, on_vector=True)
-        lag_interleave(0, 1, on_vector=True)
-        loads_exit(0, 1)
-        nc.scalar.copy(
-            out=gp_f[:].rearrange("p a (g u e) -> p (a g) u e", u=2, e=2),
-            in_=gp_bank[:, 0:256].bitcast(BF16).rearrange("p (u r e) -> p r u e", u=2, e=2)[:, 0:8],
-        )
-        loads_quant(0, 0, 256)
-        lag_quant(0)
-        loads_quant(0, 256, WIDTH)
-        warm_up(256, "ring3")
-        loads_turn(1, 0)
-        loads_turn(1, 1)
-        for j in range(RING):
-            fill(j)
-        loads_turn(2, 0)
-
-        build_diag(0)
-        loads_exit(1, 0)
-        loads_exit(1, 1)
-        for t in range(4):
-            lag_widen(1, t, on_vector=True)
-        loads_quant(1)
-        for j in period_jobs[0]:
-            empty(j)
-            fill(j + RING)
-        loads_turn(2, 1)
-        loads_turn(3, 0)
-        loads_turn(3, 1)
-        warm_up(256, "out_bank1")
-
         def run(calls):
             for call in calls:
                 if call:
                     call[0](*call[1:])
 
-        def scalar_extras(period):
-            panel = (period + 3) // 2
-            widen = [(lag_widen, panel, t) for t in range(4)] if panel < PANELS else []
-            if period == 1:
-                exits = [(loads_exit, g, half) for g in (2, 3) for half in range(2)]
-                return exits[:1] + [(lag_interleave, 1, 0, False)] + exits[1:], widen[:2]
-            exits = [(out_exit, (period - 3) // 2, r) for r in range(4)] if period >= 3 else []
-            if period % 2 == 1:
-                return widen[:1] + exits[:2], exits[2:3] + widen[1:2]
-            half = [(lag_interleave, panel, 0, False)] if panel < PANELS else []
-            return [(build_diag, period // 2)] + exits[3:] + widen[2:], half
-
-        def vector_port_work(period):
-            panel = period // 2 + 1
-            planed_unit, direct_unit = 2 * period - 2, 2 * period - 1
-            if period % 2 == 1:
-                interleave_rest(planed_unit, GPSIMD_ODD, nc.vector.tensor_copy)
-            if period == 1:
-                loads_quant(2)
-            quant(direct_unit)
-            if period == 1:
-                lag_interleave(panel, 1, on_vector=True)
-                loads_quant(3)
-            if panel < PANELS and period % 2 == 1:
-                lag_quant(panel)
-            if panel < PANELS and period % 2 == 0:
-                lag_interleave(panel, 1, on_vector=True)
-            quant(planed_unit)
+        warm_up(512, "ring3")
+        loads_turn(0, 0, "out_bank0")
+        loads_turn(0, 1, "out_bank1")
+        gp_bank = psum.tile([P, WIDTH], F32, name="out_bank2")
+        for u in range(2):
+            nc.tensor.transpose(gp_bank[:, P * u : P * (u + 1)], gp_rows[:].bitcast(F32)[:, u:256:2], ident[:])
+        warm_up(256, "ring3")
+        loads_turn(1, 0, "out_bank3")
+        loads_turn(1, 1, "ring3")
+        for t in first_order:
+            lag_widen(0, t, on_vector=(t < 3))
+        lag_interleave(0, 0, HEAD_V, True)
+        if HEAD_V < P:
+            lag_interleave(0, HEAD_V, P, False)
+        loads_exit(0, 0)
+        loads_exit(0, 1)
+        nc.scalar.copy(
+            out=gp_f[:].rearrange("p a (g u e) -> p (a g) u e", u=2, e=2),
+            in_=gp_bank[:, 0:256].bitcast(BF16).rearrange("p (u r e) -> p r u e", u=2, e=2)[:, 0:8],
+        )
+        lag_quant(0)
+        loads_quant(0, 0, 256)
+        loads_quant(0, 256, WIDTH)
+        fill(0, "out_bank0")
+        fill(2, "ring0")
+        fill(1, "out_bank1")
+        fill(3, "ring1")
+        fill(4, "ring2")
+        build_diag(0)
+        loads_exit(1, 0)
+        loads_exit(1, 1)
+        loads_turn(2, 0, "out_bank2")
+        loads_turn(2, 1, "out_bank3")
+        for t in range(4):
+            lag_widen(1, t, on_vector=True)
+        empty(0)
+        empty(2)
+        lag_interleave(1, 0, 64, True)
+        loads_quant(1)
+        empty(1)
+        loads_turn(3, 0, "ring3")
+        loads_turn(3, 1, "out_bank0")
+        loads_exit(2, 0)
+        loads_exit(2, 1)
+        lag_interleave(1, 64, P, True)
+        loads_quant(2)
+        lag_quant(1)
+        fill(5, "out_bank1")
+        fill(6, "out_bank2")
+        fill(7, "out_bank3")
+        loads_exit(3, 0)
+        loads_exit(3, 1)
+        fill(8, "out_bank0")
+        loads_quant(3)
+        fill(11)
+        fill(12)
+        for j in (3, 4):
+            empty(j)
+        for j in (9, 10):
+            fill(j)
 
         def passes_ahead(period):
-            return 4 if period == 1 else 1
+            return AHEAD1 if period == 1 else 1
 
         def passes_due(period):
             planed_unit, direct_unit, done = 2 * period - 4, 2 * period - 3, passes_ahead(period - 1)
@@ -386,26 +378,48 @@ def tile_spike_covariance_readout_s13_kernel(
                 (out_pass, n, r) for r in range(done, 4) for n in (direct_unit, planed_unit)
             ]
 
-        interleave_gpsimd(0, GPSIMD_ODD)
-        early, late = scalar_extras(1)
-        direct_jobs, plane_jobs = period_jobs[1][:4], period_jobs[1][4:]
-        for j in direct_jobs:
+        def scalar_extras(period):
+            W = lambda panel, ts: [(lag_widen, panel, t) for t in ts]
+            O = lambda panel, rs: [(out_exit, panel, r) for r in rs]
+            return {
+                1: ([], W(2, (0, 1, 2, 3))),
+                2: ([(build_diag, 1), (lag_interleave, 2, 0, 64, False)], W(3, (0,))),
+                3: (O(0, (0, 1)), O(0, (2,)) + W(3, (1,))),
+                4: ([(build_diag, 2)] + O(0, (3,)) + W(3, (2, 3)), [(lag_interleave, 3, 0, 64, False)]),
+                5: (O(1, (0, 1)), O(1, (2,))),
+                6: ([(build_diag, 3)] + O(1, (3,)), []),
+                7: (O(2, (0, 1)), O(2, (2,))),
+            }[period]
+
+        def share(period):
+            return GPSIMD_FIRST if period == 1 else GPSIMD_ODD if period % 2 else GPSIMD_EVEN
+
+        def vector_port_work(period):
+            panel = period // 2 + 1
+            planed_unit, direct_unit = 2 * period - 2, 2 * period - 1
+            if share(period) < WIDTH:
+                interleave_rest(planed_unit, share(period), nc.vector.tensor_copy)
+            quant(direct_unit)
+            if period in (3, 5):
+                lag_quant(panel)
+            if period in (2, 4):
+                lag_interleave(panel, 64, P, True)
+            quant(planed_unit)
+
+        interleave_gpsimd(0, share(1))
+        for j in (5, 6, 7, 8):
             empty(j)
-        run(early)
+        for j in (11, 12, 9, 10):
+            empty(j)
+        for j in (15, 16, 13, 14):
+            fill(j)
         vector_port_work(1)
-        for j in direct_jobs:
-            fill(j + RING)
-        out_pass(1, 0)
-        out_pass(1, 1)
-        for i, j in enumerate(plane_jobs):
-            if i >= 2:
-                out_pass(1, i)
-            empty(j)
-            fill(j + RING)
-        run(late)
+        for r in range(AHEAD1):
+            out_pass(1, r)
+        run(scalar_extras(1)[1])
 
         for period in range(2, PERIODS):
-            interleave_gpsimd(2 * period - 2, GPSIMD_ODD if period % 2 else WIDTH)
+            interleave_gpsimd(2 * period - 2, share(period))
             early, late = scalar_extras(period)
             mine = period_jobs[period]
             last_on_vector = max([i for i, j in enumerate(mine) if jobs[j][0] != "plane"])

@@ -28,7 +28,8 @@ GPSIMD_LAST = 256
 HEAD_V = 96
 GPSIMD_EVEN = 448
 GPSIMD_FIRST = 352
-AHEAD1 = 1
+AHEAD1 = 2
+SPLIT = 64
 
 
 def tile_spike_covariance_readout_s13_kernel(
@@ -105,6 +106,15 @@ def tile_spike_covariance_readout_s13_kernel(
             for i in range(4 * g, 4 * g + 4):
                 nc.scalar.activation(out=diag[:, i, :], in_=ident[:], func=ACT.Copy, scale=priv_f[:, i : i + 1])
 
+        holder = {}
+        for_gpsimd, for_vector, spare = "grouped0", "grouped1", "grouped2"
+        for period in range(1, PERIODS + 1):
+            holder[2 * period - 2], holder[2 * period - 1] = for_gpsimd, for_vector
+            if 2 <= period <= 5:
+                for_vector, spare = spare, for_vector
+            else:
+                for_gpsimd, for_vector, spare = for_vector, spare, for_gpsimd
+
         lag_planes, lag_grouped, lag_codes, lag_scales = {}, {}, {}, {}
         ld_grouped, ld_codes, ld_scales, turned = {}, {}, {}, {}
 
@@ -120,7 +130,7 @@ def tile_spike_covariance_readout_s13_kernel(
         def lag_interleave(panel, lo, hi, on_vector):
             if panel not in lag_grouped:
                 if panel == 1:
-                    lag_grouped[panel] = work.tile([P, WIDTH, 4], BF16, name="planed_grouped", bufs=1, align_bytes=ALIGN)
+                    lag_grouped[panel] = work.tile([P, WIDTH, 4], BF16, name=holder[0], bufs=1, align_bytes=ALIGN)
                 else:
                     lag_grouped[panel] = work.tile([P, WIDTH, 4], BF16, name="lag_grouped", bufs=2, align_bytes=ALIGN)
             part = slice(lo, hi)
@@ -214,7 +224,7 @@ def tile_spike_covariance_readout_s13_kernel(
             g, bank = group(n), banks[j]
             if kind == "direct":
                 if x == 0:
-                    grouped[n] = work.tile([P, 4 * WIDTH], BF16, name="direct_grouped", bufs=2, align_bytes=ALIGN)
+                    grouped[n] = work.tile([P, 4 * WIDTH], BF16, name=holder[n], bufs=1, align_bytes=ALIGN)
                 nc.vector.tensor_tensor(
                     out=grouped[n][:, WIDTH * x : WIDTH * (x + 1)].rearrange("p (c t) -> p c t", t=4),
                     in0=bank[:].rearrange("p (t c) -> p c t", t=4),
@@ -243,7 +253,7 @@ def tile_spike_covariance_readout_s13_kernel(
                         )
 
         def interleave_gpsimd(n, hi):
-            grouped[n] = work.tile([P, 4 * WIDTH], BF16, name="planed_grouped", bufs=1, align_bytes=ALIGN)
+            grouped[n] = work.tile([P, 4 * WIDTH], BF16, name=holder[n], bufs=1, align_bytes=ALIGN)
             nc.gpsimd.tensor_scalar(
                 out=grouped[n][:, 0 : 4 * hi].rearrange("p (c t) -> p c t", t=4),
                 in0=planes[n][:, :, 0:hi].rearrange("p t c -> p c t"),
@@ -383,9 +393,9 @@ def tile_spike_covariance_readout_s13_kernel(
             O = lambda panel, rs: [(out_exit, panel, r) for r in rs]
             return {
                 1: ([], W(2, (0, 1, 2, 3))),
-                2: ([(build_diag, 1), (lag_interleave, 2, 0, 64, False)], W(3, (0,))),
-                3: (O(0, (0, 1)), O(0, (2,)) + W(3, (1,))),
-                4: ([(build_diag, 2)] + O(0, (3,)) + W(3, (2, 3)), [(lag_interleave, 3, 0, 64, False)]),
+                2: ([(build_diag, 1)] + W(3, (0,)), [(lag_interleave, 2, 0, SPLIT, False)]),
+                3: (O(0, (0, 1)), O(0, (2,)) + W(3, (1, 2))),
+                4: ([(build_diag, 2)] + O(0, (3,)) + W(3, (3,)), [(lag_interleave, 3, 0, SPLIT, False)]),
                 5: (O(1, (0, 1)), O(1, (2,))),
                 6: ([(build_diag, 3)] + O(1, (3,)), []),
                 7: (O(2, (0, 1)), O(2, (2,))),
@@ -400,11 +410,11 @@ def tile_spike_covariance_readout_s13_kernel(
             if share(period) < WIDTH:
                 interleave_rest(planed_unit, share(period), nc.vector.tensor_copy)
             quant(direct_unit)
+            quant(planed_unit)
             if period in (3, 5):
                 lag_quant(panel)
             if period in (2, 4):
-                lag_interleave(panel, 64, P, True)
-            quant(planed_unit)
+                lag_interleave(panel, SPLIT, P, True)
 
         interleave_gpsimd(0, share(1))
         for j in (5, 6, 7, 8):

@@ -23,13 +23,18 @@ PANELS = M // WIDTH
 PERIODS = 2 * PANELS
 RING = 4
 ALIGN = 256
-GPSIMD_ODD = 352
-GPSIMD_LAST = 256
+GPSIMD_ODD = 384
+GPSIMD_LAST = 288
 HEAD_V = 96
-GPSIMD_EVEN = 448
-GPSIMD_FIRST = 352
+GPSIMD_EVEN = 512
+GPSIMD_FIRST = 384
 AHEAD1 = 2
-SPLIT = 64
+SPLIT = 72
+WARM2 = 256
+E7 = 2
+TAILORD = 0
+O3FIRST = 0
+A7 = 1
 
 
 def tile_spike_covariance_readout_s13_kernel(
@@ -324,7 +329,7 @@ def tile_spike_covariance_readout_s13_kernel(
         gp_bank = psum.tile([P, WIDTH], F32, name="out_bank2")
         for u in range(2):
             nc.tensor.transpose(gp_bank[:, P * u : P * (u + 1)], gp_rows[:].bitcast(F32)[:, u:256:2], ident[:])
-        warm_up(256, "ring3")
+        warm_up(WARM2, "ring3")
         loads_turn(1, 0, "out_bank3")
         loads_turn(1, 1, "ring3")
         for t in first_order:
@@ -355,14 +360,13 @@ def tile_spike_covariance_readout_s13_kernel(
             lag_widen(1, t, on_vector=True)
         empty(0)
         empty(2)
-        lag_interleave(1, 0, 64, True)
-        loads_quant(1)
         empty(1)
+        loads_quant(1)
         loads_turn(3, 0, "ring3")
         loads_turn(3, 1, "out_bank0")
         loads_exit(2, 0)
         loads_exit(2, 1)
-        lag_interleave(1, 64, P, True)
+        lag_interleave(1, 0, P, True)
         loads_quant(2)
         lag_quant(1)
         fill(5, "out_bank1")
@@ -380,7 +384,7 @@ def tile_spike_covariance_readout_s13_kernel(
             fill(j)
 
         def passes_ahead(period):
-            return AHEAD1 if period == 1 else 1
+            return AHEAD1 if period == 1 else A7 if period == 7 else 1
 
         def passes_due(period):
             planed_unit, direct_unit, done = 2 * period - 4, 2 * period - 3, passes_ahead(period - 1)
@@ -398,7 +402,7 @@ def tile_spike_covariance_readout_s13_kernel(
                 4: ([(build_diag, 2)] + O(0, (3,)) + W(3, (3,)), [(lag_interleave, 3, 0, SPLIT, False)]),
                 5: (O(1, (0, 1)), O(1, (2,))),
                 6: ([(build_diag, 3)] + O(1, (3,)), []),
-                7: (O(2, (0, 1)), O(2, (2,))),
+                7: (O(2, range(E7)), O(2, range(E7, 3))),
             }[period]
 
         def share(period):
@@ -434,7 +438,7 @@ def tile_spike_covariance_readout_s13_kernel(
             mine = period_jobs[period]
             last_on_vector = max([i for i, j in enumerate(mine) if jobs[j][0] != "plane"])
             due = passes_due(period)
-            passes = due + [None] * (len(mine) - len(due)) + [(out_pass, 2 * period - 1, 0)]
+            passes = due + [None] * (len(mine) - len(due)) + [(out_pass, 2 * period - 1, 0)] * passes_ahead(period)
             run(passes[:1])
             for i, j in enumerate(mine):
                 run(passes[i + 1 : i + 2])
@@ -447,14 +451,17 @@ def tile_spike_covariance_readout_s13_kernel(
             run(late)
 
         interleave_gpsimd(14, GPSIMD_LAST)
+        if O3FIRST:
+            out_exit(PANELS - 2, 3)
         interleave_rest(14, GPSIMD_LAST, nc.scalar.copy)
-        out_exit(PANELS - 2, 3)
+        if not O3FIRST:
+            out_exit(PANELS - 2, 3)
         run(passes_due(PERIODS))
         for j in period_jobs[PERIODS]:
             empty(j)
         quant(14)
         quant(15)
-        for blocks in ((0, 1), (2,), (3,)):
+        for blocks in (((0, 1), (2,), (3,)), ((0,), (1,), (2,), (3,)), ((0, 1, 2), (3,)))[TAILORD]:
             for r in blocks:
                 out_pass(14, r)
             for r in blocks:

@@ -24,17 +24,33 @@ PERIODS = 2 * PANELS
 RING = 4
 ALIGN = 256
 GPSIMD_ODD = 384
-GPSIMD_LAST = 288
+GPSIMD_LAST = 384
 HEAD_V = 96
 GPSIMD_EVEN = 512
 GPSIMD_FIRST = 384
 AHEAD1 = 2
 SPLIT = 72
+SPLIT1 = 16
+SPLIT3 = 72
+W2EARLY = 2
+I2EARLY = 72
+I3EARLY = 72
+W3EARLY = 2
+W3S = 3
+IVLATE = ()
+REST0S = 1
+AHEAD1A = 1
+HIDE = (1, 2, 3, 4, 5)
 WARM2 = 256
 E7 = 2
 TAILORD = 0
 O3FIRST = 0
-A7 = 1
+A6 = 1
+SKIP7 = 2
+OAT = (7,8)
+PRE = 3
+PRE14 = 2
+O2LATE = 0
 
 
 def tile_spike_covariance_readout_s13_kernel(
@@ -115,7 +131,7 @@ def tile_spike_covariance_readout_s13_kernel(
         for_gpsimd, for_vector, spare = "grouped0", "grouped1", "grouped2"
         for period in range(1, PERIODS + 1):
             holder[2 * period - 2], holder[2 * period - 1] = for_gpsimd, for_vector
-            if 2 <= period <= 5:
+            if period in HIDE:
                 for_vector, spare = spare, for_vector
             else:
                 for_gpsimd, for_vector, spare = for_vector, spare, for_gpsimd
@@ -134,10 +150,7 @@ def tile_spike_covariance_readout_s13_kernel(
 
         def lag_interleave(panel, lo, hi, on_vector):
             if panel not in lag_grouped:
-                if panel == 1:
-                    lag_grouped[panel] = work.tile([P, WIDTH, 4], BF16, name=holder[0], bufs=1, align_bytes=ALIGN)
-                else:
-                    lag_grouped[panel] = work.tile([P, WIDTH, 4], BF16, name="lag_grouped", bufs=2, align_bytes=ALIGN)
+                lag_grouped[panel] = work.tile([P, WIDTH, 4], BF16, name="lag_grouped", bufs=2, align_bytes=ALIGN)
             part = slice(lo, hi)
             src = lag_planes[panel][:].rearrange("p t (m s) -> p m t s", s=4)[:, part]
             dst = lag_grouped[panel][:].rearrange("p (s m) t -> p m t s", s=4)[:, part]
@@ -164,7 +177,10 @@ def tile_spike_covariance_readout_s13_kernel(
 
         def loads_exit(g, half):
             if half == 0:
-                ld_grouped[g] = work.tile([P, 4 * WIDTH], BF16, name="ld_grouped", bufs=3, align_bytes=ALIGN)
+                if g == 2:
+                    ld_grouped[g] = work.tile([P, 4 * WIDTH], BF16, name=holder[0], bufs=1, align_bytes=ALIGN)
+                else:
+                    ld_grouped[g] = work.tile([P, 4 * WIDTH], BF16, name="ld_grouped", bufs=3, align_bytes=ALIGN)
                 ld_codes[g] = keep.tile([P, WIDTH], U32, name="ld_codes%d" % g, align_bytes=ALIGN)
                 ld_scales[g] = keep.tile([P, WIDTH], U8, name="ld_scales%d" % g, align_bytes=ALIGN)
             dst = ld_grouped[g][:, 1024 * half : 1024 * half + 1024].bitcast(F32)
@@ -360,31 +376,31 @@ def tile_spike_covariance_readout_s13_kernel(
             lag_widen(1, t, on_vector=True)
         empty(0)
         empty(2)
-        empty(1)
-        loads_quant(1)
         loads_turn(3, 0, "ring3")
-        loads_turn(3, 1, "out_bank0")
+        loads_turn(3, 1, "ring0")
+        loads_quant(1)
+        empty(1)
+        if SPLIT1:
+            lag_interleave(1, 0, SPLIT1, False)
+        lag_interleave(1, SPLIT1, P, True)
+        fill(5, "out_bank0")
+        fill(6, "out_bank1")
         loads_exit(2, 0)
         loads_exit(2, 1)
-        lag_interleave(1, 0, P, True)
+        fill(7, "out_bank2")
+        fill(8, "out_bank3")
         loads_quant(2)
-        lag_quant(1)
-        fill(5, "out_bank1")
-        fill(6, "out_bank2")
-        fill(7, "out_bank3")
+        empty(3)
+        empty(4)
+        fill(9)
+        fill(10)
         loads_exit(3, 0)
         loads_exit(3, 1)
-        fill(8, "out_bank0")
-        loads_quant(3)
         fill(11)
         fill(12)
-        for j in (3, 4):
-            empty(j)
-        for j in (9, 10):
-            fill(j)
 
         def passes_ahead(period):
-            return AHEAD1 if period == 1 else A7 if period == 7 else 1
+            return AHEAD1 if period == 1 else A6 if period == 6 else 1
 
         def passes_due(period):
             planed_unit, direct_unit, done = 2 * period - 4, 2 * period - 3, passes_ahead(period - 1)
@@ -395,12 +411,13 @@ def tile_spike_covariance_readout_s13_kernel(
         def scalar_extras(period):
             W = lambda panel, ts: [(lag_widen, panel, t) for t in ts]
             O = lambda panel, rs: [(out_exit, panel, r) for r in rs]
+            I = lambda panel, lo, hi: [(lag_interleave, panel, lo, hi, False)] * (hi > lo)
             return {
-                1: ([], W(2, (0, 1, 2, 3))),
-                2: ([(build_diag, 1)] + W(3, (0,)), [(lag_interleave, 2, 0, SPLIT, False)]),
-                3: (O(0, (0, 1)), O(0, (2,)) + W(3, (1, 2))),
-                4: ([(build_diag, 2)] + O(0, (3,)) + W(3, (3,)), [(lag_interleave, 3, 0, SPLIT, False)]),
-                5: (O(1, (0, 1)), O(1, (2,))),
+                1: ([], W(2, range(W2EARLY))),
+                2: ([(build_diag, 1)] + W(2, range(W2EARLY, 4)), I(2, 0, I2EARLY)),
+                3: (O(0, (0,)) + I(2, I2EARLY, SPLIT) + O(0, (1,)), O(0, (2,)) + W(3, range(W3EARLY))),
+                4: ([(build_diag, 2)] + O(0, (3,)) + W(3, range(W3EARLY, W3S)), I(3, 0, I3EARLY)),
+                5: (O(1, (0,)) + I(3, I3EARLY, SPLIT3) + O(1, (1,)), O(1, (2,))),
                 6: ([(build_diag, 3)] + O(1, (3,)), []),
                 7: (O(2, range(E7)), O(2, range(E7, 3))),
             }[period]
@@ -413,23 +430,38 @@ def tile_spike_covariance_readout_s13_kernel(
             planed_unit, direct_unit = 2 * period - 2, 2 * period - 1
             if share(period) < WIDTH:
                 interleave_rest(planed_unit, share(period), nc.vector.tensor_copy)
+            if period == 4:
+                for t in range(W3S, 4):
+                    lag_widen(3, t, True)
             quant(direct_unit)
+            if period in IVLATE:
+                lag_interleave(panel, SPLIT if period == 3 else SPLIT3, P, True)
             quant(planed_unit)
             if period in (3, 5):
                 lag_quant(panel)
-            if period in (2, 4):
-                lag_interleave(panel, SPLIT, P, True)
+            if period in (2, 4) and period + 1 not in IVLATE:
+                lag_interleave(panel, SPLIT if period == 2 else SPLIT3, P, True)
 
         interleave_gpsimd(0, share(1))
         for j in (5, 6, 7, 8):
             empty(j)
-        for j in (11, 12, 9, 10):
-            empty(j)
-        for j in (15, 16, 13, 14):
-            fill(j)
-        vector_port_work(1)
-        for r in range(AHEAD1):
+        interleave_rest(0, share(1), nc.scalar.copy if REST0S else nc.vector.tensor_copy)
+        loads_quant(3)
+        quant(1)
+        lag_quant(1)
+        quant(0)
+        empty(9)
+        fill(13)
+        empty(10)
+        fill(14)
+        empty(11)
+        for r in range(AHEAD1A):
             out_pass(1, r)
+        fill(15)
+        empty(12)
+        for r in range(AHEAD1A, AHEAD1):
+            out_pass(1, r)
+        fill(16)
         run(scalar_extras(1)[1])
 
         for period in range(2, PERIODS):
@@ -439,34 +471,52 @@ def tile_spike_covariance_readout_s13_kernel(
             last_on_vector = max([i for i, j in enumerate(mine) if jobs[j][0] != "plane"])
             due = passes_due(period)
             passes = due + [None] * (len(mine) - len(due)) + [(out_pass, 2 * period - 1, 0)] * passes_ahead(period)
+            if period == 7:
+                passes = [None] * SKIP7 + due
+                early, late = [], []
             run(passes[:1])
             for i, j in enumerate(mine):
                 run(passes[i + 1 : i + 2])
                 empty(j)
                 if i == 3:
                     run(early)
+                if period == 7 and i == OAT[0]:
+                    out_exit(2, 0)
+                if period == 7 and i == OAT[1]:
+                    out_exit(2, 1)
                 if i == last_on_vector:
                     vector_port_work(period)
                 fill(j + RING)
             run(late)
+        run(passes[len(mine) + 1 :])
 
         interleave_gpsimd(14, GPSIMD_LAST)
-        if O3FIRST:
-            out_exit(PANELS - 2, 3)
+        for r in range(2):
+            if OAT[r] > 7:
+                out_exit(2, r)
+        if not O2LATE:
+            out_exit(2, 2)
         interleave_rest(14, GPSIMD_LAST, nc.scalar.copy)
-        if not O3FIRST:
-            out_exit(PANELS - 2, 3)
-        run(passes_due(PERIODS))
+        if O2LATE:
+            out_exit(2, 2)
+        out_exit(2, 3)
+        for r in range(PRE):
+            out_pass(13, r)
+            out_pass(12, r)
         for j in period_jobs[PERIODS]:
             empty(j)
         quant(14)
         quant(15)
-        for blocks in (((0, 1), (2,), (3,)), ((0,), (1,), (2,), (3,)), ((0, 1, 2), (3,)))[TAILORD]:
-            for r in blocks:
+        for r in range(PRE14):
+            out_pass(14, r)
+        for r in range(4):
+            if r >= PRE:
+                out_pass(13, r)
+                out_pass(12, r)
+            if r >= PRE14:
                 out_pass(14, r)
-            for r in blocks:
-                out_pass(15, r)
-                if r in (0, 3):
-                    out_exit(PANELS - 1, r, parts=2)
-                else:
-                    out_exit(PANELS - 1, r, copy=nc.vector.tensor_copy)
+            out_pass(15, r)
+            if r in (0, 3):
+                out_exit(PANELS - 1, r, parts=2)
+            else:
+                out_exit(PANELS - 1, r, copy=nc.vector.tensor_copy)

@@ -23,11 +23,11 @@ PANELS = M // WIDTH
 PERIODS = 2 * PANELS
 RING = 4
 ALIGN = 256
-GPSIMD_ODD = 384
-GPSIMD_LAST = 384
+GPSIMD_ODD = 368
+GPSIMD_LAST = 320
 HEAD_V = 96
-GPSIMD_EVEN = 512
-GPSIMD_FIRST = 384
+GPSIMD_EVEN = 480
+GPSIMD_FIRST = 336
 AHEAD1 = 2
 SPLIT = 72
 SPLIT1 = 16
@@ -49,8 +49,12 @@ A6 = 1
 SKIP7 = 2
 OAT = (7,8)
 PRE = 3
+RESTS = (6, 7)
+G6 = 448
+G7 = 352
+WARM3 = 384
 PRE14 = 2
-O2LATE = 0
+O2LATE = 1
 
 
 def tile_spike_covariance_readout_s13_kernel(
@@ -423,12 +427,12 @@ def tile_spike_covariance_readout_s13_kernel(
             }[period]
 
         def share(period):
-            return GPSIMD_FIRST if period == 1 else GPSIMD_ODD if period % 2 else GPSIMD_EVEN
+            return GPSIMD_FIRST if period == 1 else G6 if period == 6 else G7 if period == 7 else GPSIMD_ODD if period % 2 else GPSIMD_EVEN
 
         def vector_port_work(period):
             panel = period // 2 + 1
             planed_unit, direct_unit = 2 * period - 2, 2 * period - 1
-            if share(period) < WIDTH:
+            if share(period) < WIDTH and period not in RESTS:
                 interleave_rest(planed_unit, share(period), nc.vector.tensor_copy)
             if period == 4:
                 for t in range(W3S, 4):
@@ -446,6 +450,7 @@ def tile_spike_covariance_readout_s13_kernel(
         for j in (5, 6, 7, 8):
             empty(j)
         interleave_rest(0, share(1), nc.scalar.copy if REST0S else nc.vector.tensor_copy)
+        warm_up(WARM3, "out_bank0")
         loads_quant(3)
         quant(1)
         lag_quant(1)
@@ -466,6 +471,8 @@ def tile_spike_covariance_readout_s13_kernel(
 
         for period in range(2, PERIODS):
             interleave_gpsimd(2 * period - 2, share(period))
+            if period in RESTS:
+                interleave_rest(2 * period - 2, share(period), nc.scalar.copy)
             early, late = scalar_extras(period)
             mine = period_jobs[period]
             last_on_vector = max([i for i, j in enumerate(mine) if jobs[j][0] != "plane"])

@@ -23,11 +23,11 @@ PANELS = M // WIDTH
 PERIODS = 2 * PANELS
 RING = 4
 ALIGN = 256
-GPSIMD_ODD = 368
+GPSIMD_ODD = 400
 GPSIMD_LAST = 320
 HEAD_V = 96
-GPSIMD_EVEN = 480
-GPSIMD_FIRST = 336
+GPSIMD_EVEN = 512
+GPSIMD_FIRST = 352
 AHEAD1 = 2
 SPLIT = 72
 SPLIT1 = 16
@@ -49,10 +49,16 @@ A6 = 1
 SKIP7 = 2
 OAT = (7,8)
 PRE = 3
+FIRSTLOADS = (0, 2)
+ANCH = ()
+SW = (1,)
+GPFIRST = 1
+DIAGEARLY = 0
+WARM1 = 512
 RESTS = (6, 7)
 G6 = 448
 G7 = 352
-WARM3 = 384
+WARM3 = 128
 PRE14 = 2
 O2LATE = 1
 
@@ -68,11 +74,15 @@ def tile_spike_covariance_readout_s13_kernel(
         ctx.enter_context(tc.manual_schedule())
 
         gp_rows = keep.tile([P, WIDTH], BF16, name="gp_rows")
-        nc.vector.memset(gp_rows[:].bitcast(I32), 0)
+        nc.gpsimd.memset(gp_rows[:].bitcast(I32), 0)
+        ws_sb = keep.tile([P, 4, R], U8, name="ws_sb", align_bytes=ALIGN)
+        nc.vector.memset(ws_sb[:].rearrange("p g n -> p (g n)").bitcast(I32), 0)
         ident = keep.tile([P, P], F32, name="ident")
         make_identity(nc, ident[:])
         lag_factor = keep.tile([P, 4], F32, name="lag_factor")
         nc.scalar.dma_start(out=lag_factor[:], in_=lag_scale.rearrange("(p t) o -> p (t o)", t=4))
+        nc.scalar.dma_start(out=gp_rows[0:4, :], in_=gain.rearrange("(g x) -> g x", g=4))
+        nc.scalar.dma_start(out=gp_rows[4:8, :], in_=private.rearrange("(g x) -> g x", g=4))
 
         lag_view = lag_bytes.rearrange("(p t) j -> p t j", t=4)
         lag_raw, rows = {}, {}
@@ -95,10 +105,8 @@ def tile_spike_covariance_readout_s13_kernel(
                     rows[g, first + t] = tile[:, t, :]
 
         first_order = (0, 3, 1, 2)
-        load_lag(0, first_order)
+        load_lag(0, FIRSTLOADS)
         load_rows(0, parts=2)
-        nc.sync.dma_start(out=gp_rows[0:4, :], in_=gain.rearrange("(g x) -> g x", g=4))
-        nc.sync.dma_start(out=gp_rows[4:8, :], in_=private.rearrange("(g x) -> g x", g=4))
         load_rows(1)
         load_lag(1)
         load_rows(2)
@@ -106,8 +114,9 @@ def tile_spike_covariance_readout_s13_kernel(
         load_lag(2)
         w_sb = keep.tile([P, 4, 2 * R], U8, name="w_sb", align_bytes=ALIGN)
         nc.sync.dma_start(out=w_sb[:], in_=w_words.rearrange("g p n -> p g n"))
-        ws_sb = keep.tile([P, 4, R], U8, name="ws_sb", align_bytes=ALIGN)
-        nc.vector.memset(ws_sb[:].rearrange("p g n -> p (g n)").bitcast(I32), 0)
+        first_bank = psum.tile([P, WIDTH], F32, name="ring3")
+        zeros = ws_sb[:].rearrange("p g n -> p (g n)").bitcast(F32)
+        nc.tensor.matmul(out=first_bank[:, 0:WARM1], lhsT=zeros[:, 0:P], rhs=zeros[:, 0:WARM1], start=True, stop=True)
         ws_view = w_scales.bitcast(I32).rearrange("g q n -> q g n")
         for quad in range(4):
             nc.sync.dma_start(
@@ -343,26 +352,33 @@ def tile_spike_covariance_readout_s13_kernel(
                 if call:
                     call[0](*call[1:])
 
-        warm_up(512, "ring3")
-        loads_turn(0, 0, "out_bank0")
-        loads_turn(0, 1, "out_bank1")
         gp_bank = psum.tile([P, WIDTH], F32, name="out_bank2")
         for u in range(2):
             nc.tensor.transpose(gp_bank[:, P * u : P * (u + 1)], gp_rows[:].bitcast(F32)[:, u:256:2], ident[:])
-        warm_up(WARM2, "ring3")
+        for t in range(4):
+            lag_widen(0, t, on_vector=(t not in SW))
+        for t in ANCH:
+            bank = psum.tile([P, WIDTH], F32, name="ring3")
+            nc.tensor.matmul(out=bank[:], lhsT=lag_planes[0][:, t, 0:P], rhs=lag_planes[0][:, t, :], start=True, stop=True)
+        loads_turn(0, 0, "out_bank0")
+        loads_turn(0, 1, "out_bank1")
+        if WARM2:
+            warm_up(WARM2, "ring3")
         loads_turn(1, 0, "out_bank3")
         loads_turn(1, 1, "ring3")
-        for t in first_order:
-            lag_widen(0, t, on_vector=(t < 3))
-        lag_interleave(0, 0, HEAD_V, True)
-        if HEAD_V < P:
-            lag_interleave(0, HEAD_V, P, False)
-        loads_exit(0, 0)
-        loads_exit(0, 1)
         nc.scalar.copy(
             out=gp_f[:].rearrange("p a (g u e) -> p (a g) u e", u=2, e=2),
             in_=gp_bank[:, 0:256].bitcast(BF16).rearrange("p (u r e) -> p r u e", u=2, e=2)[:, 0:8],
         )
+        lag_interleave(0, 0, HEAD_V, True)
+        if HEAD_V < P:
+            lag_interleave(0, HEAD_V, P, False)
+        if DIAGEARLY:
+            build_diag(0)
+        loads_exit(0, 0)
+        loads_exit(0, 1)
+        if not DIAGEARLY:
+            build_diag(0)
         lag_quant(0)
         loads_quant(0, 0, 256)
         loads_quant(0, 256, WIDTH)
@@ -371,7 +387,6 @@ def tile_spike_covariance_readout_s13_kernel(
         fill(1, "out_bank1")
         fill(3, "ring1")
         fill(4, "ring2")
-        build_diag(0)
         loads_exit(1, 0)
         loads_exit(1, 1)
         loads_turn(2, 0, "out_bank2")
@@ -380,8 +395,6 @@ def tile_spike_covariance_readout_s13_kernel(
             lag_widen(1, t, on_vector=True)
         empty(0)
         empty(2)
-        loads_turn(3, 0, "ring3")
-        loads_turn(3, 1, "ring0")
         loads_quant(1)
         empty(1)
         if SPLIT1:
@@ -389,19 +402,17 @@ def tile_spike_covariance_readout_s13_kernel(
         lag_interleave(1, SPLIT1, P, True)
         fill(5, "out_bank0")
         fill(6, "out_bank1")
+        fill(7, "ring3")
+        fill(8, "ring0")
         loads_exit(2, 0)
         loads_exit(2, 1)
-        fill(7, "out_bank2")
-        fill(8, "out_bank3")
+        loads_turn(3, 0, "out_bank2")
+        loads_turn(3, 1, "out_bank3")
         loads_quant(2)
         empty(3)
         empty(4)
         fill(9)
         fill(10)
-        loads_exit(3, 0)
-        loads_exit(3, 1)
-        fill(11)
-        fill(12)
 
         def passes_ahead(period):
             return AHEAD1 if period == 1 else A6 if period == 6 else 1
@@ -447,10 +458,15 @@ def tile_spike_covariance_readout_s13_kernel(
                 lag_interleave(panel, SPLIT if period == 2 else SPLIT3, P, True)
 
         interleave_gpsimd(0, share(1))
+        interleave_rest(0, share(1), nc.scalar.copy)
+        loads_exit(3, 0)
+        loads_exit(3, 1)
         for j in (5, 6, 7, 8):
             empty(j)
-        interleave_rest(0, share(1), nc.scalar.copy if REST0S else nc.vector.tensor_copy)
-        warm_up(WARM3, "out_bank0")
+        fill(11)
+        fill(12)
+        if WARM3:
+            warm_up(WARM3, "out_bank0")
         loads_quant(3)
         quant(1)
         lag_quant(1)

@@ -23,17 +23,17 @@ PANELS = M // WIDTH
 PERIODS = 2 * PANELS
 RING = 4
 ALIGN = 256
-GPSIMD_ODD = 400
+GPSIMD_ODD = 384
 GPSIMD_LAST = 320
 HEAD_V = 96
 GPSIMD_EVEN = 512
 GPSIMD_FIRST = 352
 AHEAD1 = 2
-SPLIT = 72
+SPLIT = 64
 SPLIT1 = 16
 SPLIT3 = 72
 W2EARLY = 2
-I2EARLY = 72
+I2EARLY = 64
 I3EARLY = 72
 W3EARLY = 2
 W3S = 3
@@ -41,7 +41,7 @@ IVLATE = ()
 REST0S = 1
 AHEAD1A = 1
 HIDE = (1, 2, 3, 4, 5)
-WARM2 = 256
+WARM2 = 128
 E7 = 2
 TAILORD = 0
 O3FIRST = 0
@@ -49,16 +49,14 @@ A6 = 1
 SKIP7 = 2
 OAT = (7,8)
 PRE = 3
-FIRSTLOADS = (0, 2)
-ANCH = ()
-SW = (1,)
-GPFIRST = 1
-DIAGEARLY = 0
+ORD = (0,1,2,3)
+FIRSTLOADS = (0,2)
+SW = 1
 WARM1 = 512
 RESTS = (6, 7)
 G6 = 448
 G7 = 352
-WARM3 = 128
+WARM3 = 256
 PRE14 = 2
 O2LATE = 1
 
@@ -74,15 +72,11 @@ def tile_spike_covariance_readout_s13_kernel(
         ctx.enter_context(tc.manual_schedule())
 
         gp_rows = keep.tile([P, WIDTH], BF16, name="gp_rows")
-        nc.gpsimd.memset(gp_rows[:].bitcast(I32), 0)
-        ws_sb = keep.tile([P, 4, R], U8, name="ws_sb", align_bytes=ALIGN)
-        nc.vector.memset(ws_sb[:].rearrange("p g n -> p (g n)").bitcast(I32), 0)
+        nc.vector.memset(gp_rows[:].bitcast(I32), 0)
         ident = keep.tile([P, P], F32, name="ident")
         make_identity(nc, ident[:])
         lag_factor = keep.tile([P, 4], F32, name="lag_factor")
         nc.scalar.dma_start(out=lag_factor[:], in_=lag_scale.rearrange("(p t) o -> p (t o)", t=4))
-        nc.scalar.dma_start(out=gp_rows[0:4, :], in_=gain.rearrange("(g x) -> g x", g=4))
-        nc.scalar.dma_start(out=gp_rows[4:8, :], in_=private.rearrange("(g x) -> g x", g=4))
 
         lag_view = lag_bytes.rearrange("(p t) j -> p t j", t=4)
         lag_raw, rows = {}, {}
@@ -104,9 +98,11 @@ def tile_spike_covariance_readout_s13_kernel(
                 for t in range(step):
                     rows[g, first + t] = tile[:, t, :]
 
-        first_order = (0, 3, 1, 2)
+        first_order = ORD
         load_lag(0, FIRSTLOADS)
         load_rows(0, parts=2)
+        nc.sync.dma_start(out=gp_rows[0:4, :], in_=gain.rearrange("(g x) -> g x", g=4))
+        nc.sync.dma_start(out=gp_rows[4:8, :], in_=private.rearrange("(g x) -> g x", g=4))
         load_rows(1)
         load_lag(1)
         load_rows(2)
@@ -114,9 +110,8 @@ def tile_spike_covariance_readout_s13_kernel(
         load_lag(2)
         w_sb = keep.tile([P, 4, 2 * R], U8, name="w_sb", align_bytes=ALIGN)
         nc.sync.dma_start(out=w_sb[:], in_=w_words.rearrange("g p n -> p g n"))
-        first_bank = psum.tile([P, WIDTH], F32, name="ring3")
-        zeros = ws_sb[:].rearrange("p g n -> p (g n)").bitcast(F32)
-        nc.tensor.matmul(out=first_bank[:, 0:WARM1], lhsT=zeros[:, 0:P], rhs=zeros[:, 0:WARM1], start=True, stop=True)
+        ws_sb = keep.tile([P, 4, R], U8, name="ws_sb", align_bytes=ALIGN)
+        nc.vector.memset(ws_sb[:].rearrange("p g n -> p (g n)").bitcast(I32), 0)
         ws_view = w_scales.bitcast(I32).rearrange("g q n -> q g n")
         for quad in range(4):
             nc.sync.dma_start(
@@ -352,33 +347,27 @@ def tile_spike_covariance_readout_s13_kernel(
                 if call:
                     call[0](*call[1:])
 
+        warm_up(WARM1, "ring3")
+        loads_turn(0, 0, "out_bank0")
+        loads_turn(0, 1, "out_bank1")
         gp_bank = psum.tile([P, WIDTH], F32, name="out_bank2")
         for u in range(2):
             nc.tensor.transpose(gp_bank[:, P * u : P * (u + 1)], gp_rows[:].bitcast(F32)[:, u:256:2], ident[:])
-        for t in range(4):
-            lag_widen(0, t, on_vector=(t not in SW))
-        for t in ANCH:
-            bank = psum.tile([P, WIDTH], F32, name="ring3")
-            nc.tensor.matmul(out=bank[:], lhsT=lag_planes[0][:, t, 0:P], rhs=lag_planes[0][:, t, :], start=True, stop=True)
-        loads_turn(0, 0, "out_bank0")
-        loads_turn(0, 1, "out_bank1")
         if WARM2:
             warm_up(WARM2, "ring3")
         loads_turn(1, 0, "out_bank3")
         loads_turn(1, 1, "ring3")
+        for t in first_order:
+            lag_widen(0, t, on_vector=(t != SW))
+        lag_interleave(0, 0, HEAD_V, True)
+        if HEAD_V < P:
+            lag_interleave(0, HEAD_V, P, False)
+        loads_exit(0, 0)
+        loads_exit(0, 1)
         nc.scalar.copy(
             out=gp_f[:].rearrange("p a (g u e) -> p (a g) u e", u=2, e=2),
             in_=gp_bank[:, 0:256].bitcast(BF16).rearrange("p (u r e) -> p r u e", u=2, e=2)[:, 0:8],
         )
-        lag_interleave(0, 0, HEAD_V, True)
-        if HEAD_V < P:
-            lag_interleave(0, HEAD_V, P, False)
-        if DIAGEARLY:
-            build_diag(0)
-        loads_exit(0, 0)
-        loads_exit(0, 1)
-        if not DIAGEARLY:
-            build_diag(0)
         lag_quant(0)
         loads_quant(0, 0, 256)
         loads_quant(0, 256, WIDTH)
@@ -387,6 +376,7 @@ def tile_spike_covariance_readout_s13_kernel(
         fill(1, "out_bank1")
         fill(3, "ring1")
         fill(4, "ring2")
+        build_diag(0)
         loads_exit(1, 0)
         loads_exit(1, 1)
         loads_turn(2, 0, "out_bank2")

@@ -24,41 +24,9 @@ PERIODS = 2 * PANELS
 RING = 4
 ALIGN = 256
 GPSIMD_ODD = 384
+GPSIMD_LATE_START = 352
 GPSIMD_LAST = 320
-HEAD_V = 96
-GPSIMD_EVEN = 512
-GPSIMD_FIRST = 352
-AHEAD1 = 2
-SPLIT = 64
-SPLIT1 = 16
-SPLIT3 = 72
-W2EARLY = 2
-I2EARLY = 64
-I3EARLY = 72
-W3EARLY = 2
-W3S = 3
-IVLATE = ()
-REST0S = 1
-AHEAD1A = 1
-HIDE = (1, 2, 3, 4, 5)
-WARM2 = 128
-E7 = 2
-TAILORD = 0
-O3FIRST = 0
-A6 = 1
-SKIP7 = 2
-OAT = (7,8)
-PRE = 3
-ORD = (0,1,2,3)
-FIRSTLOADS = (0,2)
-SW = 1
-WARM1 = 512
-RESTS = (6, 7)
-G6 = 448
-G7 = 352
-WARM3 = 256
-PRE14 = 2
-O2LATE = 1
+FILLS_FIRST = 2
 
 
 def tile_spike_covariance_readout_s13_kernel(
@@ -81,11 +49,11 @@ def tile_spike_covariance_readout_s13_kernel(
         lag_view = lag_bytes.rearrange("(p t) j -> p t j", t=4)
         lag_raw, rows = {}, {}
 
-        def load_lag(panel, first_slots=(0,)):
+        def load_lag(panel, parts=1):
             raw = keep.tile([P, 4, WIDTH], U8, name="lag_raw%d" % panel, align_bytes=ALIGN)
-            step = 4 // len(first_slots)
+            step = 4 // parts
             columns = slice(WIDTH * panel, WIDTH * (panel + 1))
-            for t in first_slots:
+            for t in range(0, 4, step):
                 nc.sync.dma_start(out=raw[:, t : t + step, :], in_=lag_view[:, t : t + step, columns])
             lag_raw[panel] = raw
 
@@ -98,8 +66,7 @@ def tile_spike_covariance_readout_s13_kernel(
                 for t in range(step):
                     rows[g, first + t] = tile[:, t, :]
 
-        first_order = ORD
-        load_lag(0, FIRSTLOADS)
+        load_lag(0, parts=2)
         load_rows(0, parts=2)
         nc.sync.dma_start(out=gp_rows[0:4, :], in_=gain.rearrange("(g x) -> g x", g=4))
         nc.sync.dma_start(out=gp_rows[4:8, :], in_=private.rearrange("(g x) -> g x", g=4))
@@ -124,25 +91,20 @@ def tile_spike_covariance_readout_s13_kernel(
         gain_f, priv_f = gp_f[:, 0, :], gp_f[:, 1, :]
         diag = keep.tile([P, 16, P], BF16, name="diag")
 
+        def psum_bank(name):
+            return psum.tile([P, WIDTH], F32, name=name)
+
         def warm_up(width, bank_name):
-            bank = psum.tile([P, WIDTH], F32, name=bank_name)
             moving = ident[:].unsqueeze(1).to_broadcast([P, width // P, P])
-            nc.tensor.matmul(
-                out=bank[:, 0:width].rearrange("p (a c) -> p a c", c=P), lhsT=ident[:], rhs=moving, start=True, stop=True
-            )
+            product = psum_bank(bank_name)[:, 0:width].rearrange("p (a c) -> p a c", c=P)
+            nc.tensor.matmul(out=product, lhsT=ident[:], rhs=moving, start=True, stop=True)
 
         def build_diag(g):
             for i in range(4 * g, 4 * g + 4):
                 nc.scalar.activation(out=diag[:, i, :], in_=ident[:], func=ACT.Copy, scale=priv_f[:, i : i + 1])
 
-        holder = {}
-        for_gpsimd, for_vector, spare = "grouped0", "grouped1", "grouped2"
-        for period in range(1, PERIODS + 1):
-            holder[2 * period - 2], holder[2 * period - 1] = for_gpsimd, for_vector
-            if period in HIDE:
-                for_vector, spare = spare, for_vector
-            else:
-                for_gpsimd, for_vector, spare = for_vector, spare, for_gpsimd
+        def gpsimd_tile():
+            return work.tile([P, 4 * WIDTH], BF16, name="planed_grouped", bufs=1, align_bytes=ALIGN)
 
         lag_planes, lag_grouped, lag_codes, lag_scales = {}, {}, {}, {}
         ld_grouped, ld_codes, ld_scales, turned = {}, {}, {}, {}
@@ -156,13 +118,11 @@ def tile_spike_covariance_readout_s13_kernel(
             else:
                 nc.scalar.activation(out=dst, in_=src, func=ACT.Copy, scale=factor)
 
-        def lag_interleave(panel, lo, hi, on_vector):
+        def lag_interleave(panel, lo, hi, copy):
             if panel not in lag_grouped:
                 lag_grouped[panel] = work.tile([P, WIDTH, 4], BF16, name="lag_grouped", bufs=2, align_bytes=ALIGN)
-            part = slice(lo, hi)
-            src = lag_planes[panel][:].rearrange("p t (m s) -> p m t s", s=4)[:, part]
-            dst = lag_grouped[panel][:].rearrange("p (s m) t -> p m t s", s=4)[:, part]
-            copy = nc.vector.tensor_copy if on_vector else nc.scalar.copy
+            src = lag_planes[panel][:].rearrange("p t (m s) -> p m t s", s=4)[:, lo:hi]
+            dst = lag_grouped[panel][:].rearrange("p (s m) t -> p m t s", s=4)[:, lo:hi]
             copy(out=dst, in_=src)
 
         def lag_quant(panel):
@@ -174,28 +134,28 @@ def tile_spike_covariance_readout_s13_kernel(
                 in_=lag_grouped[panel][:].rearrange("p c t -> p (c t)"),
             )
 
-        def loads_turn(g, half, bank_name):
-            bank = psum.tile([P, WIDTH], F32, name=bank_name)
-            view = bank[:].rearrange("p (t u m) -> p t u m", t=2, u=2)
-            for t in range(2):
-                words = rows[g, 2 * half + t].bitcast(F32)
-                for u in range(2):
-                    nc.tensor.transpose(view[:, t, u, :], words[:, u:256:2], ident[:])
-            turned[g, half] = bank
+        def loads_turn(g, bank_names):
+            for half in range(2):
+                turned[g, half] = psum_bank(bank_names[half])
+                view = turned[g, half][:].rearrange("p (t u m) -> p t u m", t=2, u=2)
+                for t in range(2):
+                    words = rows[g, 2 * half + t].bitcast(F32)
+                    for u in range(2):
+                        nc.tensor.transpose(view[:, t, u, :], words[:, u:256:2], ident[:])
 
-        def loads_exit(g, half):
-            if half == 0:
-                if g == 2:
-                    ld_grouped[g] = work.tile([P, 4 * WIDTH], BF16, name=holder[0], bufs=1, align_bytes=ALIGN)
-                else:
-                    ld_grouped[g] = work.tile([P, 4 * WIDTH], BF16, name="ld_grouped", bufs=3, align_bytes=ALIGN)
-                ld_codes[g] = keep.tile([P, WIDTH], U32, name="ld_codes%d" % g, align_bytes=ALIGN)
-                ld_scales[g] = keep.tile([P, WIDTH], U8, name="ld_scales%d" % g, align_bytes=ALIGN)
-            dst = ld_grouped[g][:, 1024 * half : 1024 * half + 1024].bitcast(F32)
-            nc.scalar.copy(
-                out=dst.rearrange("p (t m u) -> p t m u", t=2, u=2),
-                in_=turned[g, half][:].rearrange("p (t u m) -> p t m u", t=2, u=2),
-            )
+        def loads_exit(g):
+            if g == 2:
+                ld_grouped[g] = gpsimd_tile()
+            else:
+                ld_grouped[g] = work.tile([P, 4 * WIDTH], BF16, name="ld_grouped", bufs=3, align_bytes=ALIGN)
+            ld_codes[g] = keep.tile([P, WIDTH], U32, name="ld_codes%d" % g, align_bytes=ALIGN)
+            ld_scales[g] = keep.tile([P, WIDTH], U8, name="ld_scales%d" % g, align_bytes=ALIGN)
+            for half in range(2):
+                dst = ld_grouped[g][:, 1024 * half : 1024 * half + 1024].bitcast(F32)
+                nc.scalar.copy(
+                    out=dst.rearrange("p (t m u) -> p t m u", t=2, u=2),
+                    in_=turned[g, half][:].rearrange("p (t u m) -> p t m u", t=2, u=2),
+                )
 
         def loads_quant(g, lo=0, hi=WIDTH):
             nc.vector.quantize_mx(
@@ -224,12 +184,10 @@ def tile_spike_covariance_readout_s13_kernel(
                 stop=True,
             )
 
-        def fill(j, bank_name=None):
-            if j >= len(jobs):
-                return
-            kind, n, x = jobs[j]
-            bank = psum.tile([P, WIDTH], F32, name=bank_name or "ring%d" % (j % RING))
-            banks[j] = bank
+        def fill(job, bank_name):
+            kind, n, x = job
+            bank = psum_bank(bank_name)
+            banks[job] = bank
             if kind == "direct":
                 for t in range(4):
                     s_pass(bank, P * t, n, t, P * x, P * (x + 1))
@@ -248,12 +206,12 @@ def tile_spike_covariance_readout_s13_kernel(
                 planes[n] = work.tile([P, 4, WIDTH], BF16, name="planes", bufs=3, align_bytes=ALIGN)
             return planes[n]
 
-        def empty(j):
-            kind, n, x = jobs[j]
-            g, bank = group(n), banks[j]
+        def empty(job):
+            kind, n, x = job
+            g, bank = group(n), banks[job]
             if kind == "direct":
                 if x == 0:
-                    grouped[n] = work.tile([P, 4 * WIDTH], BF16, name=holder[n], bufs=1, align_bytes=ALIGN)
+                    grouped[n] = work.tile([P, 4 * WIDTH], BF16, name="direct_grouped", bufs=2, align_bytes=ALIGN)
                 nc.vector.tensor_tensor(
                     out=grouped[n][:, WIDTH * x : WIDTH * (x + 1)].rearrange("p (c t) -> p c t", t=4),
                     in0=bank[:].rearrange("p (t c) -> p c t", t=4),
@@ -282,7 +240,7 @@ def tile_spike_covariance_readout_s13_kernel(
                         )
 
         def interleave_gpsimd(n, hi):
-            grouped[n] = work.tile([P, 4 * WIDTH], BF16, name=holder[n], bufs=1, align_bytes=ALIGN)
+            grouped[n] = gpsimd_tile()
             nc.gpsimd.tensor_scalar(
                 out=grouped[n][:, 0 : 4 * hi].rearrange("p (c t) -> p c t", t=4),
                 in0=planes[n][:, :, 0:hi].rearrange("p t c -> p c t"),
@@ -310,7 +268,7 @@ def tile_spike_covariance_readout_s13_kernel(
             count = added.get((panel, r), 0)
             added[panel, r] = count + 1
             if count == 0:
-                out_banks[panel, r] = psum.tile([P, WIDTH], F32, name="out_bank%d" % r)
+                out_banks[panel, r] = psum_bank("out_bank%d" % r)
             nc.tensor.matmul_mx(
                 out=out_banks[panel, r][:],
                 lhsT=w_sb[:, g, 2 * P * r : 2 * P * (r + 1)].bitcast(FP4X4),
@@ -331,204 +289,163 @@ def tile_spike_covariance_readout_s13_kernel(
                 j = WIDTH * panel + 4 * m
                 nc.sync.dma_start(out=out[P * r : P * (r + 1), j : j + 4 * step], in_=staged[:, 4 * m : 4 * (m + step)])
 
-        jobs = [("plane", 0, 0), ("windows", 0, 0), ("plane", 0, 1), ("plane", 0, 2), ("plane", 0, 3)]
-        period_jobs = [list(range(len(jobs)))]
-        for period in range(1, PERIODS + 1):
-            direct = [("direct", 2 * period - 1, q) for q in range(4)]
-            plane = [("plane", 2 * period, t) for t in range(4)] if period < PERIODS else []
-            windows = [("windows", 2 * period, 0)] if period < PERIODS and has_diag(2 * period) else []
-            leading = 1 if period > 1 else 0
-            mine = direct[:3] + plane[:leading] + direct[3:] + windows + plane[leading:]
-            period_jobs.append(list(range(len(jobs), len(jobs) + len(mine))))
-            jobs.extend(mine)
-
         def run(calls):
             for call in calls:
                 if call:
                     call[0](*call[1:])
 
-        warm_up(WARM1, "ring3")
-        loads_turn(0, 0, "out_bank0")
-        loads_turn(0, 1, "out_bank1")
-        gp_bank = psum.tile([P, WIDTH], F32, name="out_bank2")
+        period_jobs = {1: [("plane", 2, t) for t in range(4)]}
+        for period in range(2, PERIODS + 1):
+            direct = [("direct", 2 * period - 1, q) for q in range(4)]
+            plane = [("plane", 2 * period, t) for t in range(4)] if period < PERIODS else []
+            windows = [("windows", 2 * period, 0)] if period < PERIODS and has_diag(2 * period) else []
+            period_jobs[period] = direct[:3] + plane[:1] + direct[3:] + windows + plane[1:]
+        ring_jobs = [job for period in range(1, PERIODS + 1) for job in period_jobs[period]]
+
+        def ring_fill(i):
+            if i < len(ring_jobs):
+                fill(ring_jobs[i], "ring%d" % ((i + 1) % RING))
+
+        def refill(job):
+            ring_fill(ring_jobs.index(job) + RING)
+
+        plane0 = [("plane", 0, t) for t in range(4)]
+        windows0 = ("windows", 0, 0)
+        direct1 = [("direct", 1, q) for q in range(4)]
+        warm_up(WIDTH, "ring3")
+        loads_turn(0, ("out_bank0", "out_bank1"))
+        gp_bank = psum_bank("out_bank2")
         for u in range(2):
             nc.tensor.transpose(gp_bank[:, P * u : P * (u + 1)], gp_rows[:].bitcast(F32)[:, u:256:2], ident[:])
-        if WARM2:
-            warm_up(WARM2, "ring3")
-        loads_turn(1, 0, "out_bank3")
-        loads_turn(1, 1, "ring3")
-        for t in first_order:
-            lag_widen(0, t, on_vector=(t != SW))
-        lag_interleave(0, 0, HEAD_V, True)
-        if HEAD_V < P:
-            lag_interleave(0, HEAD_V, P, False)
-        loads_exit(0, 0)
-        loads_exit(0, 1)
+        warm_up(WIDTH // 2, "ring3")
+        loads_turn(1, ("out_bank3", "ring3"))
+        for t in range(4):
+            lag_widen(0, t, on_vector=(t != 1))
+        lag_interleave(0, 0, P, nc.vector.tensor_copy)
+        loads_exit(0)
         nc.scalar.copy(
             out=gp_f[:].rearrange("p a (g u e) -> p (a g) u e", u=2, e=2),
             in_=gp_bank[:, 0:256].bitcast(BF16).rearrange("p (u r e) -> p r u e", u=2, e=2)[:, 0:8],
         )
         lag_quant(0)
-        loads_quant(0, 0, 256)
-        loads_quant(0, 256, WIDTH)
-        fill(0, "out_bank0")
-        fill(2, "ring0")
-        fill(1, "out_bank1")
-        fill(3, "ring1")
-        fill(4, "ring2")
+        loads_quant(0, 0, WIDTH // 2)
+        loads_quant(0, WIDTH // 2, WIDTH)
+        fill(plane0[0], "out_bank0")
+        fill(plane0[1], "ring0")
+        fill(windows0, "out_bank1")
+        fill(plane0[2], "ring1")
+        fill(plane0[3], "ring2")
         build_diag(0)
-        loads_exit(1, 0)
-        loads_exit(1, 1)
-        loads_turn(2, 0, "out_bank2")
-        loads_turn(2, 1, "out_bank3")
+        loads_exit(1)
+        loads_turn(2, ("out_bank2", "out_bank3"))
         for t in range(4):
             lag_widen(1, t, on_vector=True)
-        empty(0)
-        empty(2)
+        empty(plane0[0])
+        empty(plane0[1])
         loads_quant(1)
-        empty(1)
-        if SPLIT1:
-            lag_interleave(1, 0, SPLIT1, False)
-        lag_interleave(1, SPLIT1, P, True)
-        fill(5, "out_bank0")
-        fill(6, "out_bank1")
-        fill(7, "ring3")
-        fill(8, "ring0")
-        loads_exit(2, 0)
-        loads_exit(2, 1)
-        loads_turn(3, 0, "out_bank2")
-        loads_turn(3, 1, "out_bank3")
+        empty(windows0)
+        lag_interleave(1, 0, P, nc.vector.tensor_copy)
+        for job, name in zip(direct1, ("out_bank0", "out_bank1", "ring3", "ring0")):
+            fill(job, name)
+        loads_exit(2)
+        loads_turn(3, ("out_bank2", "out_bank3"))
         loads_quant(2)
-        empty(3)
-        empty(4)
-        fill(9)
-        fill(10)
+        empty(plane0[2])
+        empty(plane0[3])
+        ring_fill(0)
+        ring_fill(1)
 
-        def passes_ahead(period):
-            return AHEAD1 if period == 1 else A6 if period == 6 else 1
-
-        def passes_due(period):
-            planed_unit, direct_unit, done = 2 * period - 4, 2 * period - 3, passes_ahead(period - 1)
-            return [(out_pass, planed_unit, r) for r in range(done)] + [
-                (out_pass, n, r) for r in range(done, 4) for n in (direct_unit, planed_unit)
-            ]
+        interleave_gpsimd(0, GPSIMD_LATE_START)
+        interleave_rest(0, GPSIMD_LATE_START, nc.scalar.copy)
+        loads_exit(3)
+        for job in direct1:
+            empty(job)
+        ring_fill(2)
+        ring_fill(3)
+        warm_up(WIDTH // 2, "out_bank0")
+        loads_quant(3)
+        quant(1)
+        quant(0)
+        lag_quant(1)
+        for i, job in enumerate(period_jobs[1]):
+            empty(job)
+            if i == 2:
+                out_pass(1, 0)
+            refill(job)
+        lag_widen(2, 0)
+        lag_widen(2, 1)
 
         def scalar_extras(period):
-            W = lambda panel, ts: [(lag_widen, panel, t) for t in ts]
-            O = lambda panel, rs: [(out_exit, panel, r) for r in rs]
-            I = lambda panel, lo, hi: [(lag_interleave, panel, lo, hi, False)] * (hi > lo)
-            return {
-                1: ([], W(2, range(W2EARLY))),
-                2: ([(build_diag, 1)] + W(2, range(W2EARLY, 4)), I(2, 0, I2EARLY)),
-                3: (O(0, (0,)) + I(2, I2EARLY, SPLIT) + O(0, (1,)), O(0, (2,)) + W(3, range(W3EARLY))),
-                4: ([(build_diag, 2)] + O(0, (3,)) + W(3, range(W3EARLY, W3S)), I(3, 0, I3EARLY)),
-                5: (O(1, (0,)) + I(3, I3EARLY, SPLIT3) + O(1, (1,)), O(1, (2,))),
-                6: ([(build_diag, 3)] + O(1, (3,)), []),
-                7: (O(2, range(E7)), O(2, range(E7, 3))),
-            }[period]
-
-        def share(period):
-            return GPSIMD_FIRST if period == 1 else G6 if period == 6 else G7 if period == 7 else GPSIMD_ODD if period % 2 else GPSIMD_EVEN
+            panel = (period + 3) // 2
+            widen = [(lag_widen, panel, t) for t in range(4 if panel == 2 else 3)] if panel < PANELS else []
+            exits = [(out_exit, (period - 3) // 2, r) for r in range(4)] if period >= 3 else []
+            if period == PERIODS - 1:
+                return [], exits[:1]
+            if period % 2 == 1:
+                return exits[:2], exits[2:3] + widen[:2]
+            half = [(lag_interleave, panel, 0, P // 2, nc.scalar.copy)] if panel < PANELS else []
+            return [(build_diag, period // 2)] + exits[3:] + widen[2:], half
 
         def vector_port_work(period):
             panel = period // 2 + 1
-            planed_unit, direct_unit = 2 * period - 2, 2 * period - 1
-            if share(period) < WIDTH and period not in RESTS:
-                interleave_rest(planed_unit, share(period), nc.vector.tensor_copy)
-            if period == 4:
-                for t in range(W3S, 4):
-                    lag_widen(3, t, True)
-            quant(direct_unit)
-            if period in IVLATE:
-                lag_interleave(panel, SPLIT if period == 3 else SPLIT3, P, True)
-            quant(planed_unit)
             if period in (3, 5):
+                interleave_rest(2 * period - 2, GPSIMD_ODD, nc.vector.tensor_copy)
+            if period == 4:
+                lag_widen(panel, 3, on_vector=True)
+            quant(2 * period - 1)
+            quant(2 * period - 2)
+            if panel < PANELS and period % 2 == 1:
                 lag_quant(panel)
-            if period in (2, 4) and period + 1 not in IVLATE:
-                lag_interleave(panel, SPLIT if period == 2 else SPLIT3, P, True)
+            if panel < PANELS and period % 2 == 0:
+                lag_interleave(panel, P // 2, P, nc.vector.tensor_copy)
 
-        interleave_gpsimd(0, share(1))
-        interleave_rest(0, share(1), nc.scalar.copy)
-        loads_exit(3, 0)
-        loads_exit(3, 1)
-        for j in (5, 6, 7, 8):
-            empty(j)
-        fill(11)
-        fill(12)
-        if WARM3:
-            warm_up(WARM3, "out_bank0")
-        loads_quant(3)
-        quant(1)
-        lag_quant(1)
-        quant(0)
-        empty(9)
-        fill(13)
-        empty(10)
-        fill(14)
-        empty(11)
-        for r in range(AHEAD1A):
-            out_pass(1, r)
-        fill(15)
-        empty(12)
-        for r in range(AHEAD1A, AHEAD1):
-            out_pass(1, r)
-        fill(16)
-        run(scalar_extras(1)[1])
+        def passes_due(period):
+            planed_unit, direct_unit = 2 * period - 4, 2 * period - 3
+            return [(out_pass, planed_unit, 0)] + [
+                (out_pass, n, r) for r in range(1, 4) for n in (direct_unit, planed_unit)
+            ]
 
         for period in range(2, PERIODS):
-            interleave_gpsimd(2 * period - 2, share(period))
-            if period in RESTS:
-                interleave_rest(2 * period - 2, share(period), nc.scalar.copy)
-            early, late = scalar_extras(period)
+            planed_unit = 2 * period - 2
             mine = period_jobs[period]
-            last_on_vector = max([i for i, j in enumerate(mine) if jobs[j][0] != "plane"])
             due = passes_due(period)
-            passes = due + [None] * (len(mine) - len(due)) + [(out_pass, 2 * period - 1, 0)] * passes_ahead(period)
-            if period == 7:
-                passes = [None] * SKIP7 + due
-                early, late = [], []
+            if period == PERIODS - 1:
+                interleave_gpsimd(planed_unit, GPSIMD_LATE_START)
+                interleave_rest(planed_unit, GPSIMD_LATE_START, nc.scalar.copy)
+                passes = [None] * FILLS_FIRST + due
+            else:
+                interleave_gpsimd(planed_unit, GPSIMD_ODD if period % 2 else WIDTH)
+                passes = due + [None] * (len(mine) - len(due)) + [(out_pass, 2 * period - 1, 0)]
+            early, late = scalar_extras(period)
+            last_on_vector = max([i for i, job in enumerate(mine) if job[0] != "plane"])
             run(passes[:1])
-            for i, j in enumerate(mine):
+            for i, job in enumerate(mine):
                 run(passes[i + 1 : i + 2])
-                empty(j)
+                empty(job)
                 if i == 3:
                     run(early)
-                if period == 7 and i == OAT[0]:
-                    out_exit(2, 0)
-                if period == 7 and i == OAT[1]:
-                    out_exit(2, 1)
                 if i == last_on_vector:
                     vector_port_work(period)
-                fill(j + RING)
+                refill(job)
             run(late)
-        run(passes[len(mine) + 1 :])
 
         interleave_gpsimd(14, GPSIMD_LAST)
-        for r in range(2):
-            if OAT[r] > 7:
-                out_exit(2, r)
-        if not O2LATE:
-            out_exit(2, 2)
+        out_exit(PANELS - 2, 1)
         interleave_rest(14, GPSIMD_LAST, nc.scalar.copy)
-        if O2LATE:
-            out_exit(2, 2)
-        out_exit(2, 3)
-        for r in range(PRE):
+        out_exit(PANELS - 2, 2)
+        out_exit(PANELS - 2, 3)
+        for r in range(3):
             out_pass(13, r)
             out_pass(12, r)
-        for j in period_jobs[PERIODS]:
-            empty(j)
+        for job in period_jobs[PERIODS]:
+            empty(job)
         quant(14)
         quant(15)
-        for r in range(PRE14):
-            out_pass(14, r)
-        for r in range(4):
-            if r >= PRE:
-                out_pass(13, r)
-                out_pass(12, r)
-            if r >= PRE14:
-                out_pass(14, r)
-            out_pass(15, r)
+        out_pass(14, 0)
+        out_pass(14, 1)
+        for r, units in enumerate(((15,), (15,), (14, 15), (13, 12, 14, 15))):
+            for n in units:
+                out_pass(n, r)
             if r in (0, 3):
                 out_exit(PANELS - 1, r, parts=2)
             else:

@@ -43,6 +43,8 @@ def tile_spike_covariance_readout_s13_kernel(
         nc.vector.memset(gp_rows[:].bitcast(I32), 0)
         ident = keep.tile([P, P], F32, name="ident")
         make_identity(nc, ident[:])
+        ident_bf = keep.tile([P, P], BF16, name="ident_bf")
+        nc.vector.tensor_copy(out=ident_bf[:], in_=ident[:])
         lag_factor = keep.tile([P, 4], F32, name="lag_factor")
         nc.scalar.dma_start(out=lag_factor[:], in_=lag_scale.rearrange("(p t) o -> p (t o)", t=4))
 
@@ -314,19 +316,21 @@ def tile_spike_covariance_readout_s13_kernel(
         direct1 = [("direct", 1, q) for q in range(4)]
         warm_up(WIDTH, "ring3")
         loads_turn(0, ("out_bank0", "out_bank1"))
-        gp_bank = psum_bank("out_bank2")
-        for u in range(2):
-            nc.tensor.transpose(gp_bank[:, P * u : P * (u + 1)], gp_rows[:].bitcast(F32)[:, u:256:2], ident[:])
-        warm_up(WIDTH // 2, "ring3")
+        gp_banks = [psum_bank("out_bank2"), psum_bank("ring2")]
+        for t in range(4):
+            product = gp_banks[t // 2][:, 256 * (t % 2) : 256 * (t % 2 + 1)].rearrange("p (a c) -> p a c", c=P)
+            moving = ident_bf[:].unsqueeze(1).to_broadcast([P, 2, P])
+            nc.tensor.matmul(out=product, lhsT=gp_rows[:, t:WIDTH:4], rhs=moving, start=True, stop=True)
         loads_turn(1, ("out_bank3", "ring3"))
         for t in range(4):
             lag_widen(0, t, on_vector=(t != 1))
         lag_interleave(0, 0, P, nc.vector.tensor_copy)
         loads_exit(0)
-        nc.scalar.copy(
-            out=gp_f[:].rearrange("p a (g u e) -> p (a g) u e", u=2, e=2),
-            in_=gp_bank[:, 0:256].bitcast(BF16).rearrange("p (u r e) -> p r u e", u=2, e=2)[:, 0:8],
-        )
+        for half in range(2):
+            nc.scalar.copy(
+                out=gp_f[:].rearrange("p a (g t) -> p (a g) t", t=4)[:, :, 2 * half : 2 * half + 2],
+                in_=gp_banks[half][:].rearrange("p (t r) -> p r t", t=2)[:, 0:8],
+            )
         lag_quant(0)
         loads_quant(0, 0, WIDTH // 2)
         loads_quant(0, WIDTH // 2, WIDTH)

@@ -19,14 +19,15 @@ FLOPS = 2 * M * K * M + 2 * R * M * M
 
 P = 128
 WIDTH = 512
-PANELS = M // WIDTH
-PERIODS = 2 * PANELS
-RING = 4
 ALIGN = 256
-GPSIMD_ODD = 384
-GPSIMD_LATE_START = 352
-GPSIMD_LAST = 320
-FILLS_FIRST = 2
+STRIPS = [(0, 512), (512, 512), (1024, 512), (1536, 512)]
+UNITS = [(k, ((k + d) % 4,)) for k in range(4) for d in (0, 1, 2, 3)]
+A0 = 128
+G_ODD = 384
+G_LATE = 352
+G_LAST = 320
+NW = 4
+PAIRED = ()
 
 
 def tile_spike_covariance_readout_s13_kernel(
@@ -34,423 +35,538 @@ def tile_spike_covariance_readout_s13_kernel(
 ):
     nc = tc.nc
     with ExitStack() as ctx:
-        keep = ctx.enter_context(tc.tile_pool(name="keep", bufs=1))
-        work = ctx.enter_context(tc.tile_pool(name="work", bufs=3))
+        sb = ctx.enter_context(tc.tile_pool(name="sb", bufs=1))
         psum = ctx.enter_context(tc.psum_pool(name="psum", bufs=1))
         ctx.enter_context(tc.manual_schedule())
 
-        gp_rows = keep.tile([P, WIDTH], BF16, name="gp_rows")
+        def tile(shape, dtype, name):
+            return sb.tile(shape, dtype, name=name, align_bytes=ALIGN)
+
+        warm = tile([P, P], BF16, "warm")
+        nc.vector.memset(warm[:].bitcast(I32), 0)
+        gp_rows = tile([P, WIDTH], BF16, "gp_rows")
         nc.vector.memset(gp_rows[:].bitcast(I32), 0)
-        ident = keep.tile([P, P], F32, name="ident")
+        ident = tile([P, P], F32, "ident")
         make_identity(nc, ident[:])
-        ident_bf = keep.tile([P, P], BF16, name="ident_bf")
+        ident_bf = tile([P, P], BF16, "ident_bf")
         nc.vector.tensor_copy(out=ident_bf[:], in_=ident[:])
-        lag_factor = keep.tile([P, 4], F32, name="lag_factor")
+        lag_factor = tile([P, 4], F32, "lag_factor")
         nc.scalar.dma_start(out=lag_factor[:], in_=lag_scale.rearrange("(p t) o -> p (t o)", t=4))
+        w_sb = tile([P, 4, 2 * R], U8, "w_sb")
+        ws_sb = tile([P, 4, R], U8, "ws_sb")
+        nc.vector.memset(ws_sb[:].rearrange("p g n -> p (g n)").bitcast(I32), 0)
 
         lag_view = lag_bytes.rearrange("(p t) j -> p t j", t=4)
         lag_raw, rows = {}, {}
 
-        def load_lag(panel, parts=1):
-            raw = keep.tile([P, 4, WIDTH], U8, name="lag_raw%d" % panel, align_bytes=ALIGN)
-            step = 4 // parts
-            columns = slice(WIDTH * panel, WIDTH * (panel + 1))
-            for t in range(0, 4, step):
-                nc.sync.dma_start(out=raw[:, t : t + step, :], in_=lag_view[:, t : t + step, columns])
-            lag_raw[panel] = raw
+        def load_lag(panel, first=0, step=4):
+            if panel not in lag_raw:
+                lag_raw[panel] = tile([P, 4, WIDTH], U8, "lag_raw%d" % panel)
+            nc.sync.dma_start(
+                out=lag_raw[panel][:, first : first + step, :],
+                in_=lag_view[:, first : first + step, WIDTH * panel : WIDTH * (panel + 1)],
+            )
 
         def load_rows(g, parts=1):
             src = loads[WIDTH * g : WIDTH * (g + 1), :].rearrange("(m t) k -> m t k", t=4)
             step = 4 // parts
             for first in range(0, 4, step):
-                tile = keep.tile([P, step, K], BF16, name="rows%d_%d" % (g, first), align_bytes=ALIGN)
-                nc.sync.dma_start(out=tile[:], in_=src[:, first : first + step, :])
+                part = tile([P, step, K], BF16, "rows%d_%d" % (g, first))
+                nc.sync.dma_start(out=part[:], in_=src[:, first : first + step, :])
                 for t in range(step):
-                    rows[g, first + t] = tile[:, t, :]
+                    rows[g, first + t] = part[:, t, :]
 
-        load_lag(0, parts=2)
+        def load_gp():
+            nc.sync.dma_start(out=gp_rows[0:4, :], in_=gain.rearrange("(g x) -> g x", g=4))
+            nc.sync.dma_start(out=gp_rows[4:8, :], in_=private.rearrange("(g x) -> g x", g=4))
+
+        def load_w():
+            nc.sync.dma_start(out=w_sb[:], in_=w_words.rearrange("g p n -> p g n"))
+            ws_view = w_scales.bitcast(I32).rearrange("g q n -> q g n")
+            for quad in range(4):
+                nc.sync.dma_start(
+                    out=ws_sb[32 * quad : 32 * quad + 4, :, :].bitcast(I32),
+                    in_=ws_view[4 * quad : 4 * quad + 4, :, :],
+                )
+
+        load_lag(0, 0, 2)
+        load_lag(0, 2, 2)
         load_rows(0, parts=2)
-        nc.sync.dma_start(out=gp_rows[0:4, :], in_=gain.rearrange("(g x) -> g x", g=4))
-        nc.sync.dma_start(out=gp_rows[4:8, :], in_=private.rearrange("(g x) -> g x", g=4))
+        load_gp()
         load_rows(1)
         load_lag(1)
         load_rows(2)
         load_rows(3)
         load_lag(2)
-        w_sb = keep.tile([P, 4, 2 * R], U8, name="w_sb", align_bytes=ALIGN)
-        nc.sync.dma_start(out=w_sb[:], in_=w_words.rearrange("g p n -> p g n"))
-        ws_sb = keep.tile([P, 4, R], U8, name="ws_sb", align_bytes=ALIGN)
-        nc.vector.memset(ws_sb[:].rearrange("p g n -> p (g n)").bitcast(I32), 0)
-        ws_view = w_scales.bitcast(I32).rearrange("g q n -> q g n")
-        for quad in range(4):
-            nc.sync.dma_start(
-                out=ws_sb[32 * quad : 32 * quad + 4, :, :].bitcast(I32),
-                in_=ws_view[4 * quad : 4 * quad + 4, :, :],
-            )
+        load_w()
         load_lag(3)
 
-        gp_f = keep.tile([P, 2, 16], F32, name="gp_f")
+
+        gp_f = tile([P, 2, 16], F32, "gp_f")
         gain_f, priv_f = gp_f[:, 0, :], gp_f[:, 1, :]
-        diag = keep.tile([P, 16, P], BF16, name="diag")
 
-        def psum_bank(name):
-            return psum.tile([P, WIDTH], F32, name=name)
+        held = {}
 
-        def warm_up(width, bank_name):
-            moving = ident[:].unsqueeze(1).to_broadcast([P, width // P, P])
-            product = psum_bank(bank_name)[:, 0:width].rearrange("p (a c) -> p a c", c=P)
-            nc.tensor.matmul(out=product, lhsT=ident[:], rhs=moving, start=True, stop=True)
+        def get(key, shape, dtype):
+            if key not in held:
+                name = PLACES.get(key, key if isinstance(key, str) else "_".join([str(x) for x in key]))
+                held[key] = tile(shape, dtype, name)
+            return held[key]
 
-        def build_diag(g):
-            for i in range(4 * g, 4 * g + 4):
-                nc.scalar.activation(out=diag[:, i, :], in_=ident[:], func=ACT.Copy, scale=priv_f[:, i : i + 1])
+        def bank(key):
+            if key not in held:
+                held[key] = psum.tile([P, WIDTH], F32, name=banks[key])
+            return held[key]
 
-        def gpsimd_tile():
-            return work.tile([P, 4 * WIDTH], BF16, name="planed_grouped", bufs=1, align_bytes=ALIGN)
+        def mx_tiles(key, width):
+            if key not in held:
+                name = "_".join([str(x) for x in key])
+                held[key] = (tile([P, width], U32, name + "_codes"), tile([P, width], U8, name + "_scales"))
+            return held[key]
 
-        lag_planes, lag_grouped, lag_codes, lag_scales = {}, {}, {}, {}
-        ld_grouped, ld_codes, ld_scales, turned = {}, {}, {}, {}
+        copy = {"V": nc.vector.tensor_copy, "S": nc.scalar.copy}
 
-        def lag_widen(panel, t, on_vector=False):
-            if panel not in lag_planes:
-                lag_planes[panel] = work.tile([P, 4, WIDTH], BF16, name="lag_planes", bufs=2, align_bytes=ALIGN)
-            src, dst, factor = lag_raw[panel][:, t, :].bitcast(FP8), lag_planes[panel][:, t, :], lag_factor[:, t : t + 1]
-            if on_vector:
+        def pieces(n):
+            strip, groups = UNITS[n]
+            w = STRIPS[strip][1]
+            return [(g, w * i) for i, g in enumerate(groups)]
+
+        def window(n, g):
+            strip = UNITS[n][0]
+            first, w = STRIPS[strip]
+            return w // 4 if first // WIDTH == g else 0
+
+        def warm_up(eng, k):
+            product = bank(("warm", k))[:].rearrange("p (a c) -> p a c", c=P)
+            nc.tensor.matmul(out=product, lhsT=warm[:], rhs=warm[:].unsqueeze(1).to_broadcast([P, 4, P]), start=True, stop=True)
+
+        def spread(eng, half):
+            for t in range(2):
+                product = bank(("spread", half))[:, 256 * t : 256 * (t + 1)].rearrange("p (a c) -> p a c", c=P)
+                moving = ident_bf[:].unsqueeze(1).to_broadcast([P, 2, P])
+                nc.tensor.matmul(out=product, lhsT=gp_rows[:, 2 * half + t : WIDTH : 4], rhs=moving, start=True, stop=True)
+
+        def spread_exit(eng, half):
+            copy[eng](
+                out=gp_f[:].rearrange("p a (g t) -> p (a g) t", t=4)[:, :, 2 * half : 2 * half + 2],
+                in_=bank(("spread", half))[:].rearrange("p (t r) -> p r t", t=2)[:, 0:8],
+            )
+
+        def build_diag(eng, g, count=1):
+            diag = get(("diag", g // 2), [P, 8, P], BF16)
+            at = 4 * (g % 2)
+            if eng == "G":
+                n = 4 * count
+                nc.gpsimd.tensor_tensor(
+                    out=diag[:, at : at + n, :],
+                    in0=ident[:].unsqueeze(1).to_broadcast([P, n, P]),
+                    in1=priv_f[:, 4 * g : 4 * g + n].unsqueeze(2).to_broadcast([P, n, P]),
+                    op=ALU.mult,
+                )
+                return
+            for i in range(4 * count):
+                value = priv_f[:, 4 * g + i : 4 * g + i + 1]
+                if eng == "V":
+                    nc.vector.tensor_scalar(out=diag[:, at + i, :], in0=ident_bf[:], scalar1=value, scalar2=None, op0=ALU.mult)
+                else:
+                    nc.scalar.activation(out=diag[:, at + i, :], in_=ident[:], func=ACT.Copy, scale=value)
+
+        def widen(eng, strip, t, lo=0, hi=None):
+            first, w = STRIPS[strip]
+            hi = w if hi is None else hi
+            at = first % WIDTH
+            src = lag_raw[first // WIDTH][:, t, at + lo : at + hi].bitcast(FP8)
+            dst = get(("lag_planes", strip), [P, 4, w], BF16)
+            if strip in PAIRED:
+                dst = dst[:].rearrange("p a b -> p (a b)").rearrange("p (u j e) -> p u j e", u=2, e=2)[:, t // 2, lo:hi, t % 2]
+            else:
+                dst = dst[:, t, lo:hi]
+            factor = lag_factor[:, t : t + 1]
+            if eng == "V":
                 nc.vector.tensor_scalar(out=dst, in0=src, scalar1=factor, scalar2=None, op0=ALU.mult)
             else:
                 nc.scalar.activation(out=dst, in_=src, func=ACT.Copy, scale=factor)
 
-        def lag_interleave(panel, lo, hi, copy):
-            if panel not in lag_grouped:
-                lag_grouped[panel] = work.tile([P, WIDTH, 4], BF16, name="lag_grouped", bufs=2, align_bytes=ALIGN)
-            src = lag_planes[panel][:].rearrange("p t (m s) -> p m t s", s=4)[:, lo:hi]
-            dst = lag_grouped[panel][:].rearrange("p (s m) t -> p m t s", s=4)[:, lo:hi]
-            copy(out=dst, in_=src)
-
-        def lag_quant(panel):
-            lag_codes[panel] = work.tile([P, WIDTH], U32, name="lag_codes", bufs=3, align_bytes=ALIGN)
-            lag_scales[panel] = work.tile([P, WIDTH], U8, name="lag_scales", bufs=3, align_bytes=ALIGN)
-            nc.vector.quantize_mx(
-                out=lag_codes[panel][:].bitcast(FP8X4),
-                scales=lag_scales[panel][:],
-                in_=lag_grouped[panel][:].rearrange("p c t -> p (c t)"),
-            )
-
-        def loads_turn(g, bank_names):
-            for half in range(2):
-                turned[g, half] = psum_bank(bank_names[half])
-                view = turned[g, half][:].rearrange("p (t u m) -> p t u m", t=2, u=2)
-                for t in range(2):
-                    words = rows[g, 2 * half + t].bitcast(F32)
-                    for u in range(2):
-                        nc.tensor.transpose(view[:, t, u, :], words[:, u:256:2], ident[:])
-
-        def loads_exit(g):
-            if g == 2:
-                ld_grouped[g] = gpsimd_tile()
+        def lag_interleave(eng, strip, lo, hi):
+            w = STRIPS[strip][1]
+            src, dst = held["lag_planes", strip][:], get(("lag_grouped", strip), [P, 4 * w], BF16)[:]
+            if strip in PAIRED:
+                src = src.rearrange("p a b -> p (a b)").rearrange("p (u m s e) -> p m s u e", u=2, s=4, e=2)
+                dst = dst.rearrange("p (s m u e) -> p m s u e", s=4, u=2, e=2)
             else:
-                ld_grouped[g] = work.tile([P, 4 * WIDTH], BF16, name="ld_grouped", bufs=3, align_bytes=ALIGN)
-            ld_codes[g] = keep.tile([P, WIDTH], U32, name="ld_codes%d" % g, align_bytes=ALIGN)
-            ld_scales[g] = keep.tile([P, WIDTH], U8, name="ld_scales%d" % g, align_bytes=ALIGN)
-            for half in range(2):
-                dst = ld_grouped[g][:, 1024 * half : 1024 * half + 1024].bitcast(F32)
-                nc.scalar.copy(
-                    out=dst.rearrange("p (t m u) -> p t m u", t=2, u=2),
-                    in_=turned[g, half][:].rearrange("p (t u m) -> p t m u", t=2, u=2),
-                )
+                src = src.rearrange("p t (m s) -> p m t s", s=4)
+                dst = dst.rearrange("p (s m t) -> p m t s", s=4, t=4)
+            copy[eng](out=dst[:, lo:hi], in_=src[:, lo:hi])
 
-        def loads_quant(g, lo=0, hi=WIDTH):
-            nc.vector.quantize_mx(
-                out=ld_codes[g][:, lo:hi].bitcast(FP8X4),
-                scales=ld_scales[g][:, lo:hi],
-                in_=ld_grouped[g][:, 4 * lo : 4 * hi],
+        def quantise(codes, scales, src, lo, hi):
+            nc.vector.quantize_mx(out=codes[:, lo:hi].bitcast(FP8X4), scales=scales[:, lo:hi], in_=src[:, 4 * lo : 4 * hi])
+
+        def lag_quant(eng, strip):
+            w = STRIPS[strip][1]
+            quantise(*mx_tiles(("lag", strip), w), held["lag_grouped", strip], 0, w)
+
+        def turn(eng, g, half):
+            view = bank(("turned", g, half))[:].rearrange("p (t u m) -> p t u m", t=2, u=2)
+            for t in range(2):
+                words = rows[g, 2 * half + t].bitcast(F32)
+                for u in range(2):
+                    nc.tensor.transpose(view[:, t, u, :], words[:, u:256:2], ident[:])
+
+        def turn_exit(eng, g, half):
+            dst = get(("ld_grouped", g), [P, 4 * WIDTH], BF16)[:, 1024 * half : 1024 * half + 1024].bitcast(F32)
+            copy[eng](
+                out=dst.rearrange("p (t m u) -> p t m u", t=2, u=2),
+                in_=bank(("turned", g, half))[:].rearrange("p (t u m) -> p t m u", t=2, u=2),
             )
 
-        def group(n):
-            return (n // 4 + n) % 4
+        def ld_quant(eng, g, lo=0, hi=WIDTH):
+            quantise(*mx_tiles(("ld", g), WIDTH), held["ld_grouped", g], lo, hi)
 
-        def has_diag(n):
-            return n % 4 == 0
-
-        banks, planes, grouped, codes, scales, out_banks = {}, {}, {}, {}, {}, {}
-
-        def s_pass(bank, at, n, t, lo, hi):
-            g, panel = group(n), n // 4
+        def s_pass(dst, at, strip, g, t, lo, hi):
+            ld_codes, ld_scales = held["ld", g]
+            lag_codes, lag_scales = held["lag", strip]
             nc.tensor.matmul_mx(
-                out=bank[:, at : at + hi - lo],
-                lhsT=ld_codes[g][:, P * t : P * (t + 1)].bitcast(FP8X4),
-                lhsT_scale=ld_scales[g][:, P * t : P * (t + 1)],
-                rhs=lag_codes[panel][:, lo:hi].bitcast(FP8X4),
-                rhs_scale=lag_scales[panel][:, lo:hi],
+                out=dst[:, at : at + hi - lo],
+                lhsT=ld_codes[:, P * t : P * (t + 1)].bitcast(FP8X4),
+                lhsT_scale=ld_scales[:, P * t : P * (t + 1)],
+                rhs=lag_codes[:, lo:hi].bitcast(FP8X4),
+                rhs_scale=lag_scales[:, lo:hi],
                 start=True,
                 stop=True,
             )
 
-        def fill(job, bank_name):
-            kind, n, x = job
-            bank = psum_bank(bank_name)
-            banks[job] = bank
+        def fill(eng, kind, n, x):
+            dst = bank((kind, n, x))
+            strip = UNITS[n][0]
+            w = STRIPS[strip][1]
             if kind == "direct":
+                g, at = pieces(n)[P * x // w]
                 for t in range(4):
-                    s_pass(bank, P * t, n, t, P * x, P * (x + 1))
+                    s_pass(dst, P * t, strip, g, t, P * x - at, P * x - at + P)
             elif kind == "windows":
+                g = UNITS[n][1][0]
+                v = w // 4
                 for t in range(4):
-                    s_pass(bank, P * t, n, t, P * t, P * (t + 1))
-            elif not has_diag(n):
-                s_pass(bank, 0, n, x, 0, WIDTH)
+                    lo = v * t // P * P
+                    s_pass(dst, P * t, strip, g, t, lo, lo + P)
             else:
-                for half in range(2):
-                    lo, hi = (P * (x ^ 1), P * (x ^ 1) + P) if half == x // 2 else (256 * half, 256 * half + 256)
-                    s_pass(bank, lo, n, x, lo, hi)
+                for g, at in pieces(n):
+                    if window(n, g) == P:
+                        for half in range(2):
+                            lo, hi = (P * (x ^ 1), P * (x ^ 1) + P) if half == x // 2 else (256 * half, 256 * half + 256)
+                            s_pass(dst, lo, strip, g, x, lo, hi)
+                    else:
+                        s_pass(dst, at, strip, g, x, 0, w)
 
-        def planes_of(n):
-            if n not in planes:
-                planes[n] = work.tile([P, 4, WIDTH], BF16, name="planes", bufs=3, align_bytes=ALIGN)
-            return planes[n]
+        def direct(eng, n, x):
+            g = pieces(n)[P * x // STRIPS[UNITS[n][0]][1]][0]
+            nc.vector.tensor_tensor(
+                out=get(("grouped", n), [P, 4 * WIDTH], BF16)[:, WIDTH * x : WIDTH * (x + 1)].rearrange("p (c t) -> p c t", t=4),
+                in0=bank(("direct", n, x))[:].rearrange("p (t c) -> p c t", t=4),
+                in1=gain_f[:, 4 * g : 4 * g + 4].unsqueeze(1).to_broadcast([P, P, 4]),
+                op=ALU.mult,
+            )
 
-        def empty(job):
-            kind, n, x = job
-            g, bank = group(n), banks[job]
-            if kind == "direct":
-                if x == 0:
-                    grouped[n] = work.tile([P, 4 * WIDTH], BF16, name="direct_grouped", bufs=2, align_bytes=ALIGN)
-                nc.vector.tensor_tensor(
-                    out=grouped[n][:, WIDTH * x : WIDTH * (x + 1)].rearrange("p (c t) -> p c t", t=4),
-                    in0=bank[:].rearrange("p (t c) -> p c t", t=4),
-                    in1=gain_f[:, 4 * g : 4 * g + 4].unsqueeze(1).to_broadcast([P, P, 4]),
-                    op=ALU.mult,
+        def windows(eng, n):
+            g = UNITS[n][1][0]
+            first, w = STRIPS[UNITS[n][0]]
+            v = w // 4
+            p0 = first % WIDTH // 4
+            for t in range(4):
+                at = P * t + v * t % P
+                nc.vector.scalar_tensor_tensor(
+                    out=get(("planes", n), [P, 4, WIDTH], BF16)[:, t, v * t : v * (t + 1)],
+                    in0=bank(("windows", n, 0))[:, at : at + v],
+                    scalar=gain_f[:, 4 * g + t : 4 * g + t + 1],
+                    in1=held["diag", g // 2][:, 4 * (g % 2) + t, p0 : p0 + v],
+                    op0=ALU.mult,
+                    op1=ALU.add,
                 )
-            elif kind == "windows":
-                for t in range(4):
-                    nc.vector.scalar_tensor_tensor(
-                        out=planes_of(n)[:, t, P * t : P * (t + 1)],
-                        in0=bank[:, P * t : P * (t + 1)],
-                        scalar=gain_f[:, 4 * g + t : 4 * g + t + 1],
-                        in1=diag[:, 4 * g + t, :],
-                        op0=ALU.mult,
-                        op1=ALU.add,
-                    )
-            else:
-                spans = [(0, P * x), (P * (x + 1), WIDTH)] if has_diag(n) else [(0, WIDTH)]
-                for lo, hi in spans:
+
+        def plane(eng, n, x):
+            w = STRIPS[UNITS[n][0]][1]
+            for g, at in pieces(n):
+                v = window(n, g)
+                for lo, hi in [(0, v * x), (v * x + v, w)] if v else [(0, w)]:
                     if hi > lo:
                         nc.scalar.activation(
-                            out=planes_of(n)[:, x, lo:hi],
-                            in_=bank[:, lo:hi],
+                            out=get(("planes", n), [P, 4, WIDTH], BF16)[:, x, at + lo : at + hi],
+                            in_=bank(("plane", n, x))[:, at + lo : at + hi],
                             func=ACT.Copy,
                             scale=gain_f[:, 4 * g + x : 4 * g + x + 1],
                         )
 
-        def interleave_gpsimd(n, hi):
-            grouped[n] = gpsimd_tile()
-            nc.gpsimd.tensor_scalar(
-                out=grouped[n][:, 0 : 4 * hi].rearrange("p (c t) -> p c t", t=4),
-                in0=planes[n][:, :, 0:hi].rearrange("p t c -> p c t"),
-                scalar1=1.0,
-                scalar2=0.0,
-                op0=ALU.mult,
-                op1=ALU.add,
-            )
+        def interleave(eng, n, lo, hi):
+            dst = get(("grouped", n), [P, 4 * WIDTH], BF16)[:, 4 * lo : 4 * hi]
+            src = held["planes", n][:, :, lo:hi]
+            if eng == "G":
+                nc.gpsimd.tensor_scalar(
+                    out=dst.rearrange("p (c t) -> p c t", t=4),
+                    in0=src.rearrange("p t c -> p c t"),
+                    scalar1=1.0,
+                    scalar2=0.0,
+                    op0=ALU.mult,
+                    op1=ALU.add,
+                )
+            else:
+                copy[eng](
+                    out=dst.rearrange("p (c i t) -> p c t i", i=4, t=4), in_=src.rearrange("p t (c i) -> p c t i", i=4)
+                )
 
-        def interleave_rest(n, lo, copy):
-            copy(
-                out=grouped[n][:, 4 * lo :].rearrange("p (c i t) -> p c t i", i=4, t=4),
-                in_=planes[n][:, :, lo:].rearrange("p t (c i) -> p c t i", i=4),
-            )
-
-        def quant(n):
-            codes[n] = work.tile([P, WIDTH], U32, name="codes", bufs=4, align_bytes=ALIGN)
-            scales[n] = work.tile([P, WIDTH], U8, name="scales", bufs=4, align_bytes=ALIGN)
-            nc.vector.quantize_mx(out=codes[n][:].bitcast(FP8X4), scales=scales[n][:], in_=grouped[n][:])
+        def quant(eng, n, lo=0, hi=WIDTH):
+            quantise(*mx_tiles(("c", n), WIDTH), held["grouped", n], lo, hi)
 
         added = {}
 
-        def out_pass(n, r):
-            panel, g = n // 4, group(n)
-            count = added.get((panel, r), 0)
-            added[panel, r] = count + 1
-            if count == 0:
-                out_banks[panel, r] = psum_bank("out_bank%d" % r)
-            nc.tensor.matmul_mx(
-                out=out_banks[panel, r][:],
-                lhsT=w_sb[:, g, 2 * P * r : 2 * P * (r + 1)].bitcast(FP4X4),
-                lhsT_scale=ws_sb[:, g, P * r : P * (r + 1)],
-                rhs=codes[n][:].bitcast(FP8X4),
-                rhs_scale=scales[n][:],
-                start=(count == 0),
-                stop=(count == 3),
-            )
+        def out_pass(eng, n, r, lo=0, hi=WIDTH):
+            strip = UNITS[n][0]
+            w = STRIPS[strip][1]
+            codes, scales = held["c", n]
+            for g, at in pieces(n):
+                a, b = max(lo, at), min(hi, at + w)
+                if b > a:
+                    done_cols = added.get((strip, r), 0)
+                    added[strip, r] = done_cols + b - a
+                    nc.tensor.matmul_mx(
+                        out=bank(("out", strip, r))[:, a - at : b - at],
+                        lhsT=w_sb[:, g, 2 * P * r : 2 * P * (r + 1)].bitcast(FP4X4),
+                        lhsT_scale=ws_sb[:, g, P * r : P * (r + 1)],
+                        rhs=codes[:, a:b].bitcast(FP8X4),
+                        rhs_scale=scales[:, a:b],
+                        start=(done_cols == 0),
+                        stop=(done_cols + b - a == 4 * w),
+                    )
 
-        def out_exit(panel, r, copy=nc.scalar.copy, parts=1):
-            staged = work.tile([P, WIDTH], F32, name="staged", bufs=6)
-            dst = staged[:].rearrange("p (m s) -> p m s", s=4)
-            src = out_banks[panel, r][:].rearrange("p (s m) -> p m s", s=4)
-            step = P // parts
-            for m in range(0, P, step):
-                copy(out=dst[:, m : m + step], in_=src[:, m : m + step])
-                j = WIDTH * panel + 4 * m
-                nc.sync.dma_start(out=out[P * r : P * (r + 1), j : j + 4 * step], in_=staged[:, 4 * m : 4 * (m + step)])
+        def out_exit(eng, strip, r, lo=0, hi=None):
+            w = STRIPS[strip][1]
+            hi = w if hi is None else hi
+            dst = get(("staged", strip, r), [P, w], F32)[:].rearrange("p (m s) -> p m s", s=4)
+            src = bank(("out", strip, r))[:, 0:w].rearrange("p (s m) -> p m s", s=4)
+            copy[eng](out=dst[:, lo // 4 : hi // 4], in_=src[:, lo // 4 : hi // 4])
 
-        def run(calls):
-            for call in calls:
-                if call:
-                    call[0](*call[1:])
+        def store(eng, strip, r, lo=0, hi=None):
+            first, w = STRIPS[strip]
+            hi = w if hi is None else hi
+            queue = nc.sync if eng == "D" else nc.scalar
+            queue.dma_start(out=out[P * r : P * (r + 1), first + lo : first + hi], in_=held["staged", strip, r][:, lo:hi])
 
-        period_jobs = {1: [("plane", 2, t) for t in range(4)]}
-        for period in range(2, PERIODS + 1):
-            direct = [("direct", 2 * period - 1, q) for q in range(4)]
-            plane = [("plane", 2 * period, t) for t in range(4)] if period < PERIODS else []
-            windows = [("windows", 2 * period, 0)] if period < PERIODS and has_diag(2 * period) else []
-            period_jobs[period] = direct[:3] + plane[:1] + direct[3:] + windows + plane[1:]
-        ring_jobs = [job for period in range(1, PERIODS + 1) for job in period_jobs[period]]
+        def uses(task):
+            call, a = task[0], task[1:]
+            if call is warm_up:
+                return [], [("warm", a[0])]
+            if call is spread:
+                return [], [("spread", a[0])]
+            if call is spread_exit:
+                return [("spread", a[0])], ["gp"]
+            if call is build_diag:
+                return ["gp"], [("diag", a[0] // 2), ("diag_of", a[0])] + [("diag_of", a[0] + 1)] * (len(a) > 1 and a[1] == 2)
+            if call is widen:
+                return [], [("lag_planes", a[0])]
+            if call is lag_interleave:
+                return [("lag_planes", a[0])], [("lag_grouped", a[0])]
+            if call is lag_quant:
+                return [("lag_grouped", a[0])], [("lag", a[0])]
+            if call is turn:
+                return [], [("turned", a[0], a[1])]
+            if call is turn_exit:
+                return [("turned", a[0], a[1])], [("ld_grouped", a[0])]
+            if call is ld_quant:
+                return [("ld_grouped", a[0])], [("ld", a[0])]
+            if call is fill:
+                return [("lag", UNITS[a[1]][0])] + [("ld", g) for g in UNITS[a[1]][1]], [a]
+            if call is direct:
+                return [("direct", a[0], a[1]), "gp"], [("grouped", a[0])]
+            if call is windows:
+                return [("windows", a[0], 0), ("diag_of", UNITS[a[0]][1][0])], [("planes", a[0])]
+            if call is plane:
+                return [("plane", a[0], a[1]), "gp"], [("planes", a[0])]
+            if call is interleave:
+                return [("planes", a[0])], [("grouped", a[0])]
+            if call is quant:
+                return [("grouped", a[0])], [("c",) + tuple(a)]
+            if call is out_pass:
+                return [key for key in quant_keys if key[1] == a[0] and (len(key) == 2 or len(a) == 2 or key[2] == a[2])], [("out", UNITS[a[0]][0], a[1])]
+            if call is out_exit:
+                return [("out", a[0], a[1])], [("staged", a[0], a[1]), ("staged_part",) + tuple(a)]
+            return [("staged_part",) + tuple(a)], []
 
-        def ring_fill(i):
-            if i < len(ring_jobs):
-                fill(ring_jobs[i], "ring%d" % ((i + 1) % RING))
+        T, V, S, G, D = [], [], [], [], []
+        programme = {"T": T, "S": S, "V": V, "G": G, "D": D}
+        banks = {}
 
-        def refill(job):
-            ring_fill(ring_jobs.index(job) + RING)
+        def on_bank(name, *task):
+            T.append(task)
+            key = uses(task)[1][0]
+            if key not in banks:
+                banks[key] = name
 
-        plane0 = [("plane", 0, t) for t in range(4)]
-        windows0 = ("windows", 0, 0)
-        direct1 = [("direct", 1, q) for q in range(4)]
-        warm_up(WIDTH, "ring3")
-        loads_turn(0, ("out_bank0", "out_bank1"))
-        gp_banks = [psum_bank("out_bank2"), psum_bank("ring2")]
-        for t in range(4):
-            product = gp_banks[t // 2][:, 256 * (t % 2) : 256 * (t % 2 + 1)].rearrange("p (a c) -> p a c", c=P)
-            moving = ident_bf[:].unsqueeze(1).to_broadcast([P, 2, P])
-            nc.tensor.matmul(out=product, lhsT=gp_rows[:, t:WIDTH:4], rhs=moving, start=True, stop=True)
-        loads_turn(1, ("out_bank3", "ring3"))
-        for t in range(4):
-            lag_widen(0, t, on_vector=(t != 1))
-        lag_interleave(0, 0, P, nc.vector.tensor_copy)
-        loads_exit(0)
-        for half in range(2):
-            nc.scalar.copy(
-                out=gp_f[:].rearrange("p a (g t) -> p (a g) t", t=4)[:, :, 2 * half : 2 * half + 2],
-                in_=gp_banks[half][:].rearrange("p (t r) -> p r t", t=2)[:, 0:8],
-            )
-        lag_quant(0)
-        loads_quant(0, 0, WIDTH // 2)
-        loads_quant(0, WIDTH // 2, WIDTH)
-        fill(plane0[0], "out_bank0")
-        fill(plane0[1], "ring0")
-        fill(windows0, "out_bank1")
-        fill(plane0[2], "ring1")
-        fill(plane0[3], "ring2")
-        build_diag(0)
-        loads_exit(1)
-        loads_turn(2, ("out_bank2", "out_bank3"))
-        for t in range(4):
-            lag_widen(1, t, on_vector=True)
-        empty(plane0[0])
-        empty(plane0[1])
-        loads_quant(1)
-        empty(windows0)
-        lag_interleave(1, 0, P, nc.vector.tensor_copy)
-        for job, name in zip(direct1, ("out_bank0", "out_bank1", "ring3", "ring0")):
-            fill(job, name)
-        loads_exit(2)
-        loads_turn(3, ("out_bank2", "out_bank3"))
-        loads_quant(2)
-        empty(plane0[2])
-        empty(plane0[3])
-        ring_fill(0)
-        ring_fill(1)
+        quant_keys = []
 
-        interleave_gpsimd(0, GPSIMD_LATE_START)
-        interleave_rest(0, GPSIMD_LATE_START, nc.scalar.copy)
-        loads_exit(3)
-        for job in direct1:
-            empty(job)
-        ring_fill(2)
-        ring_fill(3)
-        warm_up(WIDTH // 2, "out_bank0")
-        loads_quant(3)
-        quant(1)
-        quant(0)
-        lag_quant(1)
-        for i, job in enumerate(period_jobs[1]):
-            empty(job)
-            if i == 2:
-                out_pass(1, 0)
-            refill(job)
-        lag_widen(2, 0)
-        lag_widen(2, 1)
+        def has_windows(n):
+            return n < 16 and n % 2 == 0 and window(n, UNITS[n][1][0]) > 0
 
-        def scalar_extras(period):
-            panel = (period + 3) // 2
-            widen = [(lag_widen, panel, t) for t in range(4 if panel == 2 else 3)] if panel < PANELS else []
-            exits = [(out_exit, (period - 3) // 2, r) for r in range(4)] if period >= 3 else []
-            if period == PERIODS - 1:
-                return [], exits[:1]
-            if period % 2 == 1:
-                return exits[:2], exits[2:3] + widen[:2]
-            half = [(lag_interleave, panel, 0, P // 2, nc.scalar.copy)] if panel < PANELS else []
-            return [(build_diag, period // 2)] + exits[3:] + widen[2:], half
+        jobs = {1: [("plane", 2, t) for t in range(4)]}
+        if has_windows(2):
+            jobs[1] = jobs[1][:1] + [("windows", 2, 0)] + jobs[1][1:]
+        for k in range(2, 9):
+            d = [("direct", 2 * k - 1, q) for q in range(4)]
+            x = [("plane", 2 * k, t) for t in range(4)] if k < 8 else []
+            w = [("windows", 2 * k, 0)] if has_windows(2 * k) else []
+            jobs[k] = d[:3] + x[:1] + d[3:] + w + x[1:]
+        ring_jobs = [job for k in range(1, 9) for job in jobs[k]]
+        filled = [0]
 
-        def vector_port_work(period):
-            panel = period // 2 + 1
-            if period in (3, 5):
-                interleave_rest(2 * period - 2, GPSIMD_ODD, nc.vector.tensor_copy)
-            if period == 4:
-                lag_widen(panel, 3, on_vector=True)
-            quant(2 * period - 1)
-            quant(2 * period - 2)
-            if panel < PANELS and period % 2 == 1:
-                lag_quant(panel)
-            if panel < PANELS and period % 2 == 0:
-                lag_interleave(panel, P // 2, P, nc.vector.tensor_copy)
+        def fills(count):
+            for step in range(count):
+                if filled[0] < len(ring_jobs):
+                    on_bank(ring_names[filled[0] % 4], fill, *ring_jobs[filled[0]])
+                    filled[0] = filled[0] + 1
 
-        def passes_due(period):
-            planed_unit, direct_unit = 2 * period - 4, 2 * period - 3
-            return [(out_pass, planed_unit, 0)] + [
-                (out_pass, n, r) for r in range(1, 4) for n in (direct_unit, planed_unit)
-            ]
+        def out_name(n, r):
+            return ("ring%d" if UNITS[n][0] == 4 else "out%d") % r
 
-        for period in range(2, PERIODS):
-            planed_unit = 2 * period - 2
-            mine = period_jobs[period]
-            due = passes_due(period)
-            if period == PERIODS - 1:
-                interleave_gpsimd(planed_unit, GPSIMD_LATE_START)
-                interleave_rest(planed_unit, GPSIMD_LATE_START, nc.scalar.copy)
-                passes = [None] * FILLS_FIRST + due
+        def run_pass(task):
+            if task:
+                on_bank(out_name(task[1], task[2]), *task)
+        ring_names = ["ring1", "ring2", "ring3", "ring0"]
+        for k in range(NW):
+            on_bank("ring3", warm_up, k)
+        on_bank("out0", turn, 0, 0)
+        on_bank("out1", turn, 0, 1)
+        on_bank("out2", spread, 0)
+        on_bank("ring2", spread, 1)
+        on_bank("out3", turn, 1, 0)
+        on_bank("ring3", turn, 1, 1)
+        on_bank("out1", fill, "windows", 0, 0)
+        on_bank("out0", fill, "plane", 0, 0)
+        on_bank("ring0", fill, "plane", 0, 1)
+        on_bank("out2", turn, 2, 0)
+        on_bank("out3", turn, 2, 1)
+        on_bank("ring1", fill, "plane", 0, 2)
+        on_bank("ring2", fill, "plane", 0, 3)
+        for q, name in enumerate(("out0", "out1", "ring3", "ring0")):
+            on_bank(name, fill, "direct", 1, q)
+        on_bank("out2", turn, 3, 0)
+        on_bank("out3", turn, 3, 1)
+        fills(4)
+        on_bank("out0", warm_up, NW)
+        fills(2)
+        run_pass((out_pass, 1, 0))
+        fills(1)
+        run_pass((out_pass, 1, 1))
+        fills(1)
+        V.extend([(widen, 0, 0), (widen, 0, 2, 0, 256), (widen, 0, 3, 0, 256), (widen, 0, 2, 256, 512), (lag_interleave, 0, 0, 64), (lag_interleave, 0, 64, 112), (lag_quant, 0), (ld_quant, 0, 0, 256), (ld_quant, 0, 256, 512)])
+        V.extend([(widen, 1, t) for t in range(4)] + [(windows, 0), (ld_quant, 1), (lag_interleave, 1, 0, 128), (ld_quant, 2)])
+        V.extend([(direct, 1, q) for q in range(4)] + [(ld_quant, 3), (quant, 1), (lag_quant, 1), (build_diag, 1), (quant, 0)])
+        S.extend([(widen, 0, 1), (widen, 0, 3, 256, 512), (lag_interleave, 0, 112, 128), (turn_exit, 0, 0), (turn_exit, 0, 1), (spread_exit, 0), (spread_exit, 1), (build_diag, 0)])
+        S.extend([(turn_exit, 1, 0), (turn_exit, 1, 1), (plane, 0, 0), (plane, 0, 1), (turn_exit, 2, 0), (turn_exit, 2, 1), (plane, 0, 2), (plane, 0, 3)])
+        S.extend([(turn_exit, 3, 0), (turn_exit, 3, 1), (interleave, 0, G_LATE, WIDTH)] + [(plane, 2, t) for t in range(4)] + [(widen, 2, 0), (widen, 2, 1)])
+        G.append((interleave, 0, 0, G_LATE))
+        PLACES = {("ld_grouped", 2): "gpsimd_out"}
+        shared = [[("ld_grouped", 2)] + [("grouped", n) for n in range(0, 16, 2)]]
+        extra = {
+            2: ([(widen, 2, 2), (widen, 2, 3)], [(lag_interleave, 2, 0, 64)]),
+            3: ([(out_exit, 0, 0), (out_exit, 0, 1)], [(out_exit, 0, 2), (widen, 3, 0), (widen, 3, 1)]),
+            4: ([(out_exit, 0, 3), (widen, 3, 2), (widen, 3, 3)], [(lag_interleave, 3, 0, 64)]),
+            5: ([(out_exit, 1, 0), (out_exit, 1, 1)], [(out_exit, 1, 2)]),
+            6: ([(build_diag, 3), (out_exit, 1, 3)], []),
+            7: ([], [(out_exit, 2, 0)]),
+        }
+        slot = {}
+        port_first = {3: [(build_diag, 2)], 4: []}
+        port_last = {2: [(lag_interleave, 2, 64, 128)], 3: [(lag_quant, 2)], 4: [(lag_interleave, 3, 64, 128)], 5: [(lag_quant, 3)]}
+        share = {2: WIDTH, 3: G_ODD, 4: WIDTH, 5: G_ODD, 6: WIDTH, 7: G_LATE, 8: G_LAST}
+        ahead = {2: 2, 3: 2, 4: 2, 5: 2}
+        for k in range(2, 8):
+            a, b = 2 * k - 4, 2 * k - 3
+            due = [(out_pass, n, r) for r in range(4) for n in (b, a) if (out_pass, n, r) not in T]
+            if k == 7:
+                due = [None] * 2 + due
             else:
-                interleave_gpsimd(planed_unit, GPSIMD_ODD if period % 2 else WIDTH)
-                passes = due + [None] * (len(mine) - len(due)) + [(out_pass, 2 * period - 1, 0)]
-            early, late = scalar_extras(period)
-            last_on_vector = max([i for i, job in enumerate(mine) if job[0] != "plane"])
-            run(passes[:1])
-            for i, job in enumerate(mine):
-                run(passes[i + 1 : i + 2])
-                empty(job)
-                if i == 3:
-                    run(early)
-                if i == last_on_vector:
-                    vector_port_work(period)
-                refill(job)
-            run(late)
-
-        interleave_gpsimd(14, GPSIMD_LAST)
-        out_exit(PANELS - 2, 1)
-        interleave_rest(14, GPSIMD_LAST, nc.scalar.copy)
-        out_exit(PANELS - 2, 2)
-        out_exit(PANELS - 2, 3)
+                due = due + [None] * (len(jobs[k]) + 1 - len(due) - ahead.get(k, 1)) + [(out_pass, 2 * k - 1, r) for r in range(ahead.get(k, 1))]
+            run_pass(due[0])
+            for i in range(len(jobs[k])):
+                last = i + 1 == len(jobs[k])
+                for task in due[i + 1 :] if last else due[i + 1 : i + 2]:
+                    run_pass(task)
+                fills(1)
+            if (direct, 2 * k - 2, 0) not in V:
+                G.append((interleave, 2 * k - 2, 0, share[k]))
+            rest = [(interleave, 2 * k - 2, share[k], WIDTH)] if share[k] < WIDTH else []
+            V.extend([(direct, 2 * k - 1, q) for q in range(4)])
+            if has_windows(2 * k):
+                V.append((windows, 2 * k))
+            V.extend(slot.get(k, []))
+            if k < 7:
+                V.extend(rest)
+            else:
+                S.extend(rest)
+            V.extend(port_first.get(k, []) + [(quant, 2 * k - 1), (quant, 2 * k - 2)] + port_last.get(k, []))
+            S.extend([(plane, 2 * k, 0)] + extra[k][0] + [(plane, 2 * k, t) for t in range(1, 4)] + extra[k][1])
+        G.append((interleave, 14, 0, G_LAST))
+        S.extend([(out_exit, 2, 1), (interleave, 14, G_LAST, WIDTH), (out_exit, 2, 2), (out_exit, 2, 3)])
+        V.extend([(direct, 15, q) for q in range(4)] + [(quant, 14), (quant, 15)])
         for r in range(3):
-            out_pass(13, r)
-            out_pass(12, r)
-        for job in period_jobs[PERIODS]:
-            empty(job)
-        quant(14)
-        quant(15)
-        out_pass(14, 0)
-        out_pass(14, 1)
+            run_pass((out_pass, 13, r))
+            run_pass((out_pass, 12, r))
+        run_pass((out_pass, 14, 0))
+        run_pass((out_pass, 14, 1))
         for r, units in enumerate(((15,), (15,), (14, 15), (13, 12, 14, 15))):
             for n in units:
-                out_pass(n, r)
-            if r in (0, 3):
-                out_exit(PANELS - 1, r, parts=2)
+                run_pass((out_pass, n, r))
+        S.extend([(out_exit, 3, r, lo, lo + 256) for r in (0, 3) for lo in (0, 256)])
+        D.extend([(store, k, r) for k in range(3) for r in range(4)])
+        D.extend([(store, 3, 0, 0, 256), (store, 3, 0, 256, 512), (store, 3, 1), (store, 3, 2), (store, 3, 3, 0, 256), (store, 3, 3, 256, 512)])
+        V.extend([(out_exit, 3, 1), (out_exit, 3, 2)])
+        for n in range(16):
+            if n % 2 or (direct, n, 0) in V:
+                PLACES["grouped", n] = "direct_out%d" % ((n + 1) // 2 % 2)
             else:
-                out_exit(PANELS - 1, r, copy=nc.vector.tensor_copy)
+                PLACES["planes", n] = "planes%d" % (n // 2 % 3)
+                PLACES["grouped", n] = "gpsimd_out"
+        for name in ("direct_out0", "direct_out1", "planes0", "planes1", "planes2"):
+            shared.append([key for key in PLACES if PLACES[key] == name])
+        for name in sorted(set(banks.values())):
+            order = []
+            for task in T:
+                key = uses(task)[1][0]
+                if banks[key] == name and key not in order:
+                    order.append(key)
+            shared.append(order)
+
+
+        def apart(reader, writer):
+            return reader[0] is quant and writer[0] is direct and len(reader) == 4 and not reader[2] <= P * writer[2] < reader[3]
+
+        quant_keys = [("c",) + tuple(task[1:]) for task in programme["V"] if task[0] is quant]
+        readers, writers = {}, {}
+        for eng in programme:
+            for task in programme[eng]:
+                reads, writes = uses(task)
+                for key in reads:
+                    readers.setdefault(key, []).append((eng, task))
+                for key in writes:
+                    writers.setdefault(key, []).append((eng, task))
+        before = {}
+        for order in shared:
+            for first_key, next_key in zip(order, order[1:]):
+                before[next_key] = first_key
+        written = set()
+        position = dict([(eng, 0) for eng in programme])
+        while any([position[eng] < len(programme[eng]) for eng in programme]):
+            moved = False
+            for eng in programme:
+                while position[eng] < len(programme[eng]):
+                    task = programme[eng][position[eng]]
+                    reads, writes = uses(task)
+                    needs = [x for key in reads for x in writers[key] if not apart(task, x[1])]
+                    for key in writes:
+                        if key in before:
+                            needs = needs + writers[before[key]] + readers.get(before[key], [])
+                    if not all([x in written for x in needs]):
+                        break
+                    task[0](eng, *task[1:])
+                    written.add((eng, task))
+                    position[eng] = position[eng] + 1
+                    moved = True
+            assert moved

@@ -42,8 +42,6 @@ def tile_spike_covariance_readout_s13_kernel(
         def tile(shape, dtype, name):
             return sb.tile(shape, dtype, name=name, align_bytes=ALIGN)
 
-        warm = tile([P, P], BF16, "warm")
-        nc.vector.memset(warm[:].bitcast(I32), 0)
         gp_rows = tile([P, WIDTH], BF16, "gp_rows")
         nc.vector.memset(gp_rows[:].bitcast(I32), 0)
         ident = tile([P, P], F32, "ident")
@@ -136,9 +134,10 @@ def tile_spike_covariance_readout_s13_kernel(
             first, w = STRIPS[strip]
             return w // 4 if first // WIDTH == g else 0
 
-        def warm_up(eng, k):
-            product = bank(("warm", k))[:].rearrange("p (a c) -> p a c", c=P)
-            nc.tensor.matmul(out=product, lhsT=warm[:], rhs=warm[:].unsqueeze(1).to_broadcast([P, 4, P]), start=True, stop=True)
+        def warm_up(eng, width):
+            product = bank(("warm", width))[:, 0:width].rearrange("p (a c) -> p a c", c=P)
+            moving = ident[:].unsqueeze(1).to_broadcast([P, width // P, P])
+            nc.tensor.matmul(out=product, lhsT=ident[:], rhs=moving, start=True, stop=True)
 
         def spread(eng, half):
             for t in range(2):
@@ -429,8 +428,7 @@ def tile_spike_covariance_readout_s13_kernel(
             if task:
                 on_bank(out_name(task[1], task[2]), *task)
         ring_names = ["ring1", "ring2", "ring3", "ring0"]
-        for k in range(NW):
-            on_bank("ring3", warm_up, k)
+        on_bank("ring3", warm_up, WIDTH)
         on_bank("out0", turn, 0, 0)
         on_bank("out1", turn, 0, 1)
         on_bank("out2", spread, 0)
@@ -449,7 +447,7 @@ def tile_spike_covariance_readout_s13_kernel(
         on_bank("out2", turn, 3, 0)
         on_bank("out3", turn, 3, 1)
         fills(4)
-        on_bank("out0", warm_up, NW)
+        on_bank("out0", warm_up, WIDTH // 2)
         fills(2)
         run_pass((out_pass, 1, 0))
         fills(1)

@@ -28,6 +28,13 @@ G_LATE = 352
 G_LAST = 320
 NW = 4
 PAIRED = ()
+HALVED = (3,)
+SPLIT = ((3, 3),)
+LAST_BANKS = {("out", 3, 3, 1): "ring0"}
+S_FIRST = (0,)
+W_AT = 3
+PATTERN = {2: "PFPFPFPFPFPFFFPPF", 3: "PFPFPFPFPPFFPFPF", 4: "PFPFPFPFPFPFFPFPF", 5: "PFPFPFPFPPFFPFPF", 6: "PFPFPFFPPFPFFPF", 7: "FPFPFPFPFPFPFPF"}
+OWN_BANK = (0, 4, 8)
 
 
 def tile_spike_covariance_readout_s13_kernel(
@@ -113,7 +120,8 @@ def tile_spike_covariance_readout_s13_kernel(
 
         def bank(key):
             if key not in held:
-                held[key] = psum.tile([P, WIDTH], F32, name=banks[key])
+                shape, dtype = ([P, 2 * WIDTH], BF16) if key[0] == "mixed" else ([P, WIDTH], F32)
+                held[key] = psum.tile(shape, dtype, name=banks[key])
             return held[key]
 
         def mx_tiles(key, width):
@@ -129,10 +137,11 @@ def tile_spike_covariance_readout_s13_kernel(
             w = STRIPS[strip][1]
             return [(g, w * i) for i, g in enumerate(groups)]
 
-        def window(n, g):
-            strip = UNITS[n][0]
-            first, w = STRIPS[strip]
-            return w // 4 if first // WIDTH == g else 0
+        def has_diag(n):
+            return UNITS[n][0] == UNITS[n][1][0]
+
+        def blocks(strip):
+            return 2 if strip in HALVED else 1
 
         def warm_up(eng, width):
             product = bank(("warm", width))[:, 0:width].rearrange("p (a c) -> p a c", c=P)
@@ -187,15 +196,28 @@ def tile_spike_covariance_readout_s13_kernel(
                 nc.scalar.activation(out=dst, in_=src, func=ACT.Copy, scale=factor)
 
         def lag_interleave(eng, strip, lo, hi):
-            w = STRIPS[strip][1]
-            src, dst = held["lag_planes", strip][:], get(("lag_grouped", strip), [P, 4 * w], BF16)[:]
-            if strip in PAIRED:
-                src = src.rearrange("p a b -> p (a b)").rearrange("p (u m s e) -> p m s u e", u=2, s=4, e=2)
-                dst = dst.rearrange("p (s m u e) -> p m s u e", s=4, u=2, e=2)
-            else:
-                src = src.rearrange("p t (m s) -> p m t s", s=4)
-                dst = dst.rearrange("p (s m t) -> p m t s", s=4, t=4)
-            copy[eng](out=dst[:, lo:hi], in_=src[:, lo:hi])
+            h = blocks(strip)
+            src = held["lag_planes", strip][:].rearrange("p t (m s) -> p m t s", s=4)[:, lo:hi]
+            dst = get(("lag_grouped", strip), [P, 4 * WIDTH], BF16)[:].rearrange("p (h s m t) -> p h m t s", h=h, s=4, t=4)
+            size = P // h
+            assert lo // size == (hi - 1) // size
+            copy[eng](out=dst[:, lo // size, lo % size : (hi - 1) % size + 1], in_=src)
+
+        def mix(eng, strip, half):
+            for x in range(2):
+                lo = 256 * half + P * x
+                nc.tensor.matmul(
+                    out=bank(("mixed", strip, half))[:, WIDTH * x : WIDTH * (x + 1)].rearrange("p (c t) -> p c t", t=4),
+                    lhsT=ident_bf[:],
+                    rhs=held["lag_planes", strip][:, :, lo : lo + P].rearrange("p t c -> p c t"),
+                    start=True,
+                    stop=True,
+                )
+
+        def mix_exit(eng, strip, half):
+            dst = get(("lag_grouped", strip), [P, 4 * WIDTH], BF16)[:].rearrange("p (s m t) -> p m s t", s=4, t=4)
+            src = bank(("mixed", strip, half))[:].rearrange("p (m s t) -> p m s t", s=4, t=4)
+            copy[eng](out=dst[:, 64 * half : 64 * half + 64], in_=src)
 
         def quantise(codes, scales, src, lo, hi):
             nc.vector.quantize_mx(out=codes[:, lo:hi].bitcast(FP8X4), scales=scales[:, lo:hi], in_=src[:, 4 * lo : 4 * hi])
@@ -243,19 +265,14 @@ def tile_spike_covariance_readout_s13_kernel(
                 for t in range(4):
                     s_pass(dst, P * t, strip, g, t, P * x - at, P * x - at + P)
             elif kind == "windows":
-                g = UNITS[n][1][0]
-                v = w // 4
                 for t in range(4):
-                    lo = v * t // P * P
-                    s_pass(dst, P * t, strip, g, t, lo, lo + P)
+                    s_pass(dst, P * t, strip, UNITS[n][1][0], t, P * t, P * (t + 1))
+            elif n in OWN_BANK:
+                for half in range(2):
+                    lo, hi = (P * (x ^ 1), P * (x ^ 1) + P) if half == x // 2 else (256 * half, 256 * half + 256)
+                    s_pass(dst, lo, strip, UNITS[n][1][0], x, lo, hi)
             else:
-                for g, at in pieces(n):
-                    if window(n, g) == P:
-                        for half in range(2):
-                            lo, hi = (P * (x ^ 1), P * (x ^ 1) + P) if half == x // 2 else (256 * half, 256 * half + 256)
-                            s_pass(dst, lo, strip, g, x, lo, hi)
-                    else:
-                        s_pass(dst, at, strip, g, x, 0, w)
+                s_pass(dst, 0, strip, UNITS[n][1][0], x, 0, w)
 
         def direct(eng, n, x):
             g = pieces(n)[P * x // STRIPS[UNITS[n][0]][1]][0]
@@ -266,34 +283,28 @@ def tile_spike_covariance_readout_s13_kernel(
                 op=ALU.mult,
             )
 
-        def windows(eng, n):
-            g = UNITS[n][1][0]
-            first, w = STRIPS[UNITS[n][0]]
-            v = w // 4
-            p0 = first % WIDTH // 4
-            for t in range(4):
-                at = P * t + v * t % P
-                nc.vector.scalar_tensor_tensor(
-                    out=get(("planes", n), [P, 4, WIDTH], BF16)[:, t, v * t : v * (t + 1)],
-                    in0=bank(("windows", n, 0))[:, at : at + v],
-                    scalar=gain_f[:, 4 * g + t : 4 * g + t + 1],
-                    in1=held["diag", g // 2][:, 4 * (g % 2) + t, p0 : p0 + v],
-                    op0=ALU.mult,
-                    op1=ALU.add,
-                )
+        def window(eng, n, t):
+            g, h = UNITS[n][1][0], blocks(UNITS[n][0])
+            v = P // h
+            nc.vector.scalar_tensor_tensor(
+                out=get(("planes", n), [P, 4, WIDTH], BF16)[:, t, :].rearrange("p (h c) -> p h c", h=h)[:, :, v * t : v * (t + 1)],
+                in0=bank(("windows", n, 0) if n in OWN_BANK else ("plane", n, t))[:].rearrange("p (h c) -> p h c", h=h)[:, :, v * t : v * (t + 1)],
+                scalar=gain_f[:, 4 * g + t : 4 * g + t + 1],
+                in1=held["diag", g // 2][:, 4 * (g % 2) + t, :].rearrange("p (h c) -> p h c", h=h),
+                op0=ALU.mult,
+                op1=ALU.add,
+            )
 
         def plane(eng, n, x):
-            w = STRIPS[UNITS[n][0]][1]
-            for g, at in pieces(n):
-                v = window(n, g)
-                for lo, hi in [(0, v * x), (v * x + v, w)] if v else [(0, w)]:
-                    if hi > lo:
-                        nc.scalar.activation(
-                            out=get(("planes", n), [P, 4, WIDTH], BF16)[:, x, at + lo : at + hi],
-                            in_=bank(("plane", n, x))[:, at + lo : at + hi],
-                            func=ACT.Copy,
-                            scale=gain_f[:, 4 * g + x : 4 * g + x + 1],
-                        )
+            g, h = UNITS[n][1][0], blocks(UNITS[n][0])
+            v, w = P // h, WIDTH // h
+            dst = get(("planes", n), [P, 4, WIDTH], BF16)[:, x, :].rearrange("p (h c) -> p h c", h=h)
+            src = bank(("plane", n, x))[:].rearrange("p (h c) -> p h c", h=h)
+            for lo, hi in [(0, v * x), (v * x + v, w)] if has_diag(n) else [(0, w)]:
+                if hi > lo:
+                    nc.scalar.activation(
+                        out=dst[:, :, lo:hi], in_=src[:, :, lo:hi], func=ACT.Copy, scale=gain_f[:, 4 * g + x : 4 * g + x + 1]
+                    )
 
         def interleave(eng, n, lo, hi):
             dst = get(("grouped", n), [P, 4 * WIDTH], BF16)[:, 4 * lo : 4 * hi]
@@ -317,31 +328,38 @@ def tile_spike_covariance_readout_s13_kernel(
 
         added = {}
 
-        def out_pass(eng, n, r, lo=0, hi=WIDTH):
-            strip = UNITS[n][0]
-            w = STRIPS[strip][1]
-            codes, scales = held["c", n]
-            for g, at in pieces(n):
-                a, b = max(lo, at), min(hi, at + w)
-                if b > a:
-                    done_cols = added.get((strip, r), 0)
-                    added[strip, r] = done_cols + b - a
-                    nc.tensor.matmul_mx(
-                        out=bank(("out", strip, r))[:, a - at : b - at],
-                        lhsT=w_sb[:, g, 2 * P * r : 2 * P * (r + 1)].bitcast(FP4X4),
-                        lhsT_scale=ws_sb[:, g, P * r : P * (r + 1)],
-                        rhs=codes[:, a:b].bitcast(FP8X4),
-                        rhs_scale=scales[:, a:b],
-                        start=(done_cols == 0),
-                        stop=(done_cols + b - a == 4 * w),
-                    )
+        def out_key(strip, r, lo):
+            return ("out", strip, r, lo // 256) if (strip, r) in SPLIT else ("out", strip, r)
 
-        def out_exit(eng, strip, r, lo=0, hi=None):
-            w = STRIPS[strip][1]
-            hi = w if hi is None else hi
-            dst = get(("staged", strip, r), [P, w], F32)[:].rearrange("p (m s) -> p m s", s=4)
-            src = bank(("out", strip, r))[:, 0:w].rearrange("p (s m) -> p m s", s=4)
-            copy[eng](out=dst[:, lo // 4 : hi // 4], in_=src[:, lo // 4 : hi // 4])
+        def out_pass(eng, n, r, lo=0, hi=WIDTH):
+            strip, g = UNITS[n][0], UNITS[n][1][0]
+            codes, scales = held["c", n]
+            key = out_key(strip, r, lo)
+            size, at = (256, lo // 256 * 256) if len(key) == 4 else (WIDTH, 0)
+            done_cols = added.get(key, 0)
+            added[key] = done_cols + hi - lo
+            nc.tensor.matmul_mx(
+                out=bank(key)[:, lo - at : hi - at],
+                lhsT=w_sb[:, g, 2 * P * r : 2 * P * (r + 1)].bitcast(FP4X4),
+                lhsT_scale=ws_sb[:, g, P * r : P * (r + 1)],
+                rhs=codes[:, lo:hi].bitcast(FP8X4),
+                rhs_scale=scales[:, lo:hi],
+                start=(done_cols == 0),
+                stop=(done_cols + hi - lo == 4 * size),
+            )
+
+        def out_exit(eng, strip, r, lo=0, hi=WIDTH):
+            h, key = blocks(strip), out_key(strip, r, lo)
+            dst = get(("staged", strip, r), [P, WIDTH], F32)[:, lo:hi]
+            if len(key) == 4:
+                src = bank(key)[:, 0:256].rearrange("p (s m) -> p m s", s=4)
+                copy[eng](out=dst.rearrange("p (m s) -> p m s", s=4), in_=src)
+            elif h == 2:
+                src = bank(key)[:, lo:hi].rearrange("p (h s m) -> p h m s", s=4, m=64)
+                copy[eng](out=dst.rearrange("p (h m s) -> p h m s", s=4, m=64), in_=src)
+            else:
+                src = bank(key)[:].rearrange("p (s m) -> p m s", s=4)[:, lo // 4 : hi // 4]
+                copy[eng](out=dst.rearrange("p (m s) -> p m s", s=4), in_=src)
 
         def store(eng, strip, r, lo=0, hi=None):
             first, w = STRIPS[strip]
@@ -363,6 +381,10 @@ def tile_spike_covariance_readout_s13_kernel(
                 return [], [("lag_planes", a[0])]
             if call is lag_interleave:
                 return [("lag_planes", a[0])], [("lag_grouped", a[0])]
+            if call is mix:
+                return [("lag_planes", a[0])], [("mixed", a[0], a[1])]
+            if call is mix_exit:
+                return [("mixed", a[0], a[1])], [("lag_grouped", a[0])]
             if call is lag_quant:
                 return [("lag_grouped", a[0])], [("lag", a[0])]
             if call is turn:
@@ -375,18 +397,22 @@ def tile_spike_covariance_readout_s13_kernel(
                 return [("lag", UNITS[a[1]][0])] + [("ld", g) for g in UNITS[a[1]][1]], [a]
             if call is direct:
                 return [("direct", a[0], a[1]), "gp"], [("grouped", a[0])]
-            if call is windows:
+            if call is window and a[0] in OWN_BANK:
                 return [("windows", a[0], 0), ("diag_of", UNITS[a[0]][1][0])], [("planes", a[0])]
+            if call is window:
+                return [("plane", a[0], a[1]), ("diag_of", UNITS[a[0]][1][0])] + [("first", a[0], a[1])] * (a[1] in S_FIRST and a[0] > 0), [("planes", a[0])] + [("first", a[0], a[1])] * (a[1] not in S_FIRST or a[0] == 0)
             if call is plane:
-                return [("plane", a[0], a[1]), "gp"], [("planes", a[0])]
+                if not has_diag(a[0]) or a[0] in OWN_BANK:
+                    return [("plane", a[0], a[1]), "gp"], [("planes", a[0])]
+                return [("plane", a[0], a[1]), "gp"] + [("first", a[0], a[1])] * (a[1] not in S_FIRST or a[0] == 0), [("planes", a[0])] + [("first", a[0], a[1])] * (a[1] in S_FIRST and a[0] > 0)
             if call is interleave:
                 return [("planes", a[0])], [("grouped", a[0])]
             if call is quant:
                 return [("grouped", a[0])], [("c",) + tuple(a)]
             if call is out_pass:
-                return [key for key in quant_keys if key[1] == a[0] and (len(key) == 2 or len(a) == 2 or key[2] == a[2])], [("out", UNITS[a[0]][0], a[1])]
+                return [key for key in quant_keys if key[1] == a[0] and (len(key) == 2 or len(a) == 2 or key[2] == a[2])], [out_key(UNITS[a[0]][0], a[1], a[2] if len(a) > 2 else 0)]
             if call is out_exit:
-                return [("out", a[0], a[1])], [("staged", a[0], a[1]), ("staged_part",) + tuple(a)]
+                return [out_key(a[0], a[1], a[2] if len(a) > 2 else 0)], [("staged", a[0], a[1]), ("staged_part",) + tuple(a)]
             return [("staged_part",) + tuple(a)], []
 
         T, V, S, G, D = [], [], [], [], []
@@ -401,16 +427,11 @@ def tile_spike_covariance_readout_s13_kernel(
 
         quant_keys = []
 
-        def has_windows(n):
-            return n < 16 and n % 2 == 0 and window(n, UNITS[n][1][0]) > 0
-
         jobs = {1: [("plane", 2, t) for t in range(4)]}
-        if has_windows(2):
-            jobs[1] = jobs[1][:1] + [("windows", 2, 0)] + jobs[1][1:]
         for k in range(2, 9):
             d = [("direct", 2 * k - 1, q) for q in range(4)]
             x = [("plane", 2 * k, t) for t in range(4)] if k < 8 else []
-            w = [("windows", 2 * k, 0)] if has_windows(2 * k) else []
+            w = [("windows", 2 * k, 0)] if 2 * k in OWN_BANK else []
             jobs[k] = d[:3] + x[:1] + d[3:] + w + x[1:]
         ring_jobs = [job for k in range(1, 9) for job in jobs[k]]
         filled = [0]
@@ -421,12 +442,9 @@ def tile_spike_covariance_readout_s13_kernel(
                     on_bank(ring_names[filled[0] % 4], fill, *ring_jobs[filled[0]])
                     filled[0] = filled[0] + 1
 
-        def out_name(n, r):
-            return ("ring%d" if UNITS[n][0] == 4 else "out%d") % r
-
         def run_pass(task):
             if task:
-                on_bank(out_name(task[1], task[2]), *task)
+                on_bank(LAST_BANKS.get(uses(task)[1][0], "out%d" % task[2]), *task)
         ring_names = ["ring1", "ring2", "ring3", "ring0"]
         on_bank("ring3", warm_up, WIDTH)
         on_bank("out0", turn, 0, 0)
@@ -454,11 +472,11 @@ def tile_spike_covariance_readout_s13_kernel(
         run_pass((out_pass, 1, 1))
         fills(1)
         V.extend([(widen, 0, 0), (widen, 0, 2, 0, 256), (widen, 0, 3, 0, 256), (widen, 0, 2, 256, 512), (lag_interleave, 0, 0, 64), (lag_interleave, 0, 64, 112), (lag_quant, 0), (ld_quant, 0, 0, 256), (ld_quant, 0, 256, 512)])
-        V.extend([(widen, 1, t) for t in range(4)] + [(windows, 0), (ld_quant, 1), (lag_interleave, 1, 0, 128), (ld_quant, 2)])
-        V.extend([(direct, 1, q) for q in range(4)] + [(ld_quant, 3), (quant, 1), (lag_quant, 1), (build_diag, 1), (quant, 0)])
+        V.extend([(widen, 1, t) for t in range(4)] + [(window, 0, t) for t in range(4)] + [(ld_quant, 1), (lag_interleave, 1, 0, 128), (ld_quant, 2)])
+        V.extend([(direct, 1, q) for q in range(4)] + [(ld_quant, 3), (quant, 1), (quant, 0), (lag_quant, 1)])
         S.extend([(widen, 0, 1), (widen, 0, 3, 256, 512), (lag_interleave, 0, 112, 128), (turn_exit, 0, 0), (turn_exit, 0, 1), (spread_exit, 0), (spread_exit, 1), (build_diag, 0)])
         S.extend([(turn_exit, 1, 0), (turn_exit, 1, 1), (plane, 0, 0), (plane, 0, 1), (turn_exit, 2, 0), (turn_exit, 2, 1), (plane, 0, 2), (plane, 0, 3)])
-        S.extend([(turn_exit, 3, 0), (turn_exit, 3, 1), (interleave, 0, G_LATE, WIDTH)] + [(plane, 2, t) for t in range(4)] + [(widen, 2, 0), (widen, 2, 1)])
+        S.extend([(build_diag, 1), (turn_exit, 3, 0), (turn_exit, 3, 1), (interleave, 0, G_LATE, WIDTH)] + [(plane, 2, t) for t in range(4)] + [(widen, 2, 0), (widen, 2, 1)])
         G.append((interleave, 0, 0, G_LATE))
         PLACES = {("ld_grouped", 2): "gpsimd_out"}
         shared = [[("ld_grouped", 2)] + [("grouped", n) for n in range(0, 16, 2)]]
@@ -466,8 +484,8 @@ def tile_spike_covariance_readout_s13_kernel(
             2: ([(widen, 2, 2), (widen, 2, 3)], [(lag_interleave, 2, 0, 64)]),
             3: ([(out_exit, 0, 0), (out_exit, 0, 1)], [(out_exit, 0, 2), (widen, 3, 0), (widen, 3, 1)]),
             4: ([(out_exit, 0, 3), (widen, 3, 2), (widen, 3, 3)], [(lag_interleave, 3, 0, 64)]),
-            5: ([(out_exit, 1, 0), (out_exit, 1, 1)], [(out_exit, 1, 2)]),
-            6: ([(build_diag, 3), (out_exit, 1, 3)], []),
+            5: ([(out_exit, 1, 0), (out_exit, 1, 1)], [(out_exit, 1, 2), (build_diag, 3)]),
+            6: ([(out_exit, 1, 3)], []),
             7: ([], [(out_exit, 2, 0)]),
         }
         slot = {}
@@ -482,18 +500,20 @@ def tile_spike_covariance_readout_s13_kernel(
                 due = [None] * 2 + due
             else:
                 due = due + [None] * (len(jobs[k]) + 1 - len(due) - ahead.get(k, 1)) + [(out_pass, 2 * k - 1, r) for r in range(ahead.get(k, 1))]
-            run_pass(due[0])
-            for i in range(len(jobs[k])):
-                last = i + 1 == len(jobs[k])
-                for task in due[i + 1 :] if last else due[i + 1 : i + 2]:
-                    run_pass(task)
-                fills(1)
+            todo = [x for x in due if x]
+            for step in PATTERN[k]:
+                if step == "F":
+                    fills(1)
+                else:
+                    run_pass(todo[0])
+                    todo = todo[1:]
+            assert not todo
             if (direct, 2 * k - 2, 0) not in V:
                 G.append((interleave, 2 * k - 2, 0, share[k]))
             rest = [(interleave, 2 * k - 2, share[k], WIDTH)] if share[k] < WIDTH else []
-            V.extend([(direct, 2 * k - 1, q) for q in range(4)])
-            if has_windows(2 * k):
-                V.append((windows, 2 * k))
+            d = [(direct, 2 * k - 1, q) for q in range(4)]
+            w = [(window, 2 * k, t) for t in range(4)] if has_diag(2 * k) else []
+            V.extend(d + w if 2 * k in OWN_BANK else d[:W_AT] + w[:1] + d[W_AT:] + w[1:])
             V.extend(slot.get(k, []))
             if k < 7:
                 V.extend(rest)
@@ -509,13 +529,16 @@ def tile_spike_covariance_readout_s13_kernel(
             run_pass((out_pass, 12, r))
         run_pass((out_pass, 14, 0))
         run_pass((out_pass, 14, 1))
-        for r, units in enumerate(((15,), (15,), (14, 15), (13, 12, 14, 15))):
+        for r, units in enumerate(((15,), (15,), (14, 15))):
             for n in units:
                 run_pass((out_pass, n, r))
-        S.extend([(out_exit, 3, r, lo, lo + 256) for r in (0, 3) for lo in (0, 256)])
+        for lo in (0, 256):
+            for n in (13, 12, 14, 15):
+                run_pass((out_pass, n, 3, lo, lo + 256))
+        S.extend([(out_exit, 3, 0, 0, 256), (out_exit, 3, 0, 256, 512), (out_exit, 3, 3, 0, 256)])
         D.extend([(store, k, r) for k in range(3) for r in range(4)])
         D.extend([(store, 3, 0, 0, 256), (store, 3, 0, 256, 512), (store, 3, 1), (store, 3, 2), (store, 3, 3, 0, 256), (store, 3, 3, 256, 512)])
-        V.extend([(out_exit, 3, 1), (out_exit, 3, 2)])
+        V.extend([(out_exit, 3, 1), (out_exit, 3, 2), (out_exit, 3, 3, 256, 512)])
         for n in range(16):
             if n % 2 or (direct, n, 0) in V:
                 PLACES["grouped", n] = "direct_out%d" % ((n + 1) // 2 % 2)

@@ -29,12 +29,18 @@ G_LAST = 320
 NW = 4
 PAIRED = ()
 HALVED = (3,)
-SPLIT = ((3, 3),)
+SPLIT = ((3, 0), (3, 1), (3, 2), (3, 3))
 LAST_BANKS = {("out", 3, 3, 1): "ring0"}
 S_FIRST = (0,)
 W_AT = 3
 PATTERN = {2: "PFPFPFPFPFPFFFPPF", 3: "PFPFPFPFPPFFPFPF", 4: "PFPFPFPFPFPFFPFPF", 5: "PFPFPFPFPPFFPFPF", 6: "PFPFPFFPPFPFFPF", 7: "FPFPFPFPFPFPFPF"}
 OWN_BANK = (0, 4, 8)
+LAST_IN_HALVES = False
+G_A = 256
+S_ORDER = -1
+EXITS = "SVSVSVSV"
+def ORDER(e, l):
+    return [(0, 0, e), (1, 0, e), (0, 1, e), (2, 0, e), (1, 1, e), (3, 0, e), (0, 0, l), (1, 0, l), (2, 0, l), (3, 0, l), (0, 1, l), (1, 1, l), (2, 1, e + l), (3, 1, e + l)]
 
 
 def tile_spike_covariance_readout_s13_kernel(
@@ -220,11 +226,11 @@ def tile_spike_covariance_readout_s13_kernel(
             copy[eng](out=dst[:, 64 * half : 64 * half + 64], in_=src)
 
         def quantise(codes, scales, src, lo, hi):
-            nc.vector.quantize_mx(out=codes[:, lo:hi].bitcast(FP8X4), scales=scales[:, lo:hi], in_=src[:, 4 * lo : 4 * hi])
+            nc.vector.quantize_mx(out=codes[:, lo:hi].bitcast(FP8X4), scales=scales[:, lo:hi], in_=src)
 
         def lag_quant(eng, strip):
             w = STRIPS[strip][1]
-            quantise(*mx_tiles(("lag", strip), w), held["lag_grouped", strip], 0, w)
+            quantise(*mx_tiles(("lag", strip), w), held["lag_grouped", strip][:], 0, w)
 
         def turn(eng, g, half):
             view = bank(("turned", g, half))[:].rearrange("p (t u m) -> p t u m", t=2, u=2)
@@ -241,7 +247,7 @@ def tile_spike_covariance_readout_s13_kernel(
             )
 
         def ld_quant(eng, g, lo=0, hi=WIDTH):
-            quantise(*mx_tiles(("ld", g), WIDTH), held["ld_grouped", g], lo, hi)
+            quantise(*mx_tiles(("ld", g), WIDTH), held["ld_grouped", g][:, 4 * lo : 4 * hi], lo, hi)
 
         def s_pass(dst, at, strip, g, t, lo, hi):
             ld_codes, ld_scales = held["ld", g]
@@ -306,8 +312,13 @@ def tile_spike_covariance_readout_s13_kernel(
                         out=dst[:, :, lo:hi], in_=src[:, :, lo:hi], func=ACT.Copy, scale=gain_f[:, 4 * g + x : 4 * g + x + 1]
                     )
 
+        def grouped(n, lo, hi):
+            if n == 14 and lo >= 256 and LAST_IN_HALVES:
+                return held["grouped", 15][:, 4 * (lo - 256) : 4 * (hi - 256)]
+            return get(("grouped", n), [P, 4 * WIDTH], BF16)[:, 4 * lo : 4 * hi]
+
         def interleave(eng, n, lo, hi):
-            dst = get(("grouped", n), [P, 4 * WIDTH], BF16)[:, 4 * lo : 4 * hi]
+            dst = grouped(n, lo, hi)
             src = held["planes", n][:, :, lo:hi]
             if eng == "G":
                 nc.gpsimd.tensor_scalar(
@@ -324,7 +335,7 @@ def tile_spike_covariance_readout_s13_kernel(
                 )
 
         def quant(eng, n, lo=0, hi=WIDTH):
-            quantise(*mx_tiles(("c", n), WIDTH), held["grouped", n], lo, hi)
+            quantise(*mx_tiles(("c", n), WIDTH), grouped(n, lo, hi), lo, hi)
 
         added = {}
 
@@ -396,7 +407,7 @@ def tile_spike_covariance_readout_s13_kernel(
             if call is fill:
                 return [("lag", UNITS[a[1]][0])] + [("ld", g) for g in UNITS[a[1]][1]], [a]
             if call is direct:
-                return [("direct", a[0], a[1]), "gp"], [("grouped", a[0])]
+                return [("direct", a[0], a[1]), "gp"], [("grouped", a[0])] + [("half", 15)] * (a == (15, 0))
             if call is window and a[0] in OWN_BANK:
                 return [("windows", a[0], 0), ("diag_of", UNITS[a[0]][1][0])], [("planes", a[0])]
             if call is window:
@@ -406,9 +417,11 @@ def tile_spike_covariance_readout_s13_kernel(
                     return [("plane", a[0], a[1]), "gp"], [("planes", a[0])]
                 return [("plane", a[0], a[1]), "gp"] + [("first", a[0], a[1])] * (a[1] not in S_FIRST or a[0] == 0), [("planes", a[0])] + [("first", a[0], a[1])] * (a[1] in S_FIRST and a[0] > 0)
             if call is interleave:
-                return [("planes", a[0])], [("grouped", a[0])]
+                return [("planes", a[0])], [("grouped", 14, 1) if a[0] == 14 and a[1] >= 256 and LAST_IN_HALVES else ("grouped", a[0])]
             if call is quant:
-                return [("grouped", a[0])], [("c",) + tuple(a)]
+                if a == (14, 256, 512) and LAST_IN_HALVES:
+                    return [("grouped", 14, 1)], [("c",) + tuple(a)]
+                return [("grouped", a[0])] + [("half", 15)] * (a == (15, 0, 256)), [("c",) + tuple(a)]
             if call is out_pass:
                 return [key for key in quant_keys if key[1] == a[0] and (len(key) == 2 or len(a) == 2 or key[2] == a[2])], [out_key(UNITS[a[0]][0], a[1], a[2] if len(a) > 2 else 0)]
             if call is out_exit:
@@ -521,24 +534,18 @@ def tile_spike_covariance_readout_s13_kernel(
                 S.extend(rest)
             V.extend(port_first.get(k, []) + [(quant, 2 * k - 1), (quant, 2 * k - 2)] + port_last.get(k, []))
             S.extend([(plane, 2 * k, 0)] + extra[k][0] + [(plane, 2 * k, t) for t in range(1, 4)] + extra[k][1])
-        G.append((interleave, 14, 0, G_LAST))
-        S.extend([(out_exit, 2, 1), (interleave, 14, G_LAST, WIDTH), (out_exit, 2, 2), (out_exit, 2, 3)])
-        V.extend([(direct, 15, q) for q in range(4)] + [(quant, 14), (quant, 15)])
-        for r in range(3):
-            run_pass((out_pass, 13, r))
-            run_pass((out_pass, 12, r))
-        run_pass((out_pass, 14, 0))
-        run_pass((out_pass, 14, 1))
-        for r, units in enumerate(((15,), (15,), (14, 15))):
-            for n in units:
-                run_pass((out_pass, n, r))
-        for lo in (0, 256):
-            for n in (13, 12, 14, 15):
-                run_pass((out_pass, n, 3, lo, lo + 256))
-        S.extend([(out_exit, 3, 0, 0, 256), (out_exit, 3, 0, 256, 512), (out_exit, 3, 3, 0, 256)])
+        G.append((interleave, 14, 0, G_A))
+        S.extend([(out_exit, 2, 1), (out_exit, 2, 2)] + [(interleave, 14, G_A, WIDTH), (out_exit, 2, 3)][::S_ORDER])
+        V.extend([(direct, 15, q) for q in range(4)] + [(quant, 14, 0, 256), (quant, 15, 0, 256), (quant, 15, 256, 512), (quant, 14, 256, 512)])
+        early, late = (13, 12), (14, 15)
+        for r, h, units in ORDER(early, late):
+            for n in units if h == 0 else sorted(units, key=lambda n: n == 14):
+                on_bank(banks["direct", 15, r] if h else "out%d" % r, out_pass, n, r, 256 * h, 256 * h + 256)
+        for h in range(2):
+            for r in range(4):
+                (S if EXITS[4 * h + r] == "S" else V).append((out_exit, 3, r, 256 * h, 256 * h + 256))
         D.extend([(store, k, r) for k in range(3) for r in range(4)])
-        D.extend([(store, 3, 0, 0, 256), (store, 3, 0, 256, 512), (store, 3, 1), (store, 3, 2), (store, 3, 3, 0, 256), (store, 3, 3, 256, 512)])
-        V.extend([(out_exit, 3, 1), (out_exit, 3, 2), (out_exit, 3, 3, 256, 512)])
+        D.extend([(store, 3, r, lo, lo + 256) for lo in (0, 256) for r in range(4)])
         for n in range(16):
             if n % 2 or (direct, n, 0) in V:
                 PLACES["grouped", n] = "direct_out%d" % ((n + 1) // 2 % 2)
@@ -557,6 +564,8 @@ def tile_spike_covariance_readout_s13_kernel(
 
 
         def apart(reader, writer):
+            if reader[0] is quant and writer[0] is interleave and len(reader) == 4:
+                return writer[3] <= reader[2] or reader[3] <= writer[2]
             return reader[0] is quant and writer[0] is direct and len(reader) == 4 and not reader[2] <= P * writer[2] < reader[3]
 
         quant_keys = [("c",) + tuple(task[1:]) for task in programme["V"] if task[0] is quant]

@@ -41,6 +41,7 @@ S_ORDER = -1
 EXITS = "SVSVSVSV"
 def ORDER(e, l):
     return [(0, 0, e), (1, 0, e), (0, 1, e), (2, 0, e), (1, 1, e), (3, 0, e), (0, 0, l), (1, 0, l), (2, 0, l), (3, 0, l), (0, 1, l), (1, 1, l), (2, 1, e + l), (3, 1, e + l)]
+S_REST = (7,)
 
 
 def tile_spike_covariance_readout_s13_kernel(
@@ -55,14 +56,17 @@ def tile_spike_covariance_readout_s13_kernel(
         def tile(shape, dtype, name):
             return sb.tile(shape, dtype, name=name, align_bytes=ALIGN)
 
+        lag_factor = tile([P, 4], F32, "lag_factor")
+        nc.scalar.dma_start(out=lag_factor[:], in_=lag_scale.rearrange("(p t) o -> p (t o)", t=4))
+        table_warm = tile([P, 2], F32, "table_warm")
+        nc.vector.memset(table_warm[:, 0:1], 0.0)
+        nc.scalar.activation(out=table_warm[:, 1:2], in_=table_warm[:, 0:1], func=ACT.Copy)
         gp_rows = tile([P, WIDTH], BF16, "gp_rows")
         nc.vector.memset(gp_rows[:].bitcast(I32), 0)
         ident = tile([P, P], F32, "ident")
         make_identity(nc, ident[:])
         ident_bf = tile([P, P], BF16, "ident_bf")
         nc.vector.tensor_copy(out=ident_bf[:], in_=ident[:])
-        lag_factor = tile([P, 4], F32, "lag_factor")
-        nc.scalar.dma_start(out=lag_factor[:], in_=lag_scale.rearrange("(p t) o -> p (t o)", t=4))
         w_sb = tile([P, 4, 2 * R], U8, "w_sb")
         ws_sb = tile([P, 4, R], U8, "ws_sb")
         nc.vector.memset(ws_sb[:].rearrange("p g n -> p (g n)").bitcast(I32), 0)
@@ -78,18 +82,25 @@ def tile_spike_covariance_readout_s13_kernel(
                 in_=lag_view[:, first : first + step, WIDTH * panel : WIDTH * (panel + 1)],
             )
 
-        def load_rows(g, parts=1):
-            src = loads[WIDTH * g : WIDTH * (g + 1), :].rearrange("(m t) k -> m t k", t=4)
-            step = 4 // parts
-            for first in range(0, 4, step):
-                part = tile([P, step, K], BF16, "rows%d_%d" % (g, first))
-                nc.sync.dma_start(out=part[:], in_=src[:, first : first + step, :])
-                for t in range(step):
-                    rows[g, first + t] = part[:, t, :]
+        def load_lag_two(panel, first=0, step=4):
+            if panel not in lag_raw:
+                both = tile([P, 4, 2 * WIDTH], U8, "lag_raw%d" % panel)
+                lag_raw["both", panel], lag_raw[panel], lag_raw[panel + 1] = both, both[:, :, 0:WIDTH], both[:, :, WIDTH:]
+            nc.sync.dma_start(
+                out=lag_raw["both", panel][:, first : first + step, :],
+                in_=lag_view[:, first : first + step, WIDTH * panel : WIDTH * (panel + 2)],
+            )
 
-        def load_gp():
-            nc.sync.dma_start(out=gp_rows[0:4, :], in_=gain.rearrange("(g x) -> g x", g=4))
-            nc.sync.dma_start(out=gp_rows[4:8, :], in_=private.rearrange("(g x) -> g x", g=4))
+        def load_rows(g, first=0, step=4):
+            src = loads[WIDTH * g : WIDTH * (g + 1), :].rearrange("(m t) k -> m t k", t=4)
+            part = tile([P, step, K], BF16, "rows%d_%d" % (g, first))
+            nc.sync.dma_start(out=part[:], in_=src[:, first : first + step, :])
+            for t in range(step):
+                rows[g, first + t] = part[:, t, :]
+
+        def load_gp(queue=nc.sync):
+            queue.dma_start(out=gp_rows[0:4, :], in_=gain.rearrange("(g x) -> g x", g=4))
+            queue.dma_start(out=gp_rows[4:8, :], in_=private.rearrange("(g x) -> g x", g=4))
 
         def load_w():
             nc.sync.dma_start(out=w_sb[:], in_=w_words.rearrange("g p n -> p g n"))
@@ -102,7 +113,8 @@ def tile_spike_covariance_readout_s13_kernel(
 
         load_lag(0, 0, 2)
         load_lag(0, 2, 2)
-        load_rows(0, parts=2)
+        load_rows(0, 0, 2)
+        load_rows(0, 2, 2)
         load_gp()
         load_rows(1)
         load_lag(1)
@@ -504,7 +516,8 @@ def tile_spike_covariance_readout_s13_kernel(
         slot = {}
         port_first = {3: [(build_diag, 2)], 4: []}
         port_last = {2: [(lag_interleave, 2, 64, 128)], 3: [(lag_quant, 2)], 4: [(lag_interleave, 3, 64, 128)], 5: [(lag_quant, 3)]}
-        share = {2: WIDTH, 3: G_ODD, 4: WIDTH, 5: G_ODD, 6: WIDTH, 7: G_LATE, 8: G_LAST}
+        share = {2: 512, 3: 384, 4: 512, 5: 384, 6: 512, 7: 352}
+        lead = {}
         ahead = {2: 2, 3: 2, 4: 2, 5: 2}
         for k in range(2, 8):
             a, b = 2 * k - 4, 2 * k - 3
@@ -528,12 +541,12 @@ def tile_spike_covariance_readout_s13_kernel(
             w = [(window, 2 * k, t) for t in range(4)] if has_diag(2 * k) else []
             V.extend(d + w if 2 * k in OWN_BANK else d[:W_AT] + w[:1] + d[W_AT:] + w[1:])
             V.extend(slot.get(k, []))
-            if k < 7:
+            if k not in S_REST:
                 V.extend(rest)
             else:
                 S.extend(rest)
             V.extend(port_first.get(k, []) + [(quant, 2 * k - 1), (quant, 2 * k - 2)] + port_last.get(k, []))
-            S.extend([(plane, 2 * k, 0)] + extra[k][0] + [(plane, 2 * k, t) for t in range(1, 4)] + extra[k][1])
+            S.extend(lead.get(k, []) + [(plane, 2 * k, 0)] + extra[k][0] + [(plane, 2 * k, t) for t in range(1, 4)] + extra[k][1])
         G.append((interleave, 14, 0, G_A))
         S.extend([(out_exit, 2, 1), (out_exit, 2, 2)] + [(interleave, 14, G_A, WIDTH), (out_exit, 2, 3)][::S_ORDER])
         V.extend([(direct, 15, q) for q in range(4)] + [(quant, 14, 0, 256), (quant, 15, 0, 256), (quant, 15, 256, 512), (quant, 14, 256, 512)])

from contextlib import ExitStack

import concourse.mybir as mybir
from concourse.masks import make_identity

F32 = mybir.dt.float32
BF16 = mybir.dt.bfloat16
U32 = mybir.dt.uint32
I32 = mybir.dt.int32
U8 = mybir.dt.uint8
FP8 = mybir.dt.float8_e4m3fn
FP8X4 = mybir.dt.float8_e4m3fn_x4
FP4X4 = mybir.dt.float4_e2m1fn_x4
ALU = mybir.AluOpType
ACT = mybir.ActivationFunctionType

M, K, R = 2048, 512, 512
FLOPS = 2 * M * K * M + 2 * R * M * M

P = 128
WIDTH = 512
ALIGN = 256
STRIPS = [(0, 512), (512, 512), (1024, 512), (1536, 512)]
UNITS = [(k, ((k + d) % 4,)) for k in range(4) for d in (0, 1, 2, 3)]
A0 = 128
G_ODD = 384
G_LATE = 352
G_LAST = 320
NW = 4
PAIRED = ()
HALVED = (3,)
SPLIT = ((3, 0), (3, 1), (3, 2), (3, 3))
LAST_BANKS = {("out", 3, 3, 1): "ring0"}
S_FIRST = (0,)
W_AT = 3
PATTERN = {2: "PFPFPFPFPFPFFFPPF", 3: "PFPFPFPFPPFFPFPF", 4: "PFPFPFPFPFPFFPFPF", 5: "PFPFPFPFPPFFPFPF", 6: "PFPFPFFPPFPFFPF", 7: "FPFPFPFPFPFPFPF"}
OWN_BANK = (0, 4, 8)
LAST_IN_HALVES = False
G_A = 256
S_ORDER = -1
EXITS = "SVSVSVSV"
def ORDER(e, l):
    return [(0, 0, e), (1, 0, e), (0, 1, e), (2, 0, e), (1, 1, e), (3, 0, e), (0, 0, l), (1, 0, l), (2, 0, l), (3, 0, l), (0, 1, l), (1, 1, l), (2, 1, e + l), (3, 1, e + l)]
S_REST = (7,)


def tile_spike_covariance_readout_s13_kernel(
    tc, loads, lag_bytes, lag_scale, gain, private, w_words, w_scales, out
):
    nc = tc.nc
    with ExitStack() as ctx:
        sb = ctx.enter_context(tc.tile_pool(name="sb", bufs=1))
        psum = ctx.enter_context(tc.psum_pool(name="psum", bufs=1))
        ctx.enter_context(tc.manual_schedule())

        def tile(shape, dtype, name):
            return sb.tile(shape, dtype, name=name, align_bytes=ALIGN)

        lag_factor = tile([P, 4], F32, "lag_factor")
        nc.scalar.dma_start(out=lag_factor[:], in_=lag_scale.rearrange("(p t) o -> p (t o)", t=4))
        table_warm = tile([P, 2], F32, "table_warm")
        nc.vector.memset(table_warm[:, 0:1], 0.0)
        nc.scalar.activation(out=table_warm[:, 1:2], in_=table_warm[:, 0:1], func=ACT.Copy)
        gp_rows = tile([P, WIDTH], BF16, "gp_rows")
        nc.vector.memset(gp_rows[:].bitcast(I32), 0)
        ident = tile([P, P], F32, "ident")
        make_identity(nc, ident[:])
        ident_bf = tile([P, P], BF16, "ident_bf")
        nc.vector.tensor_copy(out=ident_bf[:], in_=ident[:])
        w_sb = tile([P, 4, 2 * R], U8, "w_sb")
        ws_sb = tile([P, 4, R], U8, "ws_sb")
        nc.vector.memset(ws_sb[:].rearrange("p g n -> p (g n)").bitcast(I32), 0)

        lag_view = lag_bytes.rearrange("(p t) j -> p t j", t=4)
        lag_raw, rows = {}, {}

        def load_lag(panel, first=0, step=4):
            if panel not in lag_raw:
                lag_raw[panel] = tile([P, 4, WIDTH], U8, "lag_raw%d" % panel)
            nc.sync.dma_start(
                out=lag_raw[panel][:, first : first + step, :],
                in_=lag_view[:, first : first + step, WIDTH * panel : WIDTH * (panel + 1)],
            )

        def load_lag_two(panel, first=0, step=4):
            if panel not in lag_raw:
                both = tile([P, 4, 2 * WIDTH], U8, "lag_raw%d" % panel)
                lag_raw["both", panel], lag_raw[panel], lag_raw[panel + 1] = both, both[:, :, 0:WIDTH], both[:, :, WIDTH:]
            nc.sync.dma_start(
                out=lag_raw["both", panel][:, first : first + step, :],
                in_=lag_view[:, first : first + step, WIDTH * panel : WIDTH * (panel + 2)],
            )

        def load_rows(g, first=0, step=4):
            src = loads[WIDTH * g : WIDTH * (g + 1), :].rearrange("(m t) k -> m t k", t=4)
            part = tile([P, step, K], BF16, "rows%d_%d" % (g, first))
            nc.sync.dma_start(out=part[:], in_=src[:, first : first + step, :])
            for t in range(step):
                rows[g, first + t] = part[:, t, :]

        def load_gp(queue=nc.sync):
            queue.dma_start(out=gp_rows[0:4, :], in_=gain.rearrange("(g x) -> g x", g=4))
            queue.dma_start(out=gp_rows[4:8, :], in_=private.rearrange("(g x) -> g x", g=4))

        def load_w():
            nc.sync.dma_start(out=w_sb[:], in_=w_words.rearrange("g p n -> p g n"))
            ws_view = w_scales.bitcast(I32).rearrange("g q n -> q g n")
            for quad in range(4):
                nc.sync.dma_start(
                    out=ws_sb[32 * quad : 32 * quad + 4, :, :].bitcast(I32),
                    in_=ws_view[4 * quad : 4 * quad + 4, :, :],
                )

        load_lag(0, 0, 2)
        load_lag(0, 2, 2)
        load_rows(0, 0, 2)
        load_rows(0, 2, 2)
        load_gp()
        load_rows(1)
        load_lag(1)
        load_rows(2)
        load_rows(3)
        load_lag(2)
        load_w()
        load_lag(3)


        gp_f = tile([P, 2, 16], F32, "gp_f")
        gain_f, priv_f = gp_f[:, 0, :], gp_f[:, 1, :]

        held = {}

        def get(key, shape, dtype):
            if key not in held:
                name = PLACES.get(key, key if isinstance(key, str) else "_".join([str(x) for x in key]))
                held[key] = tile(shape, dtype, name)
            return held[key]

        def bank(key):
            if key not in held:
                shape, dtype = ([P, 2 * WIDTH], BF16) if key[0] == "mixed" else ([P, WIDTH], F32)
                held[key] = psum.tile(shape, dtype, name=banks[key])
            return held[key]

        def mx_tiles(key, width):
            if key not in held:
                name = "_".join([str(x) for x in key])
                held[key] = (tile([P, width], U32, name + "_codes"), tile([P, width], U8, name + "_scales"))
            return held[key]

        copy = {"V": nc.vector.tensor_copy, "S": nc.scalar.copy}

        def pieces(n):
            strip, groups = UNITS[n]
            w = STRIPS[strip][1]
            return [(g, w * i) for i, g in enumerate(groups)]

        def has_diag(n):
            return UNITS[n][0] == UNITS[n][1][0]

        def blocks(strip):
            return 2 if strip in HALVED else 1

        def warm_up(eng, width):
            product = bank(("warm", width))[:, 0:width].rearrange("p (a c) -> p a c", c=P)
            moving = ident[:].unsqueeze(1).to_broadcast([P, width // P, P])
            nc.tensor.matmul(out=product, lhsT=ident[:], rhs=moving, start=True, stop=True)

        def spread(eng, half):
            for t in range(2):
                product = bank(("spread", half))[:, 256 * t : 256 * (t + 1)].rearrange("p (a c) -> p a c", c=P)
                moving = ident_bf[:].unsqueeze(1).to_broadcast([P, 2, P])
                nc.tensor.matmul(out=product, lhsT=gp_rows[:, 2 * half + t : WIDTH : 4], rhs=moving, start=True, stop=True)

        def spread_exit(eng, half):
            copy[eng](
                out=gp_f[:].rearrange("p a (g t) -> p (a g) t", t=4)[:, :, 2 * half : 2 * half + 2],
                in_=bank(("spread", half))[:].rearrange("p (t r) -> p r t", t=2)[:, 0:8],
            )

        def build_diag(eng, g, count=1):
            diag = get(("diag", g // 2), [P, 8, P], BF16)
            at = 4 * (g % 2)
            if eng == "G":
                n = 4 * count
                nc.gpsimd.tensor_tensor(
                    out=diag[:, at : at + n, :],
                    in0=ident[:].unsqueeze(1).to_broadcast([P, n, P]),
                    in1=priv_f[:, 4 * g : 4 * g + n].unsqueeze(2).to_broadcast([P, n, P]),
                    op=ALU.mult,
                )
                return
            for i in range(4 * count):
                value = priv_f[:, 4 * g + i : 4 * g + i + 1]
                if eng == "V":
                    nc.vector.tensor_scalar(out=diag[:, at + i, :], in0=ident_bf[:], scalar1=value, scalar2=None, op0=ALU.mult)
                else:
                    nc.scalar.activation(out=diag[:, at + i, :], in_=ident[:], func=ACT.Copy, scale=value)

        def widen(eng, strip, t, lo=0, hi=None):
            first, w = STRIPS[strip]
            hi = w if hi is None else hi
            at = first % WIDTH
            src = lag_raw[first // WIDTH][:, t, at + lo : at + hi].bitcast(FP8)
            dst = get(("lag_planes", strip), [P, 4, w], BF16)
            if strip in PAIRED:
                dst = dst[:].rearrange("p a b -> p (a b)").rearrange("p (u j e) -> p u j e", u=2, e=2)[:, t // 2, lo:hi, t % 2]
            else:
                dst = dst[:, t, lo:hi]
            factor = lag_factor[:, t : t + 1]
            if eng == "V":
                nc.vector.tensor_scalar(out=dst, in0=src, scalar1=factor, scalar2=None, op0=ALU.mult)
            else:
                nc.scalar.activation(out=dst, in_=src, func=ACT.Copy, scale=factor)

        def lag_interleave(eng, strip, lo, hi):
            h = blocks(strip)
            src = held["lag_planes", strip][:].rearrange("p t (m s) -> p m t s", s=4)[:, lo:hi]
            dst = get(("lag_grouped", strip), [P, 4 * WIDTH], BF16)[:].rearrange("p (h s m t) -> p h m t s", h=h, s=4, t=4)
            size = P // h
            assert lo // size == (hi - 1) // size
            copy[eng](out=dst[:, lo // size, lo % size : (hi - 1) % size + 1], in_=src)

        def mix(eng, strip, half):
            for x in range(2):
                lo = 256 * half + P * x
                nc.tensor.matmul(
                    out=bank(("mixed", strip, half))[:, WIDTH * x : WIDTH * (x + 1)].rearrange("p (c t) -> p c t", t=4),
                    lhsT=ident_bf[:],
                    rhs=held["lag_planes", strip][:, :, lo : lo + P].rearrange("p t c -> p c t"),
                    start=True,
                    stop=True,
                )

        def mix_exit(eng, strip, half):
            dst = get(("lag_grouped", strip), [P, 4 * WIDTH], BF16)[:].rearrange("p (s m t) -> p m s t", s=4, t=4)
            src = bank(("mixed", strip, half))[:].rearrange("p (m s t) -> p m s t", s=4, t=4)
            copy[eng](out=dst[:, 64 * half : 64 * half + 64], in_=src)

        def quantise(codes, scales, src, lo, hi):
            nc.vector.quantize_mx(out=codes[:, lo:hi].bitcast(FP8X4), scales=scales[:, lo:hi], in_=src)

        def lag_quant(eng, strip):
            w = STRIPS[strip][1]
            quantise(*mx_tiles(("lag", strip), w), held["lag_grouped", strip][:], 0, w)

        def turn(eng, g, half):
            view = bank(("turned", g, half))[:].rearrange("p (t u m) -> p t u m", t=2, u=2)
            for t in range(2):
                words = rows[g, 2 * half + t].bitcast(F32)
                for u in range(2):
                    nc.tensor.transpose(view[:, t, u, :], words[:, u:256:2], ident[:])

        def turn_exit(eng, g, half):
            dst = get(("ld_grouped", g), [P, 4 * WIDTH], BF16)[:, 1024 * half : 1024 * half + 1024].bitcast(F32)
            copy[eng](
                out=dst.rearrange("p (t m u) -> p t m u", t=2, u=2),
                in_=bank(("turned", g, half))[:].rearrange("p (t u m) -> p t m u", t=2, u=2),
            )

        def ld_quant(eng, g, lo=0, hi=WIDTH):
            quantise(*mx_tiles(("ld", g), WIDTH), held["ld_grouped", g][:, 4 * lo : 4 * hi], lo, hi)

        def s_pass(dst, at, strip, g, t, lo, hi):
            ld_codes, ld_scales = held["ld", g]
            lag_codes, lag_scales = held["lag", strip]
            nc.tensor.matmul_mx(
                out=dst[:, at : at + hi - lo],
                lhsT=ld_codes[:, P * t : P * (t + 1)].bitcast(FP8X4),
                lhsT_scale=ld_scales[:, P * t : P * (t + 1)],
                rhs=lag_codes[:, lo:hi].bitcast(FP8X4),
                rhs_scale=lag_scales[:, lo:hi],
                start=True,
                stop=True,
            )

        def fill(eng, kind, n, x):
            dst = bank((kind, n, x))
            strip = UNITS[n][0]
            w = STRIPS[strip][1]
            if kind == "direct":
                g, at = pieces(n)[P * x // w]
                for t in range(4):
                    s_pass(dst, P * t, strip, g, t, P * x - at, P * x - at + P)
            elif kind == "windows":
                for t in range(4):
                    s_pass(dst, P * t, strip, UNITS[n][1][0], t, P * t, P * (t + 1))
            elif n in OWN_BANK:
                for half in range(2):
                    lo, hi = (P * (x ^ 1), P * (x ^ 1) + P) if half == x // 2 else (256 * half, 256 * half + 256)
                    s_pass(dst, lo, strip, UNITS[n][1][0], x, lo, hi)
            else:
                s_pass(dst, 0, strip, UNITS[n][1][0], x, 0, w)

        def direct(eng, n, x):
            g = pieces(n)[P * x // STRIPS[UNITS[n][0]][1]][0]
            nc.vector.tensor_tensor(
                out=get(("grouped", n), [P, 4 * WIDTH], BF16)[:, WIDTH * x : WIDTH * (x + 1)].rearrange("p (c t) -> p c t", t=4),
                in0=bank(("direct", n, x))[:].rearrange("p (t c) -> p c t", t=4),
                in1=gain_f[:, 4 * g : 4 * g + 4].unsqueeze(1).to_broadcast([P, P, 4]),
                op=ALU.mult,
            )

        def window(eng, n, t):
            g, h = UNITS[n][1][0], blocks(UNITS[n][0])
            v = P // h
            nc.vector.scalar_tensor_tensor(
                out=get(("planes", n), [P, 4, WIDTH], BF16)[:, t, :].rearrange("p (h c) -> p h c", h=h)[:, :, v * t : v * (t + 1)],
                in0=bank(("windows", n, 0) if n in OWN_BANK else ("plane", n, t))[:].rearrange("p (h c) -> p h c", h=h)[:, :, v * t : v * (t + 1)],
                scalar=gain_f[:, 4 * g + t : 4 * g + t + 1],
                in1=held["diag", g // 2][:, 4 * (g % 2) + t, :].rearrange("p (h c) -> p h c", h=h),
                op0=ALU.mult,
                op1=ALU.add,
            )

        def plane(eng, n, x):
            g, h = UNITS[n][1][0], blocks(UNITS[n][0])
            v, w = P // h, WIDTH // h
            dst = get(("planes", n), [P, 4, WIDTH], BF16)[:, x, :].rearrange("p (h c) -> p h c", h=h)
            src = bank(("plane", n, x))[:].rearrange("p (h c) -> p h c", h=h)
            for lo, hi in [(0, v * x), (v * x + v, w)] if has_diag(n) else [(0, w)]:
                if hi > lo:
                    nc.scalar.activation(
                        out=dst[:, :, lo:hi], in_=src[:, :, lo:hi], func=ACT.Copy, scale=gain_f[:, 4 * g + x : 4 * g + x + 1]
                    )

        def grouped(n, lo, hi):
            if n == 14 and lo >= 256 and LAST_IN_HALVES:
                return held["grouped", 15][:, 4 * (lo - 256) : 4 * (hi - 256)]
            return get(("grouped", n), [P, 4 * WIDTH], BF16)[:, 4 * lo : 4 * hi]

        def interleave(eng, n, lo, hi):
            dst = grouped(n, lo, hi)
            src = held["planes", n][:, :, lo:hi]
            if eng == "G":
                nc.gpsimd.tensor_scalar(
                    out=dst.rearrange("p (c t) -> p c t", t=4),
                    in0=src.rearrange("p t c -> p c t"),
                    scalar1=1.0,
                    scalar2=0.0,
                    op0=ALU.mult,
                    op1=ALU.add,
                )
            else:
                copy[eng](
                    out=dst.rearrange("p (c i t) -> p c t i", i=4, t=4), in_=src.rearrange("p t (c i) -> p c t i", i=4)
                )

        def quant(eng, n, lo=0, hi=WIDTH):
            quantise(*mx_tiles(("c", n), WIDTH), grouped(n, lo, hi), lo, hi)

        added = {}

        def out_key(strip, r, lo):
            return ("out", strip, r, lo // 256) if (strip, r) in SPLIT else ("out", strip, r)

        def out_pass(eng, n, r, lo=0, hi=WIDTH):
            strip, g = UNITS[n][0], UNITS[n][1][0]
            codes, scales = held["c", n]
            key = out_key(strip, r, lo)
            size, at = (256, lo // 256 * 256) if len(key) == 4 else (WIDTH, 0)
            done_cols = added.get(key, 0)
            added[key] = done_cols + hi - lo
            nc.tensor.matmul_mx(
                out=bank(key)[:, lo - at : hi - at],
                lhsT=w_sb[:, g, 2 * P * r : 2 * P * (r + 1)].bitcast(FP4X4),
                lhsT_scale=ws_sb[:, g, P * r : P * (r + 1)],
                rhs=codes[:, lo:hi].bitcast(FP8X4),
                rhs_scale=scales[:, lo:hi],
                start=(done_cols == 0),
                stop=(done_cols + hi - lo == 4 * size),
            )

        def out_exit(eng, strip, r, lo=0, hi=WIDTH):
            h, key = blocks(strip), out_key(strip, r, lo)
            dst = get(("staged", strip, r), [P, WIDTH], F32)[:, lo:hi]
            if len(key) == 4:
                src = bank(key)[:, 0:256].rearrange("p (s m) -> p m s", s=4)
                copy[eng](out=dst.rearrange("p (m s) -> p m s", s=4), in_=src)
            elif h == 2:
                src = bank(key)[:, lo:hi].rearrange("p (h s m) -> p h m s", s=4, m=64)
                copy[eng](out=dst.rearrange("p (h m s) -> p h m s", s=4, m=64), in_=src)
            else:
                src = bank(key)[:].rearrange("p (s m) -> p m s", s=4)[:, lo // 4 : hi // 4]
                copy[eng](out=dst.rearrange("p (m s) -> p m s", s=4), in_=src)

        def store(eng, strip, r, lo=0, hi=None):
            first, w = STRIPS[strip]
            hi = w if hi is None else hi
            queue = nc.sync if eng == "D" else nc.scalar
            queue.dma_start(out=out[P * r : P * (r + 1), first + lo : first + hi], in_=held["staged", strip, r][:, lo:hi])

        def uses(task):
            call, a = task[0], task[1:]
            if call is warm_up:
                return [], [("warm", a[0])]
            if call is spread:
                return [], [("spread", a[0])]
            if call is spread_exit:
                return [("spread", a[0])], ["gp"]
            if call is build_diag:
                return ["gp"], [("diag", a[0] // 2), ("diag_of", a[0])] + [("diag_of", a[0] + 1)] * (len(a) > 1 and a[1] == 2)
            if call is widen:
                return [], [("lag_planes", a[0])]
            if call is lag_interleave:
                return [("lag_planes", a[0])], [("lag_grouped", a[0])]
            if call is mix:
                return [("lag_planes", a[0])], [("mixed", a[0], a[1])]
            if call is mix_exit:
                return [("mixed", a[0], a[1])], [("lag_grouped", a[0])]
            if call is lag_quant:
                return [("lag_grouped", a[0])], [("lag", a[0])]
            if call is turn:
                return [], [("turned", a[0], a[1])]
            if call is turn_exit:
                return [("turned", a[0], a[1])], [("ld_grouped", a[0])]
            if call is ld_quant:
                return [("ld_grouped", a[0])], [("ld", a[0])]
            if call is fill:
                return [("lag", UNITS[a[1]][0])] + [("ld", g) for g in UNITS[a[1]][1]], [a]
            if call is direct:
                return [("direct", a[0], a[1]), "gp"], [("grouped", a[0])] + [("half", 15)] * (a == (15, 0))
            if call is window and a[0] in OWN_BANK:
                return [("windows", a[0], 0), ("diag_of", UNITS[a[0]][1][0])], [("planes", a[0])]
            if call is window:
                return [("plane", a[0], a[1]), ("diag_of", UNITS[a[0]][1][0])] + [("first", a[0], a[1])] * (a[1] in S_FIRST and a[0] > 0), [("planes", a[0])] + [("first", a[0], a[1])] * (a[1] not in S_FIRST or a[0] == 0)
            if call is plane:
                if not has_diag(a[0]) or a[0] in OWN_BANK:
                    return [("plane", a[0], a[1]), "gp"], [("planes", a[0])]
                return [("plane", a[0], a[1]), "gp"] + [("first", a[0], a[1])] * (a[1] not in S_FIRST or a[0] == 0), [("planes", a[0])] + [("first", a[0], a[1])] * (a[1] in S_FIRST and a[0] > 0)
            if call is interleave:
                return [("planes", a[0])], [("grouped", 14, 1) if a[0] == 14 and a[1] >= 256 and LAST_IN_HALVES else ("grouped", a[0])]
            if call is quant:
                if a == (14, 256, 512) and LAST_IN_HALVES:
                    return [("grouped", 14, 1)], [("c",) + tuple(a)]
                return [("grouped", a[0])] + [("half", 15)] * (a == (15, 0, 256)), [("c",) + tuple(a)]
            if call is out_pass:
                return [key for key in quant_keys if key[1] == a[0] and (len(key) == 2 or len(a) == 2 or key[2] == a[2])], [out_key(UNITS[a[0]][0], a[1], a[2] if len(a) > 2 else 0)]
            if call is out_exit:
                return [out_key(a[0], a[1], a[2] if len(a) > 2 else 0)], [("staged", a[0], a[1]), ("staged_part",) + tuple(a)]
            return [("staged_part",) + tuple(a)], []

        T, V, S, G, D = [], [], [], [], []
        programme = {"T": T, "S": S, "V": V, "G": G, "D": D}
        banks = {}

        def on_bank(name, *task):
            T.append(task)
            key = uses(task)[1][0]
            if key not in banks:
                banks[key] = name

        quant_keys = []

        jobs = {1: [("plane", 2, t) for t in range(4)]}
        for k in range(2, 9):
            d = [("direct", 2 * k - 1, q) for q in range(4)]
            x = [("plane", 2 * k, t) for t in range(4)] if k < 8 else []
            w = [("windows", 2 * k, 0)] if 2 * k in OWN_BANK else []
            jobs[k] = d[:3] + x[:1] + d[3:] + w + x[1:]
        ring_jobs = [job for k in range(1, 9) for job in jobs[k]]
        filled = [0]

        def fills(count):
            for step in range(count):
                if filled[0] < len(ring_jobs):
                    on_bank(ring_names[filled[0] % 4], fill, *ring_jobs[filled[0]])
                    filled[0] = filled[0] + 1

        def run_pass(task):
            if task:
                on_bank(LAST_BANKS.get(uses(task)[1][0], "out%d" % task[2]), *task)
        ring_names = ["ring1", "ring2", "ring3", "ring0"]
        on_bank("ring3", warm_up, WIDTH)
        on_bank("out0", turn, 0, 0)
        on_bank("out1", turn, 0, 1)
        on_bank("out2", spread, 0)
        on_bank("ring2", spread, 1)
        on_bank("out3", turn, 1, 0)
        on_bank("ring3", turn, 1, 1)
        on_bank("out1", fill, "windows", 0, 0)
        on_bank("out0", fill, "plane", 0, 0)
        on_bank("ring0", fill, "plane", 0, 1)
        on_bank("out2", turn, 2, 0)
        on_bank("out3", turn, 2, 1)
        on_bank("ring1", fill, "plane", 0, 2)
        on_bank("ring2", fill, "plane", 0, 3)
        for q, name in enumerate(("out0", "out1", "ring3", "ring0")):
            on_bank(name, fill, "direct", 1, q)
        on_bank("out2", turn, 3, 0)
        on_bank("out3", turn, 3, 1)
        fills(4)
        on_bank("out0", warm_up, WIDTH // 2)
        fills(2)
        run_pass((out_pass, 1, 0))
        fills(1)
        run_pass((out_pass, 1, 1))
        fills(1)
        V.extend([(widen, 0, 0), (widen, 0, 2, 0, 256), (widen, 0, 3, 0, 256), (widen, 0, 2, 256, 512), (lag_interleave, 0, 0, 64), (lag_interleave, 0, 64, 112), (lag_quant, 0), (ld_quant, 0, 0, 256), (ld_quant, 0, 256, 512)])
        V.extend([(widen, 1, t) for t in range(4)] + [(window, 0, t) for t in range(4)] + [(ld_quant, 1), (lag_interleave, 1, 0, 128), (ld_quant, 2)])
        V.extend([(direct, 1, q) for q in range(4)] + [(ld_quant, 3), (quant, 1), (quant, 0), (lag_quant, 1)])
        S.extend([(widen, 0, 1), (widen, 0, 3, 256, 512), (lag_interleave, 0, 112, 128), (turn_exit, 0, 0), (turn_exit, 0, 1), (spread_exit, 0), (spread_exit, 1), (build_diag, 0)])
        S.extend([(turn_exit, 1, 0), (turn_exit, 1, 1), (plane, 0, 0), (plane, 0, 1), (turn_exit, 2, 0), (turn_exit, 2, 1), (plane, 0, 2), (plane, 0, 3)])
        S.extend([(build_diag, 1), (turn_exit, 3, 0), (turn_exit, 3, 1), (interleave, 0, G_LATE, WIDTH)] + [(plane, 2, t) for t in range(4)] + [(widen, 2, 0), (widen, 2, 1)])
        G.append((interleave, 0, 0, G_LATE))
        PLACES = {("ld_grouped", 2): "gpsimd_out"}
        shared = [[("ld_grouped", 2)] + [("grouped", n) for n in range(0, 16, 2)]]
        extra = {
            2: ([(widen, 2, 2), (widen, 2, 3)], [(lag_interleave, 2, 0, 64)]),
            3: ([(out_exit, 0, 0), (out_exit, 0, 1)], [(out_exit, 0, 2), (widen, 3, 0), (widen, 3, 1)]),
            4: ([(out_exit, 0, 3), (widen, 3, 2), (widen, 3, 3)], [(lag_interleave, 3, 0, 64)]),
            5: ([(out_exit, 1, 0), (out_exit, 1, 1)], [(out_exit, 1, 2), (build_diag, 3)]),
            6: ([(out_exit, 1, 3)], []),
            7: ([], [(out_exit, 2, 0)]),
        }
        slot = {}
        port_first = {3: [(build_diag, 2)], 4: []}
        port_last = {2: [(lag_interleave, 2, 64, 128)], 3: [(lag_quant, 2)], 4: [(lag_interleave, 3, 64, 128)], 5: [(lag_quant, 3)]}
        share = {2: 512, 3: 384, 4: 512, 5: 384, 6: 512, 7: 352}
        lead = {}
        ahead = {2: 2, 3: 2, 4: 2, 5: 2}
        for k in range(2, 8):
            a, b = 2 * k - 4, 2 * k - 3
            due = [(out_pass, n, r) for r in range(4) for n in (b, a) if (out_pass, n, r) not in T]
            if k == 7:
                due = [None] * 2 + due
            else:
                due = due + [None] * (len(jobs[k]) + 1 - len(due) - ahead.get(k, 1)) + [(out_pass, 2 * k - 1, r) for r in range(ahead.get(k, 1))]
            todo = [x for x in due if x]
            for step in PATTERN[k]:
                if step == "F":
                    fills(1)
                else:
                    run_pass(todo[0])
                    todo = todo[1:]
            assert not todo
            if (direct, 2 * k - 2, 0) not in V:
                G.append((interleave, 2 * k - 2, 0, share[k]))
            rest = [(interleave, 2 * k - 2, share[k], WIDTH)] if share[k] < WIDTH else []
            d = [(direct, 2 * k - 1, q) for q in range(4)]
            w = [(window, 2 * k, t) for t in range(4)] if has_diag(2 * k) else []
            V.extend(d + w if 2 * k in OWN_BANK else d[:W_AT] + w[:1] + d[W_AT:] + w[1:])
            V.extend(slot.get(k, []))
            if k not in S_REST:
                V.extend(rest)
            else:
                S.extend(rest)
            V.extend(port_first.get(k, []) + [(quant, 2 * k - 1), (quant, 2 * k - 2)] + port_last.get(k, []))
            S.extend(lead.get(k, []) + [(plane, 2 * k, 0)] + extra[k][0] + [(plane, 2 * k, t) for t in range(1, 4)] + extra[k][1])
        G.append((interleave, 14, 0, G_A))
        S.extend([(out_exit, 2, 1), (out_exit, 2, 2)] + [(interleave, 14, G_A, WIDTH), (out_exit, 2, 3)][::S_ORDER])
        V.extend([(direct, 15, q) for q in range(4)] + [(quant, 14, 0, 256), (quant, 15, 0, 256), (quant, 15, 256, 512), (quant, 14, 256, 512)])
        early, late = (13, 12), (14, 15)
        for r, h, units in ORDER(early, late):
            for n in units if h == 0 else sorted(units, key=lambda n: n == 14):
                on_bank(banks["direct", 15, r] if h else "out%d" % r, out_pass, n, r, 256 * h, 256 * h + 256)
        for h in range(2):
            for r in range(4):
                (S if EXITS[4 * h + r] == "S" else V).append((out_exit, 3, r, 256 * h, 256 * h + 256))
        D.extend([(store, k, r) for k in range(3) for r in range(4)])
        D.extend([(store, 3, r, lo, lo + 256) for lo in (0, 256) for r in range(4)])
        for n in range(16):
            if n % 2 or (direct, n, 0) in V:
                PLACES["grouped", n] = "direct_out%d" % ((n + 1) // 2 % 2)
            else:
                PLACES["planes", n] = "planes%d" % (n // 2 % 3)
                PLACES["grouped", n] = "gpsimd_out"
        for name in ("direct_out0", "direct_out1", "planes0", "planes1", "planes2"):
            shared.append([key for key in PLACES if PLACES[key] == name])
        for name in sorted(set(banks.values())):
            order = []
            for task in T:
                key = uses(task)[1][0]
                if banks[key] == name and key not in order:
                    order.append(key)
            shared.append(order)


        def apart(reader, writer):
            if reader[0] is quant and writer[0] is interleave and len(reader) == 4:
                return writer[3] <= reader[2] or reader[3] <= writer[2]
            return reader[0] is quant and writer[0] is direct and len(reader) == 4 and not reader[2] <= P * writer[2] < reader[3]

        quant_keys = [("c",) + tuple(task[1:]) for task in programme["V"] if task[0] is quant]
        readers, writers = {}, {}
        for eng in programme:
            for task in programme[eng]:
                reads, writes = uses(task)
                for key in reads:
                    readers.setdefault(key, []).append((eng, task))
                for key in writes:
                    writers.setdefault(key, []).append((eng, task))
        before = {}
        for order in shared:
            for first_key, next_key in zip(order, order[1:]):
                before[next_key] = first_key
        written = set()
        position = dict([(eng, 0) for eng in programme])
        while any([position[eng] < len(programme[eng]) for eng in programme]):
            moved = False
            for eng in programme:
                while position[eng] < len(programme[eng]):
                    task = programme[eng][position[eng]]
                    reads, writes = uses(task)
                    needs = [x for key in reads for x in writers[key] if not apart(task, x[1])]
                    for key in writes:
                        if key in before:
                            needs = needs + writers[before[key]] + readers.get(before[key], [])
                    if not all([x in written for x in needs]):
                        break
                    task[0](eng, *task[1:])
                    written.add((eng, task))
                    position[eng] = position[eng] + 1
                    moved = True
            assert moved
